import numpy as np, ml_dtypes
CORES = [40,64,80,88,96,104,120,144]
N = 8
import mx_ref
BF = ml_dtypes.bfloat16
def gentries(a):
    return np.ascontiguousarray(a.reshape(8, 16, -1).transpose(0, 2, 1)).reshape(8, -1)
def gtable(e):
    e = np.asarray(e); return np.ascontiguousarray(e.reshape(8, -1, 16).transpose(0, 2, 1)).reshape(128, -1).astype(np.int32)
def gcols(t, e):
    v = np.concatenate([t.reshape(8, 16, -1, 4), np.zeros((8, 16, 1, 4), BF)], axis=2)
    return np.ascontiguousarray(np.stack([v[g][:, e[g]] for g in range(8)])).reshape(128, -1)
def cut(t, i, w=512):
    return t[:, w * i:w * i + w]
def pick(q, e):
    c = np.concatenate([q[0].reshape(128, -1, 4), np.zeros((128, 1, 4), np.uint8)], axis=1); s = np.concatenate([q[1], np.ones((16, 1), np.uint8)], axis=1)
    return (np.ascontiguousarray(c[:, e].reshape(128, -1)), np.ascontiguousarray(s[:, e]))
def join(*qs):
    return (np.concatenate([q[0] for q in qs], axis=1), np.concatenate([q[1] for q in qs], axis=1))
def put(q, e, v):
    c, s = q[0].reshape(128, -1, 4).copy(), q[1].copy(); c[:, e] = v[0].reshape(128, -1, 4); s[:, e] = v[1]
    return (c.reshape(128, -1), s)
def pk(c, s):
    return (np.ascontiguousarray(c), mx_ref.live(s))
def emit(q):
    return q[0], q[1]
def packed(v, rng):
    q = [mx_ref.quantize(np.ascontiguousarray(v[r])) for r in range(N)]
    return np.stack([a for a, b in q]), np.stack([mx_ref.plane(b, rng) for a, b in q])
def values_of_codes():
    e, c = np.zeros((128, 128, 4), np.float32), np.zeros((128, 2, 4), np.uint8)
    e[np.arange(128), np.arange(128), 0] = 1
    c[:127, :, 0] = np.arange(256).reshape(2, 128).T[:127]
    return mx_ref.matmul(mx_ref.quantize(e.reshape(128, 512).astype(BF)), (c.reshape(128, 8), np.full((16, 2), 127, np.uint8))).T.reshape(-1).astype(np.float64)
CODE_VALUE, SCALE_VALUE = values_of_codes(), 2.0 ** (np.arange(256) - 127.0)
def decode(q):
    return (CODE_VALUE[q[0]].reshape(16, 8, -1, 4) * SCALE_VALUE[q[1]][:, None, :, None] + 0.0).reshape(128, -1).astype(np.float32)
def f(rng, *shape):
    return mx_ref.flush((rng.standard_normal(shape, dtype=np.float32) * np.exp2(rng.integers(-2, 3, shape[:-1] + (1,)))).astype(BF))
def wide(rng, *shape, cols=0):
    v = rng.standard_normal(shape, dtype=np.float32) * np.exp2(rng.integers(-12, 13, shape)).astype(np.float32)
    if cols: v *= np.repeat(np.exp2(rng.integers(-cols, cols + 1, shape[:-2] + (1, shape[-1] // 4))) * (rng.random(shape[:-2] + (1, shape[-1] // 4)) > 0.0625), 4, axis=-1).astype(np.float32)
    return mx_ref.flush(v.astype(BF))
C, E, B, NB, P, R = 320, 32, 48, 6, 288, 3
def big(v):
    v = v.astype(np.float32)
    v[np.abs(v) < np.float32(2.0 ** -16)] = 0
    return v.astype(BF)
def dominators(a, b, lost):
    dom = np.zeros((8, C, C), bool)
    dom[:, np.arange(C), np.arange(C)] = True
    d = np.full((8, P), -1)
    for k in range(NB):
        i = B * k + np.arange(B)
        one = np.take_along_axis(dom, a[:, i, None], axis=1)
        two = np.take_along_axis(dom, b[:, i, None], axis=1)
        both = one & (two | lost[:, i, None])
        d[:, i] = np.max(np.where(both, np.arange(C), -1), axis=2)
        dom[:, E + i] = dom[:, E + i] | both
    return d, np.sum(dom, axis=1)
def numbers_of(rng):
    return {"x": big(f(rng, N, 128, 4 * C)), "u": np.array(f(rng, N, 128, 512)), "v": np.array(f(rng, N, 128, 512))}
def lists_of(rng):
    n = E + B * (np.arange(P) // B)
    w = 2 ** rng.integers(0, 6, (N, 8, 1))
    e = np.argsort(rng.random((N, 8, E)), axis=2)
    l = []
    for k in range(2):
        p = rng.integers(0, n, (N, 8, P))
        l.append(np.where(p < E, np.take_along_axis(e, p % w, axis=2), p))
    return l
def stored(a, b):
    return {"pa": np.stack([gtable(e) for e in a]), "pb": np.stack([gtable(e) for e in b])}
def packedw(w, rng):
    c, p = packed(w, rng)
    return {"wc": c, "ws": p}
def weights(rng, q=-1):
    w = np.array(f(rng, N, 128, 2048)).reshape(N, 128, 4, 128, 4)
    if q >= 0:
        w[:, 16 * q:16 * q + 8] = 0
        w[:, :, :, 16 * q:16 * q + 8] = 0
    return packedw(w.reshape(N, 128, 2048), rng)
def setup_inputs(rng):
    return {**numbers_of(rng), **stored(*lists_of(rng)), **weights(rng)}
def setup_inputs_cuts(rng):
    d = numbers_of(rng)
    q = int(rng.integers(8))
    o, z = rng.permutation(N), rng.permutation(N) % 4
    size = np.array([2.0 ** -30, 2.0 ** -12, 1.0, 2.0 ** 29])[z]
    one = np.where(z % 2 == 0, 2.0 ** -30, 1.0).astype(np.float32).astype(BF)
    less = np.where(z == 0, -2.0 ** -30, 0.0).astype(np.float32).astype(BF)
    k = rng.integers(-1, 2, (N, 8, C, 4))
    k[:, :, :, 3] = 0
    for r in range(N):
        if o[r] == 0:
            k[r, :, :, 0] = np.abs(k[r, :, :, 0])
            k[r, :, :, 1] = -1
        if o[r] == 1:
            k[r, :, :, 0] = -1
            k[r, :, :, 1] = 0
        if o[r] == 2: k[r, :, :, 2] = np.arange(8)[:, None] % 2 * 2 - 1
    mark = np.where((z == 0)[:, None, None, None], 1.5 + 0.125 * k, k)
    x = d["x"].reshape(N, 8, 16, C, 4)
    x[:, q, :8] = (mark * size[:, None, None, None]).astype(np.float32).astype(BF)
    u = d["u"].reshape(N, 128, 128, 4)
    for t in range(R):
        u[:, :, t::16] = 0
        for g in range(8):
            u[:, 16 * q + g, 16 * g + t, t] = one
            u[:, 16 * q + g, 16 * g + t, 3] = less
    return {"x": x.reshape(N, 128, 4 * C), "u": u.reshape(N, 128, 512), "v": d["v"], **stored(*lists_of(rng)), **weights(rng, q)}
def column(j, i):
    return np.where(j < 0, i % E, E + B * j + i)
def setup_inputs_trees(rng):
    d = numbers_of(rng)
    a, b = lists_of(rng)
    o = rng.permutation(N)
    i, j = np.arange(P) % B, np.arange(P) // B
    for r in range(N):
        for g in range(8):
            k = (g + o[r]) % 8
            e = E // 2 + rng.permutation(E // 2)
            if k == 0:
                n = np.full(P, e[0])
                if o[r] % 2: n[rng.permutation(P)[255:]] = e[1]
                a[r, g], b[r, g] = n, n
            if k == 1:
                n = column(j - 1, np.concatenate([rng.permutation(B) for m in range(NB)]))
                a[r, g], b[r, g] = n, n
            if k == 2: a[r, g], b[r, g] = column(j - 1, i), column(rng.integers(-1, j, P), i)
            if k == 3: a[r, g], b[r, g] = column(j - 1, i), column(j - 1, i ^ 1)
            if k == 4:
                a[r, g] = np.where(j == 0, e[0], column(j - 1, rng.integers(0, B, P)))
                b[r, g] = np.where(j == 0, e[0], column(j - 1, rng.integers(0, B, P)))
            if k == 5: a[r, g], b[r, g] = column(j - 1, B - 1 + 0 * i), column(j - 1, 0 * i)
            if k == 6:
                n = np.where(j == 0, e[0], column(j - 1, i))
                a[r, g], b[r, g] = n, np.where(j == NB - 1, column(j - 1, i ^ 1), n)
            if k == 7 and o[r] % 2 == 0:
                n = np.where(rng.permutation(P) < P // 2 - 1, min(e[0], e[1]), max(e[0], e[1]))
                a[r, g], b[r, g] = n, n
    return {**d, **stored(a, b), **weights(rng)}
def setup_inputs_huge(rng):
    d = numbers_of(rng)
    a, b = lists_of(rng)
    e = int(rng.integers(N))
    x = 2.0 ** 28 * (1.7 + 0.15 * rng.random((N, 128, C, 4)))
    c = np.stack([rng.permutation(C) % 2 * 2.0 - 1.0 for r in range(N)])
    c[e] = 0
    c[(e + 1) % N] = -1
    c[(e + 2) % N] = -1
    x *= c[:, None, :, None]
    s = np.stack([rng.permutation(8 * R) % 2 * 2.0 - 1.0 for r in range(N)]).reshape(N, 1, 8, R, 1)
    k, m = [int(g) for g in rng.permutation(8)[:2]]
    i, j = [int(n) for n in rng.permutation(E - 1)[:2]]
    for r in ((e + 1) % N, (e + 2) % N):
        a[r, k] = i
        b[r, k] = j
        x[r, 16 * k:16 * k + 16, i] = -2.0 ** 30
        x[r, 16 * k:16 * k + 16, j] = -2.0 ** 30
        s[r, 0, k] = -1
    r = (e + 2) % N
    a[r, m] = np.where(np.arange(P) < B, i, E)
    b[r, m] = E - 1
    x[r, 16 * m:16 * m + 16, E - 1] = 2.0 ** 30
    s[r, 0, m] = 1
    h = (2.0 ** 30 * (1 - 0.1 * rng.random((N, 128, 8, R, 4))) * s).astype(np.float32).astype(BF)
    u = d["u"].reshape(N, 128, 128, 4)
    for t in range(R): u[:, :, t::16] = h[:, :, :, t]
    w = np.zeros((N, 128, 4, 128, 4), np.float32)
    p = np.arange(128)
    for n in range(4): w[:, p, n, p, n] = 1 - 2 * (p % 2)
    return {"x": x.astype(np.float32).reshape(N, 128, 4 * C).astype(BF), "u": u.reshape(N, 128, 512), "v": d["v"], **stored(a, b), **packedw(w.reshape(N, 128, 2048).astype(BF), rng)}
def setup_inputs_spread(rng):
    d = setup_inputs(rng)
    d["x"] = big(wide(rng, N, 128, 4 * C, cols=6))
    return d
def check_inputs(d):
    b = []
    for k in ("x", "u", "v"):
        a = np.abs(d[k].astype(np.float32))
        if not (np.isfinite(a).all() and ((a == 0) | (a >= 2.0 ** -30) & (a <= 2.0 ** 30)).all()): b.append("a value of " + k)
    n = E + B * (np.arange(P) // B)
    for k in ("pa", "pb"):
        for r in range(N):
            e = gentries(d[k][r])
            if ((e < 0) | (e >= n)).any(): b.append("an entry of " + k)
    if ((d["wc"] == 0x7F) | (d["wc"] == 0xFF)).any(): b.append("a code of wc that is no number")
    return b
def reference(x, u, v, pa, pb, wc, ws):
    qu = [mx_ref.quantize(u[r]) for r in range(N)]
    lay = [pk(wc[r], ws[r]) for r in range(N)]
    a = [gentries(pa[r]).astype(np.int64) for r in range(N)]
    b = [gentries(pb[r]).astype(np.int64) for r in range(N)]
    now = [x[r] for r in range(N)]
    od = np.zeros((N, 8, P), np.float32)
    for t in range(R):
        nodes, feed = [], []
        for r in range(N):
            s = mx_ref.matmul(qu[r], mx_ref.quantize(now[r]))[t::16]
            lost = s[:, E:] + np.float32(0.0) < 0
            d, n = dominators(a[r], b[r], lost)
            h = np.argsort(-n, axis=1, kind="stable")[:, :E]
            feed.append(mx_ref.quantize(gcols(now[r], h)))
            one = gcols(now[r], a[r]).astype(np.float32)
            two = gcols(now[r], np.where(lost, a[r], b[r])).astype(np.float32)
            m = (np.maximum(one, two) + gcols(now[r], d).astype(np.float32)).astype(BF)
            q = mx_ref.quantize(m)
            z = [np.maximum(mx_ref.matmul(pick(lay[r], np.arange(128 * i, 128 * i + 128)), q), np.float32(0.0)) * np.float32(0.015625) for i in range(4)]
            nodes.append((now[r][:, 4 * E:].astype(np.float32) + np.stack(z, axis=2).reshape(128, -1)).astype(BF))
            od[r] = d
        came = decode(join(*feed))
        for r in range(N):
            entry = np.maximum(now[r][:, :4 * E].astype(np.float32), cut(came, (r - 1) % N, 4 * E)).astype(BF)
            now[r] = np.ascontiguousarray(np.concatenate([entry, nodes[r]], axis=1))
    y = np.zeros((N, 128, C), np.float32)
    oc, osc = np.zeros((N, 128, 4 * C), np.uint8), np.zeros((N, 16, C), np.uint8)
    for r in range(N):
        q = mx_ref.quantize(now[r])
        y[r] = mx_ref.matmul(mx_ref.quantize(v[r]), q)
        oc[r], osc[r] = emit(q)
    return {"y": y, "od": od, "oc": oc, "osc": osc}

@@ -1,0 +1,504 @@
+import math
+from concourse.bass import DstId, RemoteDMATransfer
+from concourse.mybir import dt, AluOpType as A, ActivationFunctionType as F, AxisListType as AX
+
+C, E, B, NB, P, R = 320, 32, 48, 6, 288, 3
+K = C - B
+PL = 336
+ZL = 192
+X4, S_, BF, F32, U8 = "float8_e4m3fn_x4", "sbuf", "bfloat16", "float32", "uint8"
+SCRATCH = {"ps": ("psum", [128, 4096], F32)}
+for _n, _w in (("xi", 4 * C), ("xp", 12 * PL), ("ep", 128 * R), ("ut", 512), ("vt", 512), ("et", 2048), ("ones", 512),
+               ("zt", 4 * ZL), ("nd", P), ("lf", P), ("ls", P), ("d0", 96), ("jb", 1792), ("nb", 288), ("fl", 2 * K),
+               ("cs", 2 * K + 2), ("fg", 128), ("fi", 512), ("g1", 4 * P), ("g2", 4 * P), ("mt", 4 * P)):
+    SCRATCH[_n] = (S_, [128, _w], BF)
+for _n, _w in (("cf", 64), ("j16", P), ("md", P), ("dg", 32), ("it", 336), ("oh", 288), ("tabn", 560), ("scl", 32), ("jt", 32),
+               ("ab", 96), ("uu", 688), ("d1", 576), ("tt", 616), ("llf", 112), ("js", 1152), ("pk", 8), ("sm2", 32), ("key", 96),
+               ("rr", 4 * P), ("ys", C), ("odb", P)):
+    SCRATCH[_n] = (S_, [128, _w], F32)
+for _n, _w in (("pai", 32), ("pbi", 32), ("ci", 64), ("ni", 32)):
+    SCRATCH[_n] = (S_, [128, _w], "int32")
+for _n, _w in (("cu", 160), ("cw", 48), ("llu", 112)):
+    SCRATCH[_n] = (S_, [128, _w], "uint16")
+for _n, _w in (("u", 128), ("v", 128), ("up", 128 * R), ("w", 512), ("x", P), ("e", 128), ("m", P), ("i", 512),
+               ("f0", 128), ("f1", 128), ("f2", 128)):
+    SCRATCH["q" + _n] = (S_, [128, _w], X4)
+    SCRATCH["s" + _n] = (S_, [128, _w], U8)
+for _t in range(R):
+    SCRATCH["lc%d" % _t] = (S_, [128, ZL + 32], X4)
+    SCRATCH["lp%d" % _t] = (S_, [128, ZL + 128], U8)
+NDMA = 26
+SEMAPHORES = ["cv", "cs", "ct", "cg", "sent"] + ["arr%d" % t for t in range(R)] + ["dm%d" % i for i in range(NDMA)]
+CY = 1.04e-3
+LAT, NET = 0.08, 4.5
+TRIES = 150000
+PLAN = {}
+
+
+def route(T, topo, r):
+    src, dst = T.cores[r], T.cores[(r + 1) % len(T.cores)]
+    if topo.may_write(src, dst):
+        return [src, dst]
+    able = [c for c in topo.cores_of(src) if c != src and topo.may_write(c, dst)]
+    near = [c for c in able if topo.die(c) == topo.die(src)]
+    return [src, (near or able)[0], dst]
+
+
+def halves(topo, src, dst):
+    e = topo.engines(src, dst)
+    h = len(e) // 2
+    return sum(1 << i for i in e[:h]), sum(1 << i for i in e[h:2 * h]), 2 * h
+
+
+def hand(g, T, topo, src, dst, codes, plane, t):
+    rid, pid = topo.addr(dst, src)
+    m0, m1, n = halves(topo, src, dst)
+    to, sem = DstId(rid=rid, pnc=pid), T.sem["arr%d" % t]
+    g.remote_dma_fused([
+        RemoteDMATransfer(dst_ids=[to], dma_engine_mask=m0, remote_sem=sem, src=codes,
+                          dst=T["lc%d" % t][:, ZL:ZL + 32].bitcast(dt.uint8)),
+        RemoteDMATransfer(dst_ids=[to], dma_engine_mask=m1, remote_sem=sem, src=plane,
+                          dst=T["lp%d" % t][:, ZL:ZL + 128])], local_sem=T.sem.sent)
+    return n
+
+
+def relay(g, T, topo, src, me, dst):
+    n = 0
+    for t in range(R):
+        g.wait_ge(T.sem["arr%d" % t], halves(topo, src, me)[2])
+        n += hand(g, T, topo, me, dst, T["lc%d" % t][:, ZL:ZL + 32].bitcast(dt.uint8), T["lp%d" % t][:, ZL:ZL + 128], t)
+    g.wait_ge(T.sem.sent, n)
+
+
+def plan(ops):
+    n = len(ops)
+    dep = [sorted(o["dep"]) for o in ops]
+    succ = [[] for _ in ops]
+    for i in range(n):
+        for d in dep[i]:
+            succ[d].append(i)
+    qs = sorted(set(o["q"] for o in ops))
+    q = [qs.index(o["q"]) for o in ops]
+    dur, lat = [o["dur"] for o in ops], [o["lat"] for o in ops]
+    prio = [0.0] * n
+    for i in range(n - 1, -1, -1):
+        prio[i] = dur[i] + lat[i] + 1e-6 + max([prio[s] for s in succ[i]] + [0.0])
+    order = sorted(range(n), key=lambda i: -prio[i])
+    seed = [99]
+
+    def rnd():
+        seed[0] = (seed[0] * 6364136223846793005 + 1442695040888963407) % (1 << 64)
+        return (seed[0] >> 33) / float(1 << 31)
+
+    def run(od):
+        free, done = [0.0] * len(qs), [0.0] * n
+        for i in od:
+            s = free[q[i]]
+            for d in dep[i]:
+                if done[d] > s:
+                    s = done[d]
+            s += dur[i]
+            free[q[i]] = s
+            done[i] = s + lat[i]
+        return max(done) + 0.02 * sum(done) / n, done
+
+    cur, done = run(order)
+    best, bo = cur, list(order)
+    for it in range(TRIES):
+        if it % 1000 == 0:
+            order = sorted(order, key=lambda i: done[i] - lat[i] - dur[i])
+            cur, done = run(order)
+        a = int(rnd() * n)
+        i = order[a]
+        step = 1 if rnd() < 0.5 else -1
+        stop = succ[i] if step > 0 else dep[i]
+        b, left = a, 1 + int(rnd() ** 3 * 12)
+        while left and 0 <= b + step < n and order[b + step] not in stop:
+            b += step
+            if q[order[b]] == q[i]:
+                left -= 1
+        if b == a:
+            continue
+        new = order[:a] + order[a + 1:]
+        new.insert(b, i)
+        got, dn = run(new)
+        if got <= cur or rnd() < math.exp((cur - got) / (0.15 * (1 - it / TRIES) + 0.003)):
+            cur, order, done = got, new, dn
+            if got < best:
+                best, bo = got, list(new)
+    done = run(bo)[1]
+    return max(done), bo, [done[i] - lat[i] - dur[i] for i in range(n)]
+
+
+def emit(g, T, ops):
+    last_w, readers = {}, {}
+    for i, o in enumerate(ops):
+        dep = set(o["after"])
+        for k in o["r"] + o["w"]:
+            if k in last_w:
+                dep.add(last_w[k])
+        for k in o["w"]:
+            dep.update(readers.get(k, []))
+        for k in o["r"]:
+            readers.setdefault(k, []).append(i)
+        for k in o["w"]:
+            last_w[k] = i
+            readers[k] = []
+        dep.discard(i)
+        o["dep"] = dep
+    if "p" not in PLAN:
+        PLAN["p"] = plan(ops)
+    _end, order, _at = PLAN["p"]
+    place = {i: k for k, i in enumerate(order)}
+    queue = {"v": g.vector, "s": g.scalar, "t": g.tensor, "g": g, "y": g.sync}
+    count, known, ndma = {}, {q: {} for q in queue}, 0
+    for i in order:
+        o = ops[i]
+        q = o["q"]
+        if q == "net":
+            o["sig"], o["clock"] = o["sem"], {}
+            count[o["sem"][0]] = o["sem"][1]
+            continue
+        kn = known[q]
+        for d in sorted(o["dep"], key=lambda j: -place[j]):
+            p = ops[d]
+            if p["sig"] is None:
+                continue
+            name, val = p["sig"]
+            if kn.get(name, 0) < val:
+                queue[q].wait_ge(T.sem[name], val)
+                kn[name] = val
+                for a, b in p["clock"].items():
+                    kn[a] = max(kn.get(a, 0), b)
+        ins = o["fn"]()
+        o["clock"] = dict(kn)
+        if o["kind"] == "c":
+            name = "c" + q
+            count[name] = count.get(name, 0) + 1
+            ins.then_inc(T.sem[name], 1)
+            o["sig"] = (name, count[name])
+        elif o["kind"] == "d":
+            name = "dm%d" % ndma
+            ndma += 1
+            count[name] = 16
+            ins.then_inc(T.sem[name], 16)
+            o["sig"] = (name, 16)
+        else:
+            count["sent"] = count.get("sent", 0) + ins
+            o["sig"] = None
+    seen = {}
+    for q in known:
+        for a, b in known[q].items():
+            seen[a] = max(seen.get(a, 0), b)
+    for name, val in count.items():
+        if seen.get(name, 0) < val:
+            g.wait_ge(T.sem[name], val)
+
+
+def rank_program(g, core, T, topo):
+    rank = T.rank_of(core)
+    n_ranks = len(T.cores)
+    if rank is None:
+        for r in range(n_ranks):
+            way = route(T, topo, r)
+            if len(way) == 3 and way[1] == core:
+                relay(g, T, topo, way[0], core, way[2])
+        return
+    way_out, way_in = route(T, topo, rank), route(T, topo, (rank - 1) % n_ranks)
+    arrive = halves(topo, way_in[-2], core)[2]
+    V, S, ops = g.vector, g.scalar, []
+
+    def op(q, fn, r, w, dur, lat=LAT, kind="c", after=(), sem=None):
+        ops.append({"q": q, "fn": fn, "r": r.split(), "w": w.split(), "dur": dur, "lat": lat, "kind": kind,
+                    "after": list(after), "sem": sem})
+        return len(ops) - 1
+
+    def cost(n, c):
+        return max(0.07, 0.03 + n * c * CY)
+
+    def gcost(n):
+        return 0.06 + n * 1.6 * CY
+
+    def ts(out, in0, s1, s2, o0, o1, r, w, n=16, c=1.0):
+        if o1 is None:
+            return op("v", lambda: V.tensor_scalar(out, in0, s1, None, o0), r, w, cost(n, c))
+        return op("v", lambda: V.tensor_scalar(out, in0, s1, s2, o0, o1), r, w, cost(n, c))
+
+    def tt(out, a, b, o, r, w, n=16, c=2.0, dur=None):
+        return op("v", lambda: V.tensor_tensor(out, a, b, o), r, w, dur or cost(n, c))
+
+    def cp(out, a, r, w, n=16, c=1.0, dur=None):
+        return op("v", lambda: V.tensor_copy(out, a), r, w, dur or cost(n, c))
+
+    def ms(out, val, w, n=16):
+        return op("v", lambda: V.memset(out, val), "", w, cost(n, 0.7))
+
+    def scan(out, a, b, o0, o1, r, w, n, c=1.0):
+        return op("v", lambda: V.tensor_tensor_scan(out, a, b, 0.0, o0, o1), r, w, cost(n, c))
+
+    def qz(out, sc, a, r, w, n):
+        return op("v", lambda: V.quantize_mx(out, sc, a), r, w, 0.03 + n * 4 * 0.27e-3)
+
+    def act(out, a, f, r, w, n=16, gather=False, **kw):
+        return op("s", lambda: S.activation(out, a, f, **kw), r, w, gcost(n) + 0.02 if gather else 0.07 + n * CY)
+
+    def iota(out, pat, base, cm, w, n, flt=True):
+        if flt:
+            return op("g", lambda: g.iota(out, pat, base, cm, allow_small_or_imprecise_dtypes=True), "", w, 0.15 + 2 * n * CY)
+        return op("g", lambda: g.iota(out, pat, base, cm), "", w, 0.15 + 2 * n * CY)
+
+    def mm(out, lq, lsc, rq, rsc, r, w, n):
+        return op("t", lambda: g.tensor.matmul_mx(out, lq, lsc, rq, rsc, True, True), r, w, 0.03 + n * 0.6e-3, lat=0.12)
+
+    def dma(q, out, a, r, w, lat=2.0):
+        e = {"y": g.sync, "s": g.scalar, "g": g}[q]
+        return op(q, lambda: e.dma_start(out, a), r, w, 0.1, lat=lat, kind="d")
+
+    def plane(t, b, a=0, z=C + 1):
+        o = (4 * t + b) * PL
+        return T.xp[:, o + a:o + z]
+
+    u8 = dt.uint8
+    ps = T.ps
+    cf = T.cf
+    dma("y", T.xi[:], T.x[:], "", "xn xe", 2.6)
+    dma("s", T.ut[:], T.u[:], "", "ut", 2.3)
+    dma("y", T.pai[:, 0:18], T.pa[:], "", "pa", 2.6)
+    dma("s", T.pbi[:, 0:18], T.pb[:], "", "pb", 2.6)
+    dma("y", T.qw[:].bitcast(u8), T.wc[:], "pa", "qw", 3.0)
+    dma("y", T.sw[:], T.ws[:], "pa", "sw", 3.0)
+    dma("y", T.vt[:], T.v[:], "pa", "vt", 3.0)
+    iota(T.ci[:, 0:1], [[0, 1]], 0, 1, "p", 1, False)
+    iota(T.ci[:, 8:32], [[1, R], [16, 8]], 0, 0, "uli", 24, False)
+    iota(T.j16[:], [[0, 18], [1, 16]], 0, 0, "j16", P)
+    iota(T.it[:], [[1, 336]], -1, 0, "it", 336)
+    iota(T.tabn[:, 0:144], [[1, 144]], 113, 0, "tab0", 144)
+    iota(T.tabn[:, 144:256], [[1, 112]], 1, 0, "tab1", 112)
+    iota(T.tabn[:, 256:560], [[1, 304]], 1, 0, "tab2", 304)
+    iota(T.fi[:], [[0, 512]], 0, 0, "fi", 512)
+    iota(T.zt[:], [[0, 4 * ZL]], 0, 0, "zt", 4 * ZL)
+    iota(T.ones[:], [[0, 512]], 1, 0, "ones", 512)
+    lane = cf[:, 0:1]
+    ts(T.ci[:, 1:2], T.ci[:, 0:1], 15, None, A.bitwise_and, None, "p", "li")
+    cp(lane, T.ci[:, 1:2], "li", "lane")
+    cp(T.cu[:, 0:24], T.ci[:, 8:32], "uli", "ulu")
+    ts(T.nd[:], T.j16[:], lane, None, A.not_equal, None, "j16 lane", "nd", P)
+    act(T.md[:], T.nd[:], F.Copy, "nd", "md", P, scale=-1e29)
+    ts(T.dg[:], T.j16[:, 0:32], lane, None, A.is_equal, None, "j16 lane", "dg", 32)
+    act(T.jt[:], T.it[:, 1:33], F.Copy, "it", "jt", 32, scale=1.0 / 64)
+    ts(T.ci[:, 2:3], T.ci[:, 0:1], 4, None, A.logical_shift_right, None, "p", "c2")
+    tt(T.ci[:, 3:4], T.ci[:, 2:3], T.ci[:, 0:1], A.add, "c2 p", "c3")
+    ts(T.ci[:, 4:5], T.ci[:, 3:4], 1, None, A.bitwise_and, None, "c3", "c4")
+    ts(cf[:, 1:2], T.ci[:, 4:5], 304.0, None, A.mult, None, "c4", "odd")
+    ts(cf[:, 2:3], lane, 16.0, cf[:, 1:2], A.mult, A.add, "lane odd", "be")
+    ts(cf[:, 3:4], lane, 16.0, cf[:, 1:2], A.mult, A.subtract, "lane odd", "bo")
+    act(cf[:, 4:5], T.dg[:, 15:16], F.Identity, "dg bo", "bo1", scale=1000.0, bias=cf[:, 3:4])
+    act(cf[:, 5:6], T.dg[:, 0:1], F.Identity, "dg bo1", "bo2", scale=1000.0, bias=cf[:, 4:5])
+    ts(cf[:, 6:7], lane, 2.0, 1000.0, A.is_ge, A.mult, "lane", "big")
+    act(cf[:, 7:8], cf[:, 6:7], F.Identity, "big be", "be1", bias=cf[:, 2:3])
+    cl = 24
+    cp(T.cu[:, cl:cl + 1], cf[:, 2:3], "be", "cl0")
+    ts(T.cu[:, cl + 1:cl + 2], cf[:, 7:8], 256.0, 608.0, A.add, A.min, "be1", "cl1")
+    ts(T.cu[:, cl + 2:cl + 3], cf[:, 4:5], 353.0, 609.0, A.add, A.min, "bo1", "cl2")
+    ts(T.cu[:, cl + 3:cl + 4], cf[:, 2:3], 34.0, None, A.add, None, "be", "cl3")
+    ts(T.cu[:, cl + 4:cl + 5], cf[:, 5:6], 355.0, 609.0, A.add, A.min, "bo2", "cl4")
+    ts(T.cu[:, cl + 5:cl + 6], cf[:, 2:3], 36.0, None, A.add, None, "be", "cl5")
+    ts(T.cu[:, cl + 6:cl + 7], cf[:, 5:6], 357.0, 609.0, A.add, A.min, "bo2", "cl6")
+    CL = "cl0 cl1 cl2 cl3 cl4 cl5 cl6"
+    ms(T.tt[:, 608:609], 274.0, "ttp0")
+    ms(T.tt[:, 609:616], 273.0, "ttp1")
+    ts(T.ci[:, 5:6], lane, 1.0 / 3, None, A.mult, None, "lane", "c5")
+    cp(T.cu[:, 32:33], T.ci[:, 5:6], "c5", "rl0")
+    ms(T.cu[:, 33:34], 5, "rl1")
+    ms(T.scl[:, 0:1], 1.0, "sc0")
+    ms(T.scl[:, 1:2], 1.0 / 4096, "sc1")
+    ms(T.scl[:, 2:32:3], 1.0, "sc2")
+    ms(T.scl[:, 3:32:3], 1.0 / 256, "sc3")
+    ms(T.scl[:, 4:32:3], 1.0 / 65536, "sc4")
+    for k in range(2):
+        ts(cf[:, 8 + k:9 + k], lane, -1.0, -1.5 - 16 * k, A.mult, A.add, "lane", "th%d" % k)
+        ts(cf[:, 10 + k:11 + k], lane, 0.5 + 16 * k, None, A.add, None, "lane", "jj%d" % k)
+    ms(T.cs[:, 2 * K:2 * K + 2], -1.0, "csp")
+    ms(T.oh[:, 0:1], 0.0, "oh0")
+    ms(T.oh[:, 273:274], -112.0 * 65793 / 16, "oh1")
+    ms(T.oh[:, 274:275], 256.0 * 4097 / 16, "oh2")
+    OH = "oh0 oh1 oh2"
+    for c in range(17):
+        wgt = 4096.0 ** c if c < 2 else 256.0 ** ((c - 2) % 3)
+        act(T.oh[:, 1 + 16 * c:17 + 16 * c], T.dg[:, 0:16], F.Copy, "dg", "ohc%d" % c, 16, scale=wgt)
+        OH += " ohc%d" % c
+    ms(T.uu[:, 0:66], 0.0, "ue", 66)
+    ms(T.uu[:, 642:674], 0.0, "up", 32)
+    ms(T.d0[:], 0.0, "d0", 96)
+    act(T.uu[:, 3:66:2], T.it[:, 2:34], F.Copy, "it dg", "ue", 32, scale=T.dg[:, 0:1])
+    for k in range(NB):
+        act(T.d1[:, 96 * k + 1:96 * k + 96:2], T.it[:, 34 + B * k:34 + B * k + B], F.Copy, "it dg", "self%d" % k, B,
+            scale=T.dg[:, k + 1:k + 2])
+    ms(T.nb[:, 0:1], 0.0, "nb0")
+    ms(T.xp[:, 0:12 * PL:PL], 0.0, "xz")
+    for b in range(4):
+        op("g", lambda b=b: g.affine_select(T.et[:, 512 * b:512 * b + 512], T.ones[:], [[1, 512]], A.is_equal, 0.0, -b, -4),
+           "ones", "et%d" % b, 1.2)
+    qz(T.qi[:], T.si[:], T.et[:], "et0 et1 et2 et3", "qi", 512)
+    qz(T.lc0[:, 0:ZL], T.lp0[:, 0:ZL], T.zt[:], "zt", "lz0 lw0", ZL)
+    for t in range(1, R):
+        dma("y", T["lc%d" % t][:, 0:ZL].bitcast(u8), T.lc0[:, 0:ZL].bitcast(u8), "lz0", "lz%d" % t)
+        dma("y", T["lp%d" % t][:, 0:ZL], T.lp0[:, 0:ZL], "lz0", "lw%d" % t)
+    LA, LA0, LA1, LB, LB0, LB1, LD, LN, LF, LC, LR = 34, 52, 71, 90, 108, 127, 0, 18, 36, 38, 40
+    lu, lv = T.cu, T.cw
+    ts(lu[:, LA:LA + 18], T.pai[:, 0:18], 1.0, None, A.add, None, "pa", "la")
+    ts(lu[:, LA0:LA0 + 18], T.pai[:, 0:18], 2.0, 3.0, A.mult, A.add, "pa", "la0")
+    ts(lu[:, LA1:LA1 + 18], T.pai[:, 0:18], 2.0, 3.0, A.mult, A.add, "pa", "la1")
+    tt(T.ab[:, 0:18], T.pai[:, 0:18], T.pbi[:, 0:18], A.subtract, "pa pb", "amb")
+    ts(T.ab[:, 18:36], T.pbi[:, 0:18], 1.0, None, A.add, None, "pb", "bf")
+    cp(T.d1[:, 0:96:2], T.uu[:, 0:66].indirect(lu[:, LA0:LA0 + 3]), "ue la0", "a0", dur=gcost(B))
+    qz(T.qu[:], T.su[:], T.ut[:], "ut", "qu", 128)
+    qz(T.qv[:], T.sv[:], T.vt[:], "vt", "qv", 128)
+    for t in range(R):
+        cp(T.qup[:, 128 * t:128 * t + 128].bitcast(dt.uint32), T.qu[:].bitcast(dt.uint32).indirect(T.cu[:, 8 * t:8 * t + 8]),
+           "qu ulu", "qup%d" % t, dur=gcost(128))
+        act(T.sup[:, 128 * t:128 * t + 128], T.su[:].indirect(T.cu[:, 8 * t:8 * t + 8]), F.Copy, "qu ulu", "sup%d" % t, 128, True)
+    for b in range(4):
+        act(plane(0, b, 1), T.xi[:, b:4 * C:4], F.Copy, "xn xe", "pn0%d pe0%d" % (b, b), C)
+        act(T.ep[:, 32 * b:32 * b + 32], T.xi[:, b:4 * E:4], F.Copy, "xe", "ep0%d" % b, E)
+    XN = "xn xn0 xn1 xn2 xn3"
+    span = [(0, 19), (32, 48), (52, 65), (70, 80), (90, 97), (108, 112)]
+    col = [0, 29, 46, 61, 78, 93]
+    for t in range(R):
+        last = t == R - 1
+        qz(T.qx[:], T.sx[:], T.xi[:, 4 * E:4 * C], XN, "qx", P)
+        mm(ps[:, 0:P], T.qup[:, 128 * t:128 * t + 128], T.sup[:, 128 * t:128 * t + 128], T.qx[:], T.sx[:],
+           "qup%d sup%d qx" % (t, t), "bank0", P)
+        tt(T.lf[:], ps[:, 0:P], T.md[:], A.is_lt, "md bank0", "lf bank0", P, 1.0)
+        scan(T.ls[:], T.nd[:], T.lf[:], A.mult, A.add, "nd lf", "ls", P, 0.5)
+        tt(T.ab[:, 36:54], T.ls[:, 15:P:16], T.ab[:, 0:18], A.mult, "ls amb", "bq")
+        tt(T.ab[:, 54:72], T.ab[:, 36:54], T.ab[:, 18:36], A.add, "bq bf", "bc")
+        ts(lu[:, LB0:LB0 + 18], T.ab[:, 54:72], 2.0, 1.0, A.mult, A.add, "bc", "lb0")
+        ts(lu[:, LB1:LB1 + 18], T.ab[:, 54:72], 2.0, 1.0, A.mult, A.add, "bc", "lb1")
+        cp(lu[:, LB:LB + 18], T.ab[:, 54:72], "bc", "lb")
+        US = "ue"
+        for k in range(NB):
+            w = 2 * (33 + B * k)
+            a0, b0 = (LA1, LB1) if k % 2 else (LA0, LB0)
+            if k:
+                cp(T.d1[:, 96 * k:96 * k + 96:2], T.uu[:, 0:w].indirect(lu[:, a0 + 3 * k:a0 + 3 * k + 3]),
+                   US + " la%d" % (k % 2), "a%d" % k, dur=gcost(B))
+            tt(T.d0[:, 1:96:2], T.uu[:, 0:w].indirect(lu[:, b0 + 3 * k:b0 + 3 * k + 3]), T.d1[:, 96 * k:96 * k + 96:2], A.is_equal,
+               US + " lb%d a%d d0" % (k % 2, k), "d0", dur=gcost(B))
+            scan(T.uu[:, w:w + 96], T.d0[:], T.d1[:, 96 * k:96 * k + 96], A.mult, A.add, "d0 a%d self%d" % (k, k), "u%d" % k, 96)
+            US += " u%d" % k
+        op("v", lambda: V.transpose(T.tt[:, 0:288], T.uu[:, 67:642:2]), US, "tt1", cost(288, 1))
+        op("v", lambda: V.transpose(T.tt[:, 288:608], T.uu[:, 35:674:2]), US + " up", "tt2", cost(320, 1))
+        cp(T.llf[:], T.tt[:].indirect(T.cu[:, cl:cl + 7]), "tt1 tt2 ttp0 ttp1 " + CL, "l0 l1 l2 l3 l4 l5", dur=gcost(112))
+        cp(T.llu[:], T.llf[:], "l0 l1 l2 l3 l4 l5", "llu", 112)
+        for a, b in ((4, 5), (2, 3), (0, 1), (2, 4), (0, 2)):
+            va = T.llf[:, col[a] + 3 * b:col[a] + 18]
+            tt(va, va, T.llf[:, col[b] + 3 * b:col[b] + 18], A.max, "l%d l%d" % (a, b), "l%d" % a)
+        cp(lv[:, LD:LD + 18], T.llf[:, 0:18], "l0", "ld")
+        o = 0
+        for l, (a, z) in enumerate(span):
+            n = 16 * (z - a)
+            src = T.oh[:, 0:275].indirect(T.llu[:, a:z])
+            if (t, l) in ((0, 2), (2, 1), (2, 5)):
+                cp(T.js[:, o:o + n], src, "llu " + OH, "js%d" % l, dur=gcost(n))
+                op("v", lambda o=o, n=n, l=l: V.tensor_reduce(T.pk[:, l:l + 1], T.js[:, o:o + n], AX.X, A.add), "js%d" % l, "pk%d" % l,
+                   cost(n, 1))
+            else:
+                act(T.js[:, o:o + n], src, F.Copy, "llu " + OH, "js%d pk%d" % (l, l), n, True, accum_out=T.pk[:, l:l + 1])
+            o += n
+        tt(T.ni[:], T.pk[:, 0:6].indirect(T.cu[:, 32:34]), T.scl[:], A.mult, "pk0 pk1 pk2 pk3 pk4 pk5 rl0 rl1 sc0 sc1 sc2 sc3 sc4",
+           "n0 n1 n2", dur=gcost(32))
+        ts(T.ni[:, 0:1], T.ni[:, 0:1], 4095, None, A.bitwise_and, None, "n0", "n0")
+        ts(T.ni[:, 2:17], T.ni[:, 2:17], 255, None, A.bitwise_and, None, "n2", "n2")
+        cp(lv[:, LN:LN + 17], T.ni[:, 0:17], "n0 n1 n2", "ln")
+        nsrc = T.tabn[:].indirect(lv[:, LN:LN + 17])
+        if last:
+            cp(T.nb[:, 1:K + 1], nsrc, "tab0 tab1 tab2 ln", "nb", dur=gcost(K))
+        else:
+            act(T.nb[:, 1:K + 1], nsrc, F.Copy, "tab0 tab1 tab2 ln", "nb", K, True)
+        sm = T.sm2
+        for k in range(2):
+            act(T.jb[:, K * k:K * k + K], T.nb[:, 1:K + 1], F.Sign, "nb th%d" % k, "jb%d s%d" % (k, k), K,
+                bias=cf[:, 8 + k:9 + k], accum_out=sm[:, k:k + 1])
+        ts(lv[:, LF:LF + 2], sm[:, 0:2], float(2 * E - K), None, A.is_ge, None, "s0 s1", "lfl")
+        act(T.jb[:, 544:576], T.j16[:, 0:16].indirect(lv[:, LF:LF + 2]), F.Copy, "j16 lfl", "jb2 tau", 32, True, accum_out=sm[:, 2:3])
+        ts(T.fl[:, 0:K], T.nb[:, 1:K + 1], sm[:, 2:3], 1.0, A.subtract, A.is_gt, "nb tau", "fa", K, 0.5)
+        ts(T.fl[:, K:2 * K], T.nb[:, 1:K + 1], sm[:, 2:3], 1.0, A.subtract, A.is_equal, "nb tau", "fb", K, 0.5)
+        scan(T.cs[:, 0:2 * K], T.fl[:], T.fl[:], A.add, A.max, "fa fb", "cs", 2 * K, 0.5)
+        for k in range(2):
+            act(T.jb[:, 576 + 560 * k:1122 + 560 * k], T.cs[:], F.Sign, "cs csp jj%d" % k, "jb%d i%d" % (3 + k, k), 2 * K,
+                bias=cf[:, 10 + k:11 + k], scale=-1.0, accum_out=sm[:, 4 + k:5 + k])
+            ts(sm[:, 6 + k:7 + k], sm[:, 4 + k:5 + k], 1.0, float(K), A.is_lt, A.mult, "i%d" % k, "j%d" % k)
+            ts(lv[:, LC + k:LC + k + 1], sm[:, 4 + k:5 + k], 0.5, sm[:, 6 + k:7 + k], A.mult, A.add, "i%d j%d" % (k, k), "lc%d" % k)
+        for b in range(4):
+            act(T.fg[:, 32 * b:32 * b + 32], plane(t, b).indirect(lv[:, LC:LC + 2]), F.Copy,
+                "xz pn%d%d pe%d%d lc0 lc1" % (t, b, t, b), "fg%d" % b, 32, True)
+        tt(T.key[:, 0:32], T.nb[:, 0:K + 1].indirect(lv[:, LC:LC + 2]), T.jt[:], A.subtract, "nb nb0 lc0 lc1 jt", "key", dur=gcost(32))
+        tt(T.key[:, 32:64], T.key[:, 0:32], T.dg[:], A.mult, "key dg", "k1", 32)
+        scan(T.key[:, 64:96], T.nd[:, 0:32], T.key[:, 32:64], A.mult, A.add, "nd k1", "k2", 32)
+        for k in range(2):
+            act(T.jb[:, 1696 + 32 * k:1728 + 32 * k], T.key[:, 0:32], F.Sign, "key k2", "jb%d r%d" % (5 + k, k), 32,
+                bias=T.key[:, 79 + 16 * k:80 + 16 * k], scale=-1.0, accum_out=sm[:, 10 + k:11 + k])
+        for b in range(4):
+            ts(lv[:, LR + 2 * b:LR + 2 * b + 2], sm[:, 10:12], -2.0, 62.0 + b, A.mult, A.add, "r0 r1", "lr%d" % b)
+        cp(T.fi[:, 0:128].indirect(lv[:, LR:LR + 8]), T.fg[:], "fg0 fg1 fg2 fg3 lr0 lr1 lr2 lr3", "fi", dur=0.55)
+        qz(T["qf%d" % t][:], T["sf%d" % t][:], T.fi[:], "fi", "qf%d" % t, 128)
+        sent = op("g", lambda t=t: hand(g, T, topo, core, way_out[1], T["qf%d" % t][:, 0:32].bitcast(u8), T["sf%d" % t][:], t),
+                  "qf%d" % t, "", 0.3, kind="r")
+        op("net", None, "", "land%d" % t, 0.0, lat=NET, kind="n", after=[sent], sem=("arr%d" % t, arrive))
+        for b in range(4):
+            pr = "xz pn%d%d pe%d%d " % (t, b, t, b)
+            cut = slice(P * b, P * b + P)
+            act(T.g1[:, cut], plane(t, b).indirect(lu[:, LA:LA + 18]), F.Copy, pr + "la", "g1%d" % b, P, True)
+            tt(T.g2[:, cut], plane(t, b).indirect(lu[:, LB:LB + 18]), T.g1[:, cut], A.max, pr + "lb g1%d" % b, "g2%d" % b, dur=gcost(P))
+            tt(T.mt[:, b:4 * P:4], plane(t, b).indirect(lv[:, LD:LD + 18]), T.g2[:, cut], A.add, pr + "ld g2%d" % b, "mt%d" % b,
+               dur=gcost(P))
+        qz(T.qm[:], T.sm[:], T.mt[:], "mt0 mt1 mt2 mt3", "qm", P)
+        for b in range(4):
+            z = ps[:, 512 * (b + 1):512 * (b + 1) + P]
+            bank = "bank%d" % (b + 1)
+            cut = slice(P * b, P * b + P)
+            mm(z, T.qw[:, 128 * b:128 * b + 128], T.sw[:, 128 * b:128 * b + 128], T.qm[:], T.sm[:], "qw sw qm", bank, P)
+            act(T.rr[:, cut], z, F.Relu, bank, "rr%d %s" % (b, bank), P, scale=0.015625)
+            tt(T.xi[:, 4 * E + b:4 * C:4], T.rr[:, cut], plane(t, b, E + 1), A.add, "rr%d pn%d%d xn" % (b, t, b), "xn%d" % b, P)
+            if not last:
+                act(plane(t + 1, b, E + 1), T.xi[:, 4 * E + b:4 * C:4], F.Copy, "xn%d" % b, "pn%d%d" % (t + 1, b), P)
+
+        def unpack(t=t):
+            ins = None
+            for b in (3, 2, 1, 0):
+                a = 96 - 32 * b
+                ins = g.tensor.matmul_mx(ps[:, 2560:2560 + ZL + 32 - a], T.qi[:, 128 * b:128 * b + 128], T.si[:, 128 * b:128 * b + 128],
+                                         T["lc%d" % t][:, a:ZL + 32], T["lp%d" % t][:, a:ZL + 32], b == 3, b == 0)
+            return ins
+        op("t", unpack, "qi lz%d lw%d land%d" % (t, t, t), "bank5", 0.55, lat=0.12)
+        dd = 2560 + 96
+        EP = "ep%d0 ep%d1 ep%d2 ep%d3" % (t, t, t, t)
+        if not last:
+            n = t + 1
+            tt(T.ep[:, 128 * n:128 * n + 128], ps[:, dd:dd + 128], T.ep[:, 128 * t:128 * t + 128], A.max, "bank5 " + EP,
+               "bank5 ep%d0 ep%d1 ep%d2 ep%d3" % (n, n, n, n), 128, 1.0)
+            for b in range(4):
+                act(plane(n, b, 1, E + 1), T.ep[:, 128 * n + 32 * b:128 * n + 32 * b + 32], F.Copy, "ep%d%d" % (n, b),
+                    "pe%d%d" % (n, b), E)
+        else:
+            for b in range(4):
+                tt(T.fi[:, b:4 * E:4], ps[:, dd + 32 * b:dd + 32 * b + 32], T.ep[:, 128 * t + 32 * b:128 * t + 32 * b + 32], A.max,
+                   "bank5 fi qf%d " % t + EP, "xe%d" % b, 32, 1.0)
+    act(T.odb[:], T.it[:, 0:K + 1].indirect(lv[:, LD:LD + 18]), F.Copy, "it ld", "odb", P, True)
+    dma("y", T.od[:], T.odb[0:128:16, :], "odb", "")
+    qz(T.qx[:], T.sx[:], T.xi[:, 4 * E:4 * C], XN, "qx", P)
+    mm(ps[:, 0:P], T.qv[:], T.sv[:], T.qx[:], T.sx[:], "qv qx", "bank0", P)
+    act(T.ys[:, E:C], ps[:, 0:P], F.Copy, "bank0", "bank0 yn", P)
+    dma("y", T.oc[:, 4 * E:4 * C], T.qx[:].bitcast(u8), "qx", "")
+    dma("y", T.y[:, E:C], T.ys[:, E:C], "yn", "")
+    for k in range(4):
+        dma("y", T.osc[4 * k:4 * k + 4, E:C], T.sx[32 * k:32 * k + 4, :], "qx", "")
+    qz(T.qe[:], T.se[:], T.fi[:], "fi xe0 xe1 xe2 xe3", "qe", 128)
+    mm(ps[:, 3072:3072 + 128], T.qv[:], T.sv[:], T.qe[:], T.se[:], "qv qe", "bank6", 128)
+    cp(T.ys[:, 0:E], ps[:, 3072:3072 + E], "bank6", "bank6 ye", 32)
+    dma("y", T.oc[:, 0:4 * E], T.qe[:, 0:E].bitcast(u8), "qe", "")
+    for k in range(4):
+        dma("ys"[k % 2], T.osc[4 * k:4 * k + 4, 0:E], T.se[32 * k:32 * k + 4, 0:E], "qe", "")
+    dma("s", T.y[:, 0:E], T.ys[:, 0:E], "ye", "")
+    emit(g, T, ops)

@@ -5,33 +5,30 @@ from concourse.mybir import dt, AluOpType as A, ActivationFunctionType as F, Axi
 C, E, B, NB, P, R = 320, 32, 48, 6, 288, 3
 K = C - B
 PL = 336
-ZL = 192
 X4, S_, BF, F32, U8 = "float8_e4m3fn_x4", "sbuf", "bfloat16", "float32", "uint8"
 SCRATCH = {"ps": ("psum", [128, 4096], F32)}
-for _n, _w in (("xi", 4 * C), ("xp", 12 * PL), ("ep", 128 * R), ("ut", 512), ("vt", 512), ("et", 2048), ("ones", 512),
-               ("zt", 4 * ZL), ("nd", P), ("lf", P), ("ls", P), ("d0", 96), ("jb", 1792), ("nb", 288), ("fl", 2 * K),
-               ("cs", 2 * K + 2), ("fg", 128), ("fi", 512), ("g1", 4 * P), ("g2", 4 * P), ("mt", 4 * P)):
+for _n, _w in (("xi", 4 * C), ("xp", 12 * PL), ("ut", 512), ("vt", 512), ("et", 2048), ("ones", 512), ("nd", P), ("lf", P),
+               ("ls", P), ("d0", 128), ("jb", 1792), ("nb", 288), ("fl", 2 * K), ("cs", 2 * K + 2), ("fi", 512), ("dp", 4 * K),
+               ("g1", 4 * P), ("g2", 4 * P), ("mt", 4 * P)):
     SCRATCH[_n] = (S_, [128, _w], BF)
-for _n, _w in (("cf", 64), ("j16", P), ("md", P), ("dg", 32), ("it", 336), ("oh", 288), ("tabn", 560), ("scl", 32), ("jt", 32),
-               ("ab", 96), ("uu", 688), ("d1", 576), ("tt", 616), ("llf", 112), ("js", 1152), ("pk", 8), ("sm2", 32), ("key", 96),
-               ("rr", 4 * P), ("ys", C), ("odb", P)):
+for _n, _w in (("cf", 64), ("j16", P), ("md", P), ("dg", 32), ("it", 336), ("oh", 288), ("tabn", 560), ("scl", 32), ("jt", 64),
+               ("ab", 96), ("uu", 688), ("d1", 576), ("tt", 616), ("llf", 112), ("js", 1152), ("pk", 8), ("sm2", 32), ("key", 128),
+               ("hb", 128), ("rr", 4 * P), ("ys", C), ("odb", P)):
     SCRATCH[_n] = (S_, [128, _w], F32)
 for _n, _w in (("pai", 32), ("pbi", 32), ("ci", 64), ("ni", 32)):
     SCRATCH[_n] = (S_, [128, _w], "int32")
-for _n, _w in (("cu", 160), ("cw", 48), ("llu", 112)):
+for _n, _w in (("cu", 160), ("cw", 48), ("llu", 112), ("hs0", 2), ("hs1", 2), ("hs2", 2), ("hl0", 2), ("hl1", 2), ("hl2", 2)):
     SCRATCH[_n] = (S_, [128, _w], "uint16")
 for _n, _w in (("u", 128), ("v", 128), ("up", 128 * R), ("w", 512), ("x", P), ("e", 128), ("m", P), ("i", 512),
-               ("f0", 128), ("f1", 128), ("f2", 128)):
+               ("f0", K), ("f1", K), ("f2", K), ("l0", K), ("l1", K), ("l2", K)):
     SCRATCH["q" + _n] = (S_, [128, _w], X4)
     SCRATCH["s" + _n] = (S_, [128, _w], U8)
-for _t in range(R):
-    SCRATCH["lc%d" % _t] = (S_, [128, ZL + 32], X4)
-    SCRATCH["lp%d" % _t] = (S_, [128, ZL + 128], U8)
-NDMA = 26
-SEMAPHORES = ["cv", "cs", "ct", "cg", "sent"] + ["arr%d" % t for t in range(R)] + ["dm%d" % i for i in range(NDMA)]
-CY = 1.04e-3
-LAT, NET = 0.08, 4.5
-TRIES = 150000
+NDMA = 22
+SEMAPHORES = (["cv", "cs", "ct", "cg", "sent"] + ["big%d" % t for t in range(R)] + ["lst%d" % t for t in range(R)]
+              + ["dm%d" % i for i in range(NDMA)])
+CY = 0.85e-3
+CASES = ((0.06, 1.0, 0.08, 4.5), (0.0, 1.0, 0.2, 4.5), (0.04, 1.3, 0.12, 5.5))
+TRIES = 100000
 PLAN = {}
 
 
@@ -44,29 +41,25 @@ def route(T, topo, r):
     return [src, (near or able)[0], dst]
 
 
-def halves(topo, src, dst):
-    e = topo.engines(src, dst)
-    h = len(e) // 2
-    return sum(1 << i for i in e[:h]), sum(1 << i for i in e[h:2 * h]), 2 * h
-
-
-def hand(g, T, topo, src, dst, codes, plane, t):
+def hand(g, T, topo, src, dst, pairs, sem):
     rid, pid = topo.addr(dst, src)
-    m0, m1, n = halves(topo, src, dst)
-    to, sem = DstId(rid=rid, pnc=pid), T.sem["arr%d" % t]
-    g.remote_dma_fused([
-        RemoteDMATransfer(dst_ids=[to], dma_engine_mask=m0, remote_sem=sem, src=codes,
-                          dst=T["lc%d" % t][:, ZL:ZL + 32].bitcast(dt.uint8)),
-        RemoteDMATransfer(dst_ids=[to], dma_engine_mask=m1, remote_sem=sem, src=plane,
-                          dst=T["lp%d" % t][:, ZL:ZL + 128])], local_sem=T.sem.sent)
-    return n
+    for out, in_ in pairs:
+        g.remote_dma(out, in_, T.sem[sem], T.sem.sent, pid, rid, topo.mask(src, dst))
+    return len(pairs) * len(topo.engines(src, dst))
+
+
+def hand_big(g, T, topo, src, dst, a, t):
+    return hand(g, T, topo, src, dst, [(T["ql%d" % t][:].bitcast(dt.uint8), T["q%s%d" % (a, t)][:].bitcast(dt.uint8)),
+                                       (T["sl%d" % t][:], T["s%s%d" % (a, t)][:])], "big%d" % t)
 
 
 def relay(g, T, topo, src, me, dst):
-    n = 0
+    n, e = 0, len(topo.engines(src, me))
     for t in range(R):
-        g.wait_ge(T.sem["arr%d" % t], halves(topo, src, me)[2])
-        n += hand(g, T, topo, me, dst, T["lc%d" % t][:, ZL:ZL + 32].bitcast(dt.uint8), T["lp%d" % t][:, ZL:ZL + 128], t)
+        g.wait_ge(T.sem["big%d" % t], 2 * e)
+        n += hand_big(g, T, topo, me, dst, "l", t)
+        g.wait_ge(T.sem["lst%d" % t], e)
+        n += hand(g, T, topo, me, dst, [(T["hl%d" % t][:], T["hl%d" % t][:])], "lst%d" % t)
     g.wait_ge(T.sem.sent, n)
 
 
@@ -79,7 +72,13 @@ def plan(ops):
             succ[d].append(i)
     qs = sorted(set(o["q"] for o in ops))
     q = [qs.index(o["q"]) for o in ops]
-    dur, lat = [o["dur"] for o in ops], [o["lat"] for o in ops]
+    either = [i for i in range(n) if ops[i]["alt"]]
+    iv, is_ = qs.index("v"), qs.index("s")
+    cases = []
+    for add, f, w, net in CASES:
+        cases.append(([o["dur"] * f + add if o["kind"] == "c" else o["dur"] for o in ops],
+                      [o["lat"] + (w if o["kind"] == "c" else net if o["kind"] == "n" else 0.0) for o in ops]))
+    dur, lat = cases[0]
     prio = [0.0] * n
     for i in range(n - 1, -1, -1):
         prio[i] = dur[i] + lat[i] + 1e-6 + max([prio[s] for s in succ[i]] + [0.0])
@@ -91,43 +90,54 @@ def plan(ops):
         return (seed[0] >> 33) / float(1 << 31)
 
     def run(od):
-        free, done = [0.0] * len(qs), [0.0] * n
-        for i in od:
-            s = free[q[i]]
-            for d in dep[i]:
-                if done[d] > s:
-                    s = done[d]
-            s += dur[i]
-            free[q[i]] = s
-            done[i] = s + lat[i]
-        return max(done) + 0.02 * sum(done) / n, done
+        total = 0.0
+        for du, la in cases[::-1]:
+            free, done = [0.0] * len(qs), [0.0] * n
+            for i in od:
+                s = free[q[i]]
+                for d in dep[i]:
+                    if done[d] > s:
+                        s = done[d]
+                s += du[i]
+                free[q[i]] = s
+                done[i] = s + la[i]
+            total += max(done) + 0.02 * sum(done) / n
+        return total / len(cases), done
 
     cur, done = run(order)
-    best, bo = cur, list(order)
+    best, bo, bq = cur, list(order), list(q)
     for it in range(TRIES):
         if it % 1000 == 0:
             order = sorted(order, key=lambda i: done[i] - lat[i] - dur[i])
             cur, done = run(order)
-        a = int(rnd() * n)
-        i = order[a]
-        step = 1 if rnd() < 0.5 else -1
-        stop = succ[i] if step > 0 else dep[i]
-        b, left = a, 1 + int(rnd() ** 3 * 12)
-        while left and 0 <= b + step < n and order[b + step] not in stop:
-            b += step
-            if q[order[b]] == q[i]:
-                left -= 1
-        if b == a:
-            continue
-        new = order[:a] + order[a + 1:]
-        new.insert(b, i)
+        flip, new = None, order
+        if rnd() < 0.04:
+            flip = either[int(rnd() * len(either))]
+            q[flip] = iv + is_ - q[flip]
+        else:
+            a = int(rnd() * n)
+            i = order[a]
+            step = 1 if rnd() < 0.5 else -1
+            stop = succ[i] if step > 0 else dep[i]
+            b, left = a, 1 + int(rnd() ** 3 * 12)
+            while left and 0 <= b + step < n and order[b + step] not in stop:
+                b += step
+                if q[order[b]] == q[i]:
+                    left -= 1
+            if b == a:
+                continue
+            new = order[:a] + order[a + 1:]
+            new.insert(b, i)
         got, dn = run(new)
         if got <= cur or rnd() < math.exp((cur - got) / (0.15 * (1 - it / TRIES) + 0.003)):
             cur, order, done = got, new, dn
             if got < best:
-                best, bo = got, list(new)
+                best, bo, bq = got, list(new), list(q)
+        elif flip is not None:
+            q[flip] = iv + is_ - q[flip]
+    q[:] = bq
     done = run(bo)[1]
-    return max(done), bo, [done[i] - lat[i] - dur[i] for i in range(n)]
+    return best, bo, [done[i] - lat[i] - dur[i] for i in range(n)], [qs[k] for k in bq]
 
 
 def emit(g, T, ops):
@@ -148,14 +158,16 @@ def emit(g, T, ops):
         o["dep"] = dep
     if "p" not in PLAN:
         PLAN["p"] = plan(ops)
-    _end, order, _at = PLAN["p"]
+    _end, order, _at, where = PLAN["p"]
     place = {i: k for k, i in enumerate(order)}
     queue = {"v": g.vector, "s": g.scalar, "t": g.tensor, "g": g, "y": g.sync}
     count, known, ndma = {}, {q: {} for q in queue}, 0
     for i in order:
         o = ops[i]
-        q = o["q"]
-        if q == "net":
+        q = where[i]
+        if q != o["q"]:
+            o["q"], o["fn"] = q, o["alt"]
+        if o["kind"] == "n":
             o["sig"], o["clock"] = o["sem"], {}
             count[o["sem"][0]] = o["sem"][1]
             continue
@@ -205,16 +217,16 @@ def rank_program(g, core, T, topo):
                 relay(g, T, topo, way[0], core, way[2])
         return
     way_out, way_in = route(T, topo, rank), route(T, topo, (rank - 1) % n_ranks)
-    arrive = halves(topo, way_in[-2], core)[2]
+    arrive = len(topo.engines(way_in[-2], core))
     V, S, ops = g.vector, g.scalar, []
 
-    def op(q, fn, r, w, dur, lat=LAT, kind="c", after=(), sem=None):
+    def op(q, fn, r, w, dur, lat=0.0, kind="c", after=(), sem=None, alt=None):
         ops.append({"q": q, "fn": fn, "r": r.split(), "w": w.split(), "dur": dur, "lat": lat, "kind": kind,
-                    "after": list(after), "sem": sem})
+                    "after": list(after), "sem": sem, "alt": alt})
         return len(ops) - 1
 
     def cost(n, c):
-        return max(0.07, 0.03 + n * c * CY)
+        return max(0.06, 0.03 + n * c * CY)
 
     def gcost(n):
         return 0.06 + n * 1.6 * CY
@@ -230,25 +242,30 @@ def rank_program(g, core, T, topo):
     def cp(out, a, r, w, n=16, c=1.0, dur=None):
         return op("v", lambda: V.tensor_copy(out, a), r, w, dur or cost(n, c))
 
-    def ms(out, val, w, n=16):
-        return op("v", lambda: V.memset(out, val), "", w, cost(n, 0.7))
-
     def scan(out, a, b, o0, o1, r, w, n, c=1.0):
         return op("v", lambda: V.tensor_tensor_scan(out, a, b, 0.0, o0, o1), r, w, cost(n, c))
 
     def qz(out, sc, a, r, w, n):
-        return op("v", lambda: V.quantize_mx(out, sc, a), r, w, 0.03 + n * 4 * 0.27e-3)
+        return op("v", lambda: V.quantize_mx(out, sc, a), r, w, 0.03 + n * 4 * 0.22e-3)
 
     def act(out, a, f, r, w, n=16, gather=False, **kw):
-        return op("s", lambda: S.activation(out, a, f, **kw), r, w, gcost(n) + 0.02 if gather else 0.07 + n * CY)
+        return op("s", lambda: S.activation(out, a, f, **kw), r, w, gcost(n) + 0.02 if gather else 0.06 + n * CY)
+
+    def move(out, a, r, w, n, gather=False):
+        return op("s", lambda: S.activation(out, a, F.Copy), r, w, gcost(n) + 0.01 if gather else 0.06 + n * CY,
+                  alt=lambda: V.tensor_copy(out, a))
 
     def iota(out, pat, base, cm, w, n, flt=True):
         if flt:
-            return op("g", lambda: g.iota(out, pat, base, cm, allow_small_or_imprecise_dtypes=True), "", w, 0.15 + 2 * n * CY)
-        return op("g", lambda: g.iota(out, pat, base, cm), "", w, 0.15 + 2 * n * CY)
+            return op("g", lambda: g.iota(out, pat, base, cm, allow_small_or_imprecise_dtypes=True), "", w, 0.13 + 2 * n * CY)
+        return op("g", lambda: g.iota(out, pat, base, cm), "", w, 0.13 + 2 * n * CY)
+
+    def fill(out, val, w, n):
+        return op("s", lambda: S.activation(out, T.it[:, 0:n], F.Identity, scale=0.0, bias=val), "it", w, 0.06 + n * CY,
+                  alt=lambda: V.memset(out, val))
 
     def mm(out, lq, lsc, rq, rsc, r, w, n):
-        return op("t", lambda: g.tensor.matmul_mx(out, lq, lsc, rq, rsc, True, True), r, w, 0.03 + n * 0.6e-3, lat=0.12)
+        return op("t", lambda: g.tensor.matmul_mx(out, lq, lsc, rq, rsc, True, True), r, w, 0.03 + n * 0.6e-3, lat=0.04)
 
     def dma(q, out, a, r, w, lat=2.0):
         e = {"y": g.sync, "s": g.scalar, "g": g}[q]
@@ -261,6 +278,7 @@ def rank_program(g, core, T, topo):
     u8 = dt.uint8
     ps = T.ps
     cf = T.cf
+    I_ = F.Identity
     dma("y", T.xi[:], T.x[:], "", "xn xe", 2.6)
     dma("s", T.ut[:], T.u[:], "", "ut", 2.3)
     dma("y", T.pai[:, 0:18], T.pa[:], "", "pa", 2.6)
@@ -269,6 +287,7 @@ def rank_program(g, core, T, topo):
     dma("y", T.sw[:], T.ws[:], "pa", "sw", 3.0)
     dma("y", T.vt[:], T.v[:], "pa", "vt", 3.0)
     iota(T.ci[:, 0:1], [[0, 1]], 0, 1, "p", 1, False)
+    iota(T.ci[:, 6:7], [[0, 1]], 5, 0, "c6", 1, False)
     iota(T.ci[:, 8:32], [[1, R], [16, 8]], 0, 0, "uli", 24, False)
     iota(T.j16[:], [[0, 18], [1, 16]], 0, 0, "j16", P)
     iota(T.it[:], [[1, 336]], -1, 0, "it", 336)
@@ -276,7 +295,6 @@ def rank_program(g, core, T, topo):
     iota(T.tabn[:, 144:256], [[1, 112]], 1, 0, "tab1", 112)
     iota(T.tabn[:, 256:560], [[1, 304]], 1, 0, "tab2", 304)
     iota(T.fi[:], [[0, 512]], 0, 0, "fi", 512)
-    iota(T.zt[:], [[0, 4 * ZL]], 0, 0, "zt", 4 * ZL)
     iota(T.ones[:], [[0, 512]], 1, 0, "ones", 512)
     lane = cf[:, 0:1]
     ts(T.ci[:, 1:2], T.ci[:, 0:1], 15, None, A.bitwise_and, None, "p", "li")
@@ -285,87 +303,87 @@ def rank_program(g, core, T, topo):
     ts(T.nd[:], T.j16[:], lane, None, A.not_equal, None, "j16 lane", "nd", P)
     act(T.md[:], T.nd[:], F.Copy, "nd", "md", P, scale=-1e29)
     ts(T.dg[:], T.j16[:, 0:32], lane, None, A.is_equal, None, "j16 lane", "dg", 32)
-    act(T.jt[:], T.it[:, 1:33], F.Copy, "it", "jt", 32, scale=1.0 / 64)
     ts(T.ci[:, 2:3], T.ci[:, 0:1], 4, None, A.logical_shift_right, None, "p", "c2")
     tt(T.ci[:, 3:4], T.ci[:, 2:3], T.ci[:, 0:1], A.add, "c2 p", "c3")
     ts(T.ci[:, 4:5], T.ci[:, 3:4], 1, None, A.bitwise_and, None, "c3", "c4")
     ts(cf[:, 1:2], T.ci[:, 4:5], 304.0, None, A.mult, None, "c4", "odd")
-    ts(cf[:, 2:3], lane, 16.0, cf[:, 1:2], A.mult, A.add, "lane odd", "be")
+    act(cf[:, 16:17], lane, I_, "lane odd", "be", scale=16.0, bias=cf[:, 1:2])
     ts(cf[:, 3:4], lane, 16.0, cf[:, 1:2], A.mult, A.subtract, "lane odd", "bo")
-    act(cf[:, 4:5], T.dg[:, 15:16], F.Identity, "dg bo", "bo1", scale=1000.0, bias=cf[:, 3:4])
-    act(cf[:, 5:6], T.dg[:, 0:1], F.Identity, "dg bo1", "bo2", scale=1000.0, bias=cf[:, 4:5])
-    ts(cf[:, 6:7], lane, 2.0, 1000.0, A.is_ge, A.mult, "lane", "big")
-    act(cf[:, 7:8], cf[:, 6:7], F.Identity, "big be", "be1", bias=cf[:, 2:3])
+    act(cf[:, 4:5], T.dg[:, 15:16], I_, "dg bo", "bo1", scale=1000.0, bias=cf[:, 3:4])
+    act(cf[:, 5:6], T.dg[:, 0:1], I_, "dg bo1", "bo2", scale=1000.0, bias=cf[:, 4:5])
+    act(cf[:, 6:7], T.dg[:, 0:1], I_, "dg be", "big", scale=-1000.0, bias=cf[:, 16:17])
+    act(cf[:, 7:8], T.dg[:, 1:2], I_, "dg big", "be1", scale=-1000.0, bias=cf[:, 6:7])
     cl = 24
-    cp(T.cu[:, cl:cl + 1], cf[:, 2:3], "be", "cl0")
-    ts(T.cu[:, cl + 1:cl + 2], cf[:, 7:8], 256.0, 608.0, A.add, A.min, "be1", "cl1")
-    ts(T.cu[:, cl + 2:cl + 3], cf[:, 4:5], 353.0, 609.0, A.add, A.min, "bo1", "cl2")
-    ts(T.cu[:, cl + 3:cl + 4], cf[:, 2:3], 34.0, None, A.add, None, "be", "cl3")
-    ts(T.cu[:, cl + 4:cl + 5], cf[:, 5:6], 355.0, 609.0, A.add, A.min, "bo2", "cl4")
-    ts(T.cu[:, cl + 5:cl + 6], cf[:, 2:3], 36.0, None, A.add, None, "be", "cl5")
-    ts(T.cu[:, cl + 6:cl + 7], cf[:, 5:6], 357.0, 609.0, A.add, A.min, "bo2", "cl6")
-    CL = "cl0 cl1 cl2 cl3 cl4 cl5 cl6"
-    ms(T.tt[:, 608:609], 274.0, "ttp0")
-    ms(T.tt[:, 609:616], 273.0, "ttp1")
+    ts(cf[:, 17:18], cf[:, 7:8], 1256.0, 608.0, A.add, A.min, "be1", "cl1")
+    for c, src, tag, add in ((18, 4, "bo1", 353.0), (19, 16, "be", 34.0), (20, 5, "bo2", 355.0), (21, 16, "be", 36.0), (22, 5, "bo2", 357.0)):
+        act(cf[:, c:c + 1], cf[:, src:src + 1], I_, tag, "cl%d" % (c - 16), bias=add)
+    ts(T.cu[:, cl:cl + 7], cf[:, 16:23], 609.0, None, A.min, None, "be cl1 cl2 cl3 cl4 cl5 cl6", "cl")
+    fill(T.tt[:, 608:609], 274.0, "ttp0", 1)
+    fill(T.tt[:, 609:616], 273.0, "ttp1", 7)
     ts(T.ci[:, 5:6], lane, 1.0 / 3, None, A.mult, None, "lane", "c5")
-    cp(T.cu[:, 32:33], T.ci[:, 5:6], "c5", "rl0")
-    ms(T.cu[:, 33:34], 5, "rl1")
-    ms(T.scl[:, 0:1], 1.0, "sc0")
-    ms(T.scl[:, 1:2], 1.0 / 4096, "sc1")
-    ms(T.scl[:, 2:32:3], 1.0, "sc2")
-    ms(T.scl[:, 3:32:3], 1.0 / 256, "sc3")
-    ms(T.scl[:, 4:32:3], 1.0 / 65536, "sc4")
+    cp(T.cu[:, 32:34], T.ci[:, 5:7], "c5 c6", "rl")
+    fill(T.scl[:, 0:1], 1.0, "sc0", 1)
+    fill(T.scl[:, 1:2], 1.0 / 4096, "sc1", 1)
+    fill(T.scl[:, 2:32:3], 1.0, "sc2", 10)
+    fill(T.scl[:, 3:32:3], 1.0 / 256, "sc3", 10)
+    fill(T.scl[:, 4:32:3], 1.0 / 65536, "sc4", 10)
     for k in range(2):
-        ts(cf[:, 8 + k:9 + k], lane, -1.0, -1.5 - 16 * k, A.mult, A.add, "lane", "th%d" % k)
-        ts(cf[:, 10 + k:11 + k], lane, 0.5 + 16 * k, None, A.add, None, "lane", "jj%d" % k)
-    ms(T.cs[:, 2 * K:2 * K + 2], -1.0, "csp")
-    ms(T.oh[:, 0:1], 0.0, "oh0")
-    ms(T.oh[:, 273:274], -112.0 * 65793 / 16, "oh1")
-    ms(T.oh[:, 274:275], 256.0 * 4097 / 16, "oh2")
+        act(cf[:, 8 + k:9 + k], lane, I_, "lane", "th%d" % k, scale=-1.0, bias=-1.5 - 16 * k)
+        act(cf[:, 10 + k:11 + k], lane, I_, "lane", "jj%d" % k, bias=0.5 + 16 * k)
+        act(cf[:, 12 + k:13 + k], cf[:, 10 + k:11 + k], F.Copy, "jj%d" % k, "jn%d" % k, scale=-1.0 / 64)
+        act(T.jt[:, 32 * k:32 * k + 32], T.it[:, 1:33], I_, "it jn%d" % k, "jt%d" % k, 32, scale=1.0 / 64, bias=cf[:, 12 + k:13 + k])
+    fill(T.cs[:, 2 * K:2 * K + 2], -1.0, "csp", 2)
+    fill(T.oh[:, 0:1], 0.0, "oh0", 1)
+    fill(T.oh[:, 273:274], -112.0 * 65793 / 16, "oh1", 1)
+    fill(T.oh[:, 274:275], 256.0 * 4097 / 16, "oh2", 1)
     OH = "oh0 oh1 oh2"
     for c in range(17):
         wgt = 4096.0 ** c if c < 2 else 256.0 ** ((c - 2) % 3)
         act(T.oh[:, 1 + 16 * c:17 + 16 * c], T.dg[:, 0:16], F.Copy, "dg", "ohc%d" % c, 16, scale=wgt)
         OH += " ohc%d" % c
-    ms(T.uu[:, 0:66], 0.0, "ue", 66)
-    ms(T.uu[:, 642:674], 0.0, "up", 32)
-    ms(T.d0[:], 0.0, "d0", 96)
+    fill(T.uu[:, 0:66], 0.0, "ue", 66)
+    fill(T.uu[:, 642:674], 0.0, "up", 32)
+    fill(T.d0[:], 0.0, "d0", 128)
     act(T.uu[:, 3:66:2], T.it[:, 2:34], F.Copy, "it dg", "ue", 32, scale=T.dg[:, 0:1])
     for k in range(NB):
         act(T.d1[:, 96 * k + 1:96 * k + 96:2], T.it[:, 34 + B * k:34 + B * k + B], F.Copy, "it dg", "self%d" % k, B,
             scale=T.dg[:, k + 1:k + 2])
-    ms(T.nb[:, 0:1], 0.0, "nb0")
-    ms(T.xp[:, 0:12 * PL:PL], 0.0, "xz")
+    fill(T.nb[:, 0:1], 0.0, "nb0", 1)
+    fill(T.xp[:, 0:12 * PL:PL], 0.0, "xz", 12)
     for b in range(4):
         op("g", lambda b=b: g.affine_select(T.et[:, 512 * b:512 * b + 512], T.ones[:], [[1, 512]], A.is_equal, 0.0, -b, -4),
-           "ones", "et%d" % b, 1.2)
+           "ones", "et%d" % b, 1.05)
     qz(T.qi[:], T.si[:], T.et[:], "et0 et1 et2 et3", "qi", 512)
-    qz(T.lc0[:, 0:ZL], T.lp0[:, 0:ZL], T.zt[:], "zt", "lz0 lw0", ZL)
-    for t in range(1, R):
-        dma("y", T["lc%d" % t][:, 0:ZL].bitcast(u8), T.lc0[:, 0:ZL].bitcast(u8), "lz0", "lz%d" % t)
-        dma("y", T["lp%d" % t][:, 0:ZL], T.lp0[:, 0:ZL], "lz0", "lw%d" % t)
-    LA, LA0, LA1, LB, LB0, LB1, LD, LN, LF, LC, LR = 34, 52, 71, 90, 108, 127, 0, 18, 36, 38, 40
+    LA, LA0, LA1, LB, LB0, LD, LN, LF, LC, LR = 34, 52, 71, 90, 108, 0, 18, 36, 38, 40
     lu, lv = T.cu, T.cw
     ts(lu[:, LA:LA + 18], T.pai[:, 0:18], 1.0, None, A.add, None, "pa", "la")
     ts(lu[:, LA0:LA0 + 18], T.pai[:, 0:18], 2.0, 3.0, A.mult, A.add, "pa", "la0")
     ts(lu[:, LA1:LA1 + 18], T.pai[:, 0:18], 2.0, 3.0, A.mult, A.add, "pa", "la1")
     tt(T.ab[:, 0:18], T.pai[:, 0:18], T.pbi[:, 0:18], A.subtract, "pa pb", "amb")
     ts(T.ab[:, 18:36], T.pbi[:, 0:18], 1.0, None, A.add, None, "pb", "bf")
-    cp(T.d1[:, 0:96:2], T.uu[:, 0:66].indirect(lu[:, LA0:LA0 + 3]), "ue la0", "a0", dur=gcost(B))
+    move(T.d1[:, 0:96:2], T.uu[:, 0:66].indirect(lu[:, LA0:LA0 + 3]), "ue la0", "a0", B, True)
     qz(T.qu[:], T.su[:], T.ut[:], "ut", "qu", 128)
     qz(T.qv[:], T.sv[:], T.vt[:], "vt", "qv", 128)
     for t in range(R):
         cp(T.qup[:, 128 * t:128 * t + 128].bitcast(dt.uint32), T.qu[:].bitcast(dt.uint32).indirect(T.cu[:, 8 * t:8 * t + 8]),
            "qu ulu", "qup%d" % t, dur=gcost(128))
-        act(T.sup[:, 128 * t:128 * t + 128], T.su[:].indirect(T.cu[:, 8 * t:8 * t + 8]), F.Copy, "qu ulu", "sup%d" % t, 128, True)
+        move(T.sup[:, 128 * t:128 * t + 128], T.su[:].indirect(T.cu[:, 8 * t:8 * t + 8]), "qu ulu", "sup%d" % t, 128, True)
     for b in range(4):
         act(plane(0, b, 1), T.xi[:, b:4 * C:4], F.Copy, "xn xe", "pn0%d pe0%d" % (b, b), C)
-        act(T.ep[:, 32 * b:32 * b + 32], T.xi[:, b:4 * E:4], F.Copy, "xe", "ep0%d" % b, E)
-    XN = "xn xn0 xn1 xn2 xn3"
+    XN, XE = "xn xn0 xn1 xn2 xn3", " xe xe0 xe1 xe2 xe3"
     span = [(0, 19), (32, 48), (52, 65), (70, 80), (90, 97), (108, 112)]
     col = [0, 29, 46, 61, 78, 93]
     for t in range(R):
         last = t == R - 1
+        qz(T["qf%d" % t][:], T["sf%d" % t][:], T.xi[:, 0:4 * K], XN + XE, "qf%d" % t, K)
+        sent = op("g", lambda t=t: hand_big(g, T, topo, core, way_out[1], "f", t), "qf%d" % t, "", 0.8, kind="r")
+        op("nb", None, "", "land%d" % t, 0.0, lat=3.5, kind="n", after=[sent], sem=("big%d" % t, 2 * arrive))
+        for b in range(4):
+            o = 512 * (5 + b % 3)
+            bank = "bank%d" % (5 + b % 3)
+            mm(ps[:, o:o + K], T.qi[:, 128 * b:128 * b + 128], T.si[:, 128 * b:128 * b + 128], T["ql%d" % t][:], T["sl%d" % t][:],
+               "qi land%d" % t, bank, K)
+            move(T.dp[:, K * b:K * b + K], ps[:, o:o + K], bank, "dp%d %s" % (b, bank), K)
         qz(T.qx[:], T.sx[:], T.xi[:, 4 * E:4 * C], XN, "qx", P)
         mm(ps[:, 0:P], T.qup[:, 128 * t:128 * t + 128], T.sup[:, 128 * t:128 * t + 128], T.qx[:], T.sx[:],
            "qup%d sup%d qx" % (t, t), "bank0", P)
@@ -374,23 +392,23 @@ def rank_program(g, core, T, topo):
         tt(T.ab[:, 36:54], T.ls[:, 15:P:16], T.ab[:, 0:18], A.mult, "ls amb", "bq")
         tt(T.ab[:, 54:72], T.ab[:, 36:54], T.ab[:, 18:36], A.add, "bq bf", "bc")
         ts(lu[:, LB0:LB0 + 18], T.ab[:, 54:72], 2.0, 1.0, A.mult, A.add, "bc", "lb0")
-        ts(lu[:, LB1:LB1 + 18], T.ab[:, 54:72], 2.0, 1.0, A.mult, A.add, "bc", "lb1")
         cp(lu[:, LB:LB + 18], T.ab[:, 54:72], "bc", "lb")
         US = "ue"
         for k in range(NB):
-            w = 2 * (33 + B * k)
-            a0, b0 = (LA1, LB1) if k % 2 else (LA0, LB0)
+            w, x = 2 * (33 + B * k), k % 2
+            a0 = LA1 if x else LA0
             if k:
-                cp(T.d1[:, 96 * k:96 * k + 96:2], T.uu[:, 0:w].indirect(lu[:, a0 + 3 * k:a0 + 3 * k + 3]),
-                   US + " la%d" % (k % 2), "a%d" % k, dur=gcost(B))
-            tt(T.d0[:, 1:96:2], T.uu[:, 0:w].indirect(lu[:, b0 + 3 * k:b0 + 3 * k + 3]), T.d1[:, 96 * k:96 * k + 96:2], A.is_equal,
-               US + " lb%d a%d d0" % (k % 2, k), "d0", dur=gcost(B))
-            scan(T.uu[:, w:w + 96], T.d0[:], T.d1[:, 96 * k:96 * k + 96], A.mult, A.add, "d0 a%d self%d" % (k, k), "u%d" % k, 96)
+                move(T.d1[:, 96 * k:96 * k + 96:2], T.uu[:, 0:w].indirect(lu[:, a0 + 3 * k:a0 + 3 * k + 3]),
+                     US + " la%d" % x, "a%d" % k, B, True)
+            tt(T.d0[:, 33 - 32 * x:128:2], T.uu[:, 0:w].indirect(lu[:, LB0 + 3 * k - x:LB0 + 3 * k + 3]),
+               T.d1[:, 96 * k - 32 * x:96 * k + 96:2], A.is_equal, US + " lb0 a%d a%d d0" % (k - x, k), "d0", dur=gcost(B + 16 * x))
+            scan(T.uu[:, w:w + 96], T.d0[:, 32:128], T.d1[:, 96 * k:96 * k + 96], A.mult, A.add, "d0 a%d self%d" % (k, k), "u%d" % k, 96)
             US += " u%d" % k
         op("v", lambda: V.transpose(T.tt[:, 0:288], T.uu[:, 67:642:2]), US, "tt1", cost(288, 1))
         op("v", lambda: V.transpose(T.tt[:, 288:608], T.uu[:, 35:674:2]), US + " up", "tt2", cost(320, 1))
-        cp(T.llf[:], T.tt[:].indirect(T.cu[:, cl:cl + 7]), "tt1 tt2 ttp0 ttp1 " + CL, "l0 l1 l2 l3 l4 l5", dur=gcost(112))
-        cp(T.llu[:], T.llf[:], "l0 l1 l2 l3 l4 l5", "llu", 112)
+        pick = T.tt[:].indirect(T.cu[:, cl:cl + 7])
+        cp(T.llu[:], pick, "tt1 tt2 ttp0 ttp1 cl", "llu", dur=gcost(112))
+        move(T.llf[:], pick, "tt1 tt2 ttp0 ttp1 cl", "l0 l1 l2 l3 l4 l5", 112, True)
         for a, b in ((4, 5), (2, 3), (0, 1), (2, 4), (0, 2)):
             va = T.llf[:, col[a] + 3 * b:col[a] + 18]
             tt(va, va, T.llf[:, col[b] + 3 * b:col[b] + 18], A.max, "l%d l%d" % (a, b), "l%d" % a)
@@ -399,23 +417,19 @@ def rank_program(g, core, T, topo):
         for l, (a, z) in enumerate(span):
             n = 16 * (z - a)
             src = T.oh[:, 0:275].indirect(T.llu[:, a:z])
-            if (t, l) in ((0, 2), (2, 1), (2, 5)):
+            if (t, l) == (2, 1):
                 cp(T.js[:, o:o + n], src, "llu " + OH, "js%d" % l, dur=gcost(n))
                 op("v", lambda o=o, n=n, l=l: V.tensor_reduce(T.pk[:, l:l + 1], T.js[:, o:o + n], AX.X, A.add), "js%d" % l, "pk%d" % l,
                    cost(n, 1))
             else:
                 act(T.js[:, o:o + n], src, F.Copy, "llu " + OH, "js%d pk%d" % (l, l), n, True, accum_out=T.pk[:, l:l + 1])
             o += n
-        tt(T.ni[:], T.pk[:, 0:6].indirect(T.cu[:, 32:34]), T.scl[:], A.mult, "pk0 pk1 pk2 pk3 pk4 pk5 rl0 rl1 sc0 sc1 sc2 sc3 sc4",
+        tt(T.ni[:], T.pk[:, 0:6].indirect(T.cu[:, 32:34]), T.scl[:], A.mult, "pk0 pk1 pk2 pk3 pk4 pk5 rl sc0 sc1 sc2 sc3 sc4",
            "n0 n1 n2", dur=gcost(32))
         ts(T.ni[:, 0:1], T.ni[:, 0:1], 4095, None, A.bitwise_and, None, "n0", "n0")
         ts(T.ni[:, 2:17], T.ni[:, 2:17], 255, None, A.bitwise_and, None, "n2", "n2")
         cp(lv[:, LN:LN + 17], T.ni[:, 0:17], "n0 n1 n2", "ln")
-        nsrc = T.tabn[:].indirect(lv[:, LN:LN + 17])
-        if last:
-            cp(T.nb[:, 1:K + 1], nsrc, "tab0 tab1 tab2 ln", "nb", dur=gcost(K))
-        else:
-            act(T.nb[:, 1:K + 1], nsrc, F.Copy, "tab0 tab1 tab2 ln", "nb", K, True)
+        move(T.nb[:, 1:K + 1], T.tabn[:].indirect(lv[:, LN:LN + 17]), "tab0 tab1 tab2 ln", "nb", K, True)
         sm = T.sm2
         for k in range(2):
             act(T.jb[:, K * k:K * k + K], T.nb[:, 1:K + 1], F.Sign, "nb th%d" % k, "jb%d s%d" % (k, k), K,
@@ -428,28 +442,30 @@ def rank_program(g, core, T, topo):
         for k in range(2):
             act(T.jb[:, 576 + 560 * k:1122 + 560 * k], T.cs[:], F.Sign, "cs csp jj%d" % k, "jb%d i%d" % (3 + k, k), 2 * K,
                 bias=cf[:, 10 + k:11 + k], scale=-1.0, accum_out=sm[:, 4 + k:5 + k])
-            ts(sm[:, 6 + k:7 + k], sm[:, 4 + k:5 + k], 1.0, float(K), A.is_lt, A.mult, "i%d" % k, "j%d" % k)
-            ts(lv[:, LC + k:LC + k + 1], sm[:, 4 + k:5 + k], 0.5, sm[:, 6 + k:7 + k], A.mult, A.add, "i%d j%d" % (k, k), "lc%d" % k)
-        for b in range(4):
-            act(T.fg[:, 32 * b:32 * b + 32], plane(t, b).indirect(lv[:, LC:LC + 2]), F.Copy,
-                "xz pn%d%d pe%d%d lc0 lc1" % (t, b, t, b), "fg%d" % b, 32, True)
-        tt(T.key[:, 0:32], T.nb[:, 0:K + 1].indirect(lv[:, LC:LC + 2]), T.jt[:], A.subtract, "nb nb0 lc0 lc1 jt", "key", dur=gcost(32))
-        tt(T.key[:, 32:64], T.key[:, 0:32], T.dg[:], A.mult, "key dg", "k1", 32)
-        scan(T.key[:, 64:96], T.nd[:, 0:32], T.key[:, 32:64], A.mult, A.add, "nd k1", "k2", 32)
+        ts(sm[:, 6:8], sm[:, 4:6], 1.0, float(K), A.is_lt, A.mult, "i0 i1", "j")
         for k in range(2):
-            act(T.jb[:, 1696 + 32 * k:1728 + 32 * k], T.key[:, 0:32], F.Sign, "key k2", "jb%d r%d" % (5 + k, k), 32,
-                bias=T.key[:, 79 + 16 * k:80 + 16 * k], scale=-1.0, accum_out=sm[:, 10 + k:11 + k])
-        for b in range(4):
-            ts(lv[:, LR + 2 * b:LR + 2 * b + 2], sm[:, 10:12], -2.0, 62.0 + b, A.mult, A.add, "r0 r1", "lr%d" % b)
-        cp(T.fi[:, 0:128].indirect(lv[:, LR:LR + 8]), T.fg[:], "fg0 fg1 fg2 fg3 lr0 lr1 lr2 lr3", "fi", dur=0.55)
-        qz(T["qf%d" % t][:], T["sf%d" % t][:], T.fi[:], "fi", "qf%d" % t, 128)
-        sent = op("g", lambda t=t: hand(g, T, topo, core, way_out[1], T["qf%d" % t][:, 0:32].bitcast(u8), T["sf%d" % t][:], t),
-                  "qf%d" % t, "", 0.3, kind="r")
-        op("net", None, "", "land%d" % t, 0.0, lat=NET, kind="n", after=[sent], sem=("arr%d" % t, arrive))
+            ts(lv[:, LC + k:LC + k + 1], sm[:, 4 + k:5 + k], 0.5, sm[:, 6 + k:7 + k], A.mult, A.add, "i%d j" % k, "lc%d" % k)
+        cand = T.nb[:, 0:K + 1].indirect(lv[:, LC:LC + 2])
+        tt(T.key[:, 64:96], cand, T.dg[:], A.mult, "nb nb0 lc0 lc1 dg", "k1", dur=gcost(32))
+        scan(T.key[:, 96:128], T.nd[:, 0:32], T.key[:, 64:96], A.mult, A.add, "nd k1", "k2", 32)
+        move(T.hb[:, 0:32], T.it[:, 0:K + 1].indirect(lv[:, LC:LC + 2]), "it lc0 lc1", "wb", 32, True)
+        for k in range(2):
+            tt(T.key[:, 32 * k:32 * k + 32], cand, T.jt[:, 32 * k:32 * k + 32], A.subtract, "nb nb0 lc0 lc1 jt%d" % k, "key%d" % k,
+               dur=gcost(32))
+            act(T.jb[:, 1696 + 32 * k:1728 + 32 * k], T.key[:, 32 * k:32 * k + 32], F.Sign, "key%d k2" % k, "jb%d r%d" % (5 + k, k), 32,
+                bias=T.key[:, 111 + 16 * k:112 + 16 * k], scale=-1.0, accum_out=sm[:, 10 + k:11 + k])
+        ts(lv[:, LR:LR + 2], sm[:, 10:12], -0.5, 15.0, A.mult, A.add, "r0 r1", "lr")
+        cp(T.hb[:, 32:64].indirect(lv[:, LR:LR + 2]), T.hb[:, 0:32], "wb lr", "hb", dur=0.16)
+        tt(T.hb[:, 64:96], T.hb[:, 32:64], T.dg[:], A.mult, "hb dg", "h1", 32)
+        scan(T.hb[:, 96:128], T.nd[:, 0:32], T.hb[:, 64:96], A.mult, A.add, "nd h1", "h2", 32)
+        cp(T["hs%d" % t][:], T.hb[:, 111:128:16], "h2", "hs%d" % t)
+        sent = op("g", lambda t=t: hand(g, T, topo, core, way_out[1], [(T["hl%d" % t][:], T["hs%d" % t][:])], "lst%d" % t),
+                  "hs%d" % t, "", 0.3, kind="r", after=[sent])
+        op("nl", None, "", "list%d" % t, 0.0, kind="n", after=[sent], sem=("lst%d" % t, arrive))
         for b in range(4):
             pr = "xz pn%d%d pe%d%d " % (t, b, t, b)
             cut = slice(P * b, P * b + P)
-            act(T.g1[:, cut], plane(t, b).indirect(lu[:, LA:LA + 18]), F.Copy, pr + "la", "g1%d" % b, P, True)
+            move(T.g1[:, cut], plane(t, b).indirect(lu[:, LA:LA + 18]), pr + "la", "g1%d" % b, P, True)
             tt(T.g2[:, cut], plane(t, b).indirect(lu[:, LB:LB + 18]), T.g1[:, cut], A.max, pr + "lb g1%d" % b, "g2%d" % b, dur=gcost(P))
             tt(T.mt[:, b:4 * P:4], plane(t, b).indirect(lv[:, LD:LD + 18]), T.g2[:, cut], A.add, pr + "ld g2%d" % b, "mt%d" % b,
                dur=gcost(P))
@@ -463,40 +479,26 @@ def rank_program(g, core, T, topo):
             tt(T.xi[:, 4 * E + b:4 * C:4], T.rr[:, cut], plane(t, b, E + 1), A.add, "rr%d pn%d%d xn" % (b, t, b), "xn%d" % b, P)
             if not last:
                 act(plane(t + 1, b, E + 1), T.xi[:, 4 * E + b:4 * C:4], F.Copy, "xn%d" % b, "pn%d%d" % (t + 1, b), P)
-
-        def unpack(t=t):
-            ins = None
-            for b in (3, 2, 1, 0):
-                a = 96 - 32 * b
-                ins = g.tensor.matmul_mx(ps[:, 2560:2560 + ZL + 32 - a], T.qi[:, 128 * b:128 * b + 128], T.si[:, 128 * b:128 * b + 128],
-                                         T["lc%d" % t][:, a:ZL + 32], T["lp%d" % t][:, a:ZL + 32], b == 3, b == 0)
-            return ins
-        op("t", unpack, "qi lz%d lw%d land%d" % (t, t, t), "bank5", 0.55, lat=0.12)
-        dd = 2560 + 96
-        EP = "ep%d0 ep%d1 ep%d2 ep%d3" % (t, t, t, t)
-        if not last:
-            n = t + 1
-            tt(T.ep[:, 128 * n:128 * n + 128], ps[:, dd:dd + 128], T.ep[:, 128 * t:128 * t + 128], A.max, "bank5 " + EP,
-               "bank5 ep%d0 ep%d1 ep%d2 ep%d3" % (n, n, n, n), 128, 1.0)
-            for b in range(4):
-                act(plane(n, b, 1, E + 1), T.ep[:, 128 * n + 32 * b:128 * n + 32 * b + 32], F.Copy, "ep%d%d" % (n, b),
-                    "pe%d%d" % (n, b), E)
-        else:
-            for b in range(4):
-                tt(T.fi[:, b:4 * E:4], ps[:, dd + 32 * b:dd + 32 * b + 32], T.ep[:, 128 * t + 32 * b:128 * t + 32 * b + 32], A.max,
-                   "bank5 fi qf%d " % t + EP, "xe%d" % b, 32, 1.0)
-    act(T.odb[:], T.it[:, 0:K + 1].indirect(lv[:, LD:LD + 18]), F.Copy, "it ld", "odb", P, True)
+        for b in range(4):
+            came = T.dp[:, K * b:K * b + K].indirect(T["hl%d" % t][:])
+            rd = "dp%d list%d pe%d%d" % (b, t, t, b)
+            if last:
+                tt(T.fi[:, b:4 * E:4], came, plane(t, b, 1, E + 1), A.max, rd + " fi", "xf%d" % b, dur=gcost(32))
+            else:
+                tt(plane(t + 1, b, 1, E + 1), came, plane(t, b, 1, E + 1), A.max, rd, "pe%d%d" % (t + 1, b), dur=gcost(32))
+                move(T.xi[:, b:4 * E:4], plane(t + 1, b, 1, E + 1), "pe%d%d xe" % (t + 1, b), "xe%d" % b, E)
+    move(T.odb[:], T.it[:, 0:K + 1].indirect(lv[:, LD:LD + 18]), "it ld", "odb", P, True)
     dma("y", T.od[:], T.odb[0:128:16, :], "odb", "")
     qz(T.qx[:], T.sx[:], T.xi[:, 4 * E:4 * C], XN, "qx", P)
     mm(ps[:, 0:P], T.qv[:], T.sv[:], T.qx[:], T.sx[:], "qv qx", "bank0", P)
-    act(T.ys[:, E:C], ps[:, 0:P], F.Copy, "bank0", "bank0 yn", P)
+    move(T.ys[:, E:C], ps[:, 0:P], "bank0", "bank0 yn", P)
     dma("y", T.oc[:, 4 * E:4 * C], T.qx[:].bitcast(u8), "qx", "")
     dma("y", T.y[:, E:C], T.ys[:, E:C], "yn", "")
     for k in range(4):
-        dma("y", T.osc[4 * k:4 * k + 4, E:C], T.sx[32 * k:32 * k + 4, :], "qx", "")
-    qz(T.qe[:], T.se[:], T.fi[:], "fi xe0 xe1 xe2 xe3", "qe", 128)
+        dma("ys"[k % 2], T.osc[4 * k:4 * k + 4, E:C], T.sx[32 * k:32 * k + 4, :], "qx", "")
+    qz(T.qe[:], T.se[:], T.fi[:], "fi xf0 xf1 xf2 xf3", "qe", 128)
     mm(ps[:, 3072:3072 + 128], T.qv[:], T.sv[:], T.qe[:], T.se[:], "qv qe", "bank6", 128)
-    cp(T.ys[:, 0:E], ps[:, 3072:3072 + E], "bank6", "bank6 ye", 32)
+    move(T.ys[:, 0:E], ps[:, 3072:3072 + E], "bank6", "bank6 ye", 32)
     dma("y", T.oc[:, 0:4 * E], T.qe[:, 0:E].bitcast(u8), "qe", "")
     for k in range(4):
         dma("ys"[k % 2], T.osc[4 * k:4 * k + 4, 0:E], T.se[32 * k:32 * k + 4, 0:E], "qe", "")

@@ -1,34 +1,34 @@
 import math
-from concourse.bass import DstId, RemoteDMATransfer
-from concourse.mybir import dt, AluOpType as A, ActivationFunctionType as F, AxisListType as AX
+import numpy as np
+from concourse.mybir import dt, AluOpType as A, ActivationFunctionType as F
 
 C, E, B, NB, P, R = 320, 32, 48, 6, 288, 3
 K = C - B
 PL = 336
 X4, S_, BF, F32, U8 = "float8_e4m3fn_x4", "sbuf", "bfloat16", "float32", "uint8"
 SCRATCH = {"ps": ("psum", [128, 4096], F32)}
-for _n, _w in (("xi", 4 * C), ("xp", 12 * PL), ("ut", 512), ("vt", 512), ("et", 2048), ("ones", 512), ("nd", P), ("lf", P),
-               ("ls", P), ("d0", 128), ("jb", 1792), ("nb", 288), ("fl", 2 * K), ("cs", 2 * K + 2), ("fi", 512), ("dp", 4 * K),
-               ("g1", 4 * P), ("g2", 4 * P), ("mt", 4 * P)):
+for _n, _w in (("xi", 4 * C), ("xp", 12 * PL), ("ut", 512), ("vt", 512), ("et", 2048), ("ones", 512), ("uu", 672), ("ba", 2 * P),
+               ("lm", 2 * P), ("sc", 240), ("hw", P), ("j16", P), ("ls", P), ("tt", 624), ("jb", 1792), ("nb", 288), ("fl", 2 * K),
+               ("cs", 2 * K + 2), ("fc", 128), ("ft", 512), ("g1", 4 * P), ("g2", 4 * P), ("mt", 4 * P)):
     SCRATCH[_n] = (S_, [128, _w], BF)
-for _n, _w in (("cf", 64), ("j16", P), ("md", P), ("dg", 32), ("it", 336), ("oh", 288), ("tabn", 560), ("scl", 32), ("jt", 64),
-               ("ab", 96), ("uu", 688), ("d1", 576), ("tt", 616), ("llf", 112), ("js", 1152), ("pk", 8), ("sm2", 32), ("key", 128),
-               ("hb", 128), ("rr", 4 * P), ("ys", C), ("odb", P)):
+for _n, _w in (("cf", 128), ("dg", 32), ("nd", 32), ("it", 336), ("oh", 64), ("oz", 48), ("tabn", 592), ("scl", 32), ("jt", 32),
+               ("sel", 108), ("qa", 112), ("val", 120), ("sd", 112), ("so", 112), ("js", 1152), ("pk", 8), ("sm2", 32),
+               ("key", 96), ("rr", 4 * P), ("ys", C), ("odb", P)):
     SCRATCH[_n] = (S_, [128, _w], F32)
 for _n, _w in (("pai", 32), ("pbi", 32), ("ci", 64), ("ni", 32)):
     SCRATCH[_n] = (S_, [128, _w], "int32")
-for _n, _w in (("cu", 160), ("cw", 48), ("llu", 112), ("hs0", 2), ("hs1", 2), ("hs2", 2), ("hl0", 2), ("hl1", 2), ("hl2", 2)):
+for _n, _w in (("cu", 160), ("cw", 80), ("llu", 80)):
     SCRATCH[_n] = (S_, [128, _w], "uint16")
 for _n, _w in (("u", 128), ("v", 128), ("up", 128 * R), ("w", 512), ("x", P), ("e", 128), ("m", P), ("i", 512),
-               ("f0", K), ("f1", K), ("f2", K), ("l0", K), ("l1", K), ("l2", K)):
+               ("f", E * R + 128 * R)):
     SCRATCH["q" + _n] = (S_, [128, _w], X4)
     SCRATCH["s" + _n] = (S_, [128, _w], U8)
 NDMA = 22
-SEMAPHORES = (["cv", "cs", "ct", "cg", "sent"] + ["big%d" % t for t in range(R)] + ["lst%d" % t for t in range(R)]
+SEMAPHORES = (["cv", "cs", "ct", "cg", "sent"] + ["%s%d" % (k, t) for k in ("qf", "sf") for t in range(R)]
               + ["dm%d" % i for i in range(NDMA)])
-CY = 0.85e-3
-CASES = ((0.06, 1.0, 0.08, 4.5), (0.0, 1.0, 0.2, 4.5), (0.04, 1.3, 0.12, 5.5))
-TRIES = 100000
+CY = 0.83e-3
+CASES = ((0.03, 1.2, 0.10, 3.0), (0.0, 1.0, 0.2, 3.0), (0.04, 1.4, 0.12, 4.0))
+TRIES = 60000
 PLAN = {}
 
 
@@ -41,25 +41,25 @@ def route(T, topo, r):
     return [src, (near or able)[0], dst]
 
 
-def hand(g, T, topo, src, dst, pairs, sem):
+def landing(t):
+    return E * (R - 1 - t)
+
+
+def hand(g, T, topo, src, dst, name, t, frm):
     rid, pid = topo.addr(dst, src)
-    for out, in_ in pairs:
-        g.remote_dma(out, in_, T.sem[sem], T.sem.sent, pid, rid, topo.mask(src, dst))
-    return len(pairs) * len(topo.engines(src, dst))
-
-
-def hand_big(g, T, topo, src, dst, a, t):
-    return hand(g, T, topo, src, dst, [(T["ql%d" % t][:].bitcast(dt.uint8), T["q%s%d" % (a, t)][:].bitcast(dt.uint8)),
-                                       (T["sl%d" % t][:], T["s%s%d" % (a, t)][:])], "big%d" % t)
+    out, in_ = T[name][:, landing(t):landing(t) + E], T[name][:, frm:frm + E]
+    if name == "qf":
+        out, in_ = out.bitcast(dt.uint8), in_.bitcast(dt.uint8)
+    g.remote_dma(out, in_, T.sem["%s%d" % (name, t)], T.sem.sent, pid, rid, topo.mask(src, dst))
+    return len(topo.engines(src, dst))
 
 
 def relay(g, T, topo, src, me, dst):
     n, e = 0, len(topo.engines(src, me))
     for t in range(R):
-        g.wait_ge(T.sem["big%d" % t], 2 * e)
-        n += hand_big(g, T, topo, me, dst, "l", t)
-        g.wait_ge(T.sem["lst%d" % t], e)
-        n += hand(g, T, topo, me, dst, [(T["hl%d" % t][:], T["hl%d" % t][:])], "lst%d" % t)
+        for name in ("qf", "sf"):
+            g.wait_ge(T.sem["%s%d" % (name, t)], e)
+            n += hand(g, T, topo, me, dst, name, t, landing(t))
     g.wait_ge(T.sem.sent, n)
 
 
@@ -70,19 +70,35 @@ def plan(ops):
     for i in range(n):
         for d in dep[i]:
             succ[d].append(i)
-    qs = sorted(set(o["q"] for o in ops))
-    q = [qs.index(o["q"]) for o in ops]
-    either = [i for i in range(n) if ops[i]["alt"]]
-    iv, is_ = qs.index("v"), qs.index("s")
+    qs = sorted(set(k for o in ops for k in o["alt"]))
+    alt = [[qs.index(k) for k in o["alt"]] for o in ops]
+    either = [i for i in range(n) if len(alt[i]) > 1]
     cases = []
     for add, f, w, net in CASES:
-        cases.append(([o["dur"] * f + add if o["kind"] == "c" else o["dur"] for o in ops],
+        cases.append(([{qs.index(k): d * f + add if o["kind"] == "c" else d for k, (_fn, d) in o["alt"].items()} for o in ops],
                       [o["lat"] + (w if o["kind"] == "c" else net if o["kind"] == "n" else 0.0) for o in ops]))
     dur, lat = cases[0]
     prio = [0.0] * n
     for i in range(n - 1, -1, -1):
-        prio[i] = dur[i] + lat[i] + 1e-6 + max([prio[s] for s in succ[i]] + [0.0])
-    order = sorted(range(n), key=lambda i: -prio[i])
+        prio[i] = dur[i][alt[i][0]] + lat[i] + 1e-6 + max([prio[s] for s in succ[i]] + [0.0])
+    q, order, left = [a[0] for a in alt], [], [len(d) for d in dep]
+    free, done, ready = [0.0] * len(qs), [0.0] * n, [i for i in range(n) if not dep[i]]
+    while ready:
+        start = {}
+        for i in ready:
+            s = max([done[d] for d in dep[i]] + [0.0])
+            q[i] = min(alt[i], key=lambda k: max(s, free[k]) + dur[i][k])
+            start[i] = max(s, free[q[i]])
+        first = min(start.values())
+        i = max((j for j in ready if start[j] <= first + 0.15), key=lambda j: prio[j])
+        free[q[i]] = start[i] + dur[i][q[i]]
+        done[i] = free[q[i]] + lat[i]
+        order.append(i)
+        ready.remove(i)
+        for s in succ[i]:
+            left[s] -= 1
+            if not left[s]:
+                ready.append(s)
     seed = [99]
 
     def rnd():
@@ -94,12 +110,13 @@ def plan(ops):
         for du, la in cases[::-1]:
             free, done = [0.0] * len(qs), [0.0] * n
             for i in od:
-                s = free[q[i]]
+                k = q[i]
+                s = free[k]
                 for d in dep[i]:
                     if done[d] > s:
                         s = done[d]
-                s += du[i]
-                free[q[i]] = s
+                s += du[i][k]
+                free[k] = s
                 done[i] = s + la[i]
             total += max(done) + 0.02 * sum(done) / n
         return total / len(cases), done
@@ -108,56 +125,69 @@ def plan(ops):
     best, bo, bq = cur, list(order), list(q)
     for it in range(TRIES):
         if it % 1000 == 0:
-            order = sorted(order, key=lambda i: done[i] - lat[i] - dur[i])
+            order = sorted(order, key=lambda i: done[i] - lat[i] - dur[i][q[i]])
             cur, done = run(order)
         flip, new = None, order
-        if rnd() < 0.04:
+        if rnd() < 0.06:
             flip = either[int(rnd() * len(either))]
-            q[flip] = iv + is_ - q[flip]
+            was = q[flip]
+            other = [k for k in alt[flip] if k != was]
+            q[flip] = other[int(rnd() * len(other))]
         else:
             a = int(rnd() * n)
             i = order[a]
             step = 1 if rnd() < 0.5 else -1
             stop = succ[i] if step > 0 else dep[i]
-            b, left = a, 1 + int(rnd() ** 3 * 12)
-            while left and 0 <= b + step < n and order[b + step] not in stop:
+            b, more = a, 1 + int(rnd() ** 3 * 12)
+            while more and 0 <= b + step < n and order[b + step] not in stop:
                 b += step
                 if q[order[b]] == q[i]:
-                    left -= 1
+                    more -= 1
             if b == a:
                 continue
             new = order[:a] + order[a + 1:]
             new.insert(b, i)
         got, dn = run(new)
-        if got <= cur or rnd() < math.exp((cur - got) / (0.15 * (1 - it / TRIES) + 0.003)):
+        if got <= cur or rnd() < math.exp((cur - got) / (0.08 * (1 - it / TRIES) + 0.003)):
             cur, order, done = got, new, dn
             if got < best:
                 best, bo, bq = got, list(new), list(q)
         elif flip is not None:
-            q[flip] = iv + is_ - q[flip]
+            q[flip] = was
     q[:] = bq
     done = run(bo)[1]
-    return best, bo, [done[i] - lat[i] - dur[i] for i in range(n)], [qs[k] for k in bq]
+    return best, bo, [done[i] - lat[i] - dur[i][q[i]] for i in range(n)], [qs[k] for k in bq]
+
+
+def depend(ops):
+    wrote = {n: np.full(v[1][1], -1) for n, v in SCRATCH.items()}
+    read = {n: [] for n in SCRATCH}
+    for i, o in enumerate(ops):
+        dep = set(o["after"])
+        rd = [x for x in o["r"] if x[0] in SCRATCH and x[0] != "ps"]
+        wr = [x for x in o["w"] if x[0] in SCRATCH and x[0] != "ps"]
+        wr += [("ps", x[1] // 512 * 512, x[1] // 512 * 512 + 512, 1) for x in o["r"] + o["w"] if x[0] == "ps"]
+        for n, a, z, s in rd + wr:
+            dep.update(int(k) for k in set(wrote[n][a:z:s].tolist()) if k >= 0)
+        for n, a, z, s in wr:
+            for j, mask in read[n]:
+                if mask[a:z:s].any():
+                    dep.add(j)
+                    mask[a:z:s] = False
+            wrote[n][a:z:s] = i
+        for n, a, z, s in rd:
+            mask = np.zeros(len(wrote[n]), bool)
+            mask[a:z:s] = True
+            read[n].append((i, mask))
+        dep.discard(i)
+        o["dep"] = dep
 
 
 def emit(g, T, ops):
-    last_w, readers = {}, {}
-    for i, o in enumerate(ops):
-        dep = set(o["after"])
-        for k in o["r"] + o["w"]:
-            if k in last_w:
-                dep.add(last_w[k])
-        for k in o["w"]:
-            dep.update(readers.get(k, []))
-        for k in o["r"]:
-            readers.setdefault(k, []).append(i)
-        for k in o["w"]:
-            last_w[k] = i
-            readers[k] = []
-        dep.discard(i)
-        o["dep"] = dep
     if "p" not in PLAN:
+        depend(ops)
         PLAN["p"] = plan(ops)
+        PLAN["dep"] = [o["dep"] for o in ops]
     _end, order, _at, where = PLAN["p"]
     place = {i: k for k, i in enumerate(order)}
     queue = {"v": g.vector, "s": g.scalar, "t": g.tensor, "g": g, "y": g.sync}
@@ -165,14 +195,12 @@ def emit(g, T, ops):
     for i in order:
         o = ops[i]
         q = where[i]
-        if q != o["q"]:
-            o["q"], o["fn"] = q, o["alt"]
         if o["kind"] == "n":
             o["sig"], o["clock"] = o["sem"], {}
             count[o["sem"][0]] = o["sem"][1]
             continue
         kn = known[q]
-        for d in sorted(o["dep"], key=lambda j: -place[j]):
+        for d in sorted(PLAN["dep"][i], key=lambda j: -place[j]):
             p = ops[d]
             if p["sig"] is None:
                 continue
@@ -182,7 +210,7 @@ def emit(g, T, ops):
                 kn[name] = val
                 for a, b in p["clock"].items():
                     kn[a] = max(kn.get(a, 0), b)
-        ins = o["fn"]()
+        ins = o["alt"][q][0]()
         o["clock"] = dict(kn)
         if o["kind"] == "c":
             name = "c" + q
@@ -220,287 +248,341 @@ def rank_program(g, core, T, topo):
     arrive = len(topo.engines(way_in[-2], core))
     V, S, ops = g.vector, g.scalar, []
 
-    def op(q, fn, r, w, dur, lat=0.0, kind="c", after=(), sem=None, alt=None):
-        ops.append({"q": q, "fn": fn, "r": r.split(), "w": w.split(), "dur": dur, "lat": lat, "kind": kind,
-                    "after": list(after), "sem": sem, "alt": alt})
+    def v(name, a=0, z=None, s=1):
+        return (name, a, SCRATCH[name][1][1] if z is None else z, s)
+
+    def col(name, a):
+        return (name, a, a + 1, 1)
+
+    def ap(x, cast=None):
+        if not isinstance(x, tuple):
+            return x
+        if len(x) == 2:
+            return ap(x[0], cast).indirect(ap(x[1]))
+        y = T[x[0]][:, x[1]:x[2]:x[3]] if x[3] != 1 else T[x[0]][:, x[1]:x[2]]
+        return y.bitcast(cast) if cast else y
+
+    def views(*xs):
+        got = []
+        for x in xs:
+            if isinstance(x, tuple):
+                got += list(x) if len(x) == 2 else [x]
+        return got
+
+    def size(x):
+        return 16 * size(x[1]) if len(x) == 2 else len(range(x[1], x[2], x[3]))
+
+    def narrow(*xs):
+        return all(SCRATCH[x[0]][2] in (BF, "uint16") for x in xs)
+
+    def op(alt, r, w, lat=0.0, kind="c", after=(), sem=None):
+        ops.append({"alt": alt, "r": r, "w": w, "lat": lat, "kind": kind, "after": list(after), "sem": sem})
         return len(ops) - 1
 
-    def cost(n, c):
-        return max(0.06, 0.03 + n * c * CY)
+    def vcost(out, a, *more, c=None):
+        if len(a) == 2:
+            return 0.05 + size(a) * 1.56 * CY
+        return max(64, size(a) * (c or (0.5 if narrow(out, a, *more) else 1.0))) * CY
 
-    def gcost(n):
-        return 0.06 + n * 1.6 * CY
+    def scost(a):
+        return 0.065 + size(a) * (1.56 if len(a) == 2 else 1.0) * CY
 
-    def ts(out, in0, s1, s2, o0, o1, r, w, n=16, c=1.0):
+    def ts(out, a, s1, o0, s2=None, o1=None):
         if o1 is None:
-            return op("v", lambda: V.tensor_scalar(out, in0, s1, None, o0), r, w, cost(n, c))
-        return op("v", lambda: V.tensor_scalar(out, in0, s1, s2, o0, o1), r, w, cost(n, c))
+            fn = lambda: V.tensor_scalar(ap(out), ap(a), ap(s1), None, o0)
+        else:
+            fn = lambda: V.tensor_scalar(ap(out), ap(a), ap(s1), ap(s2), o0, o1)
+        return op({"v": (fn, vcost(out, a))}, views(a, s1, s2), [out])
 
-    def tt(out, a, b, o, r, w, n=16, c=2.0, dur=None):
-        return op("v", lambda: V.tensor_tensor(out, a, b, o), r, w, dur or cost(n, c))
+    def tt(out, a, b, o):
+        c = 1.0 if "ps" in (a[0], b[0]) else 2.0
+        return op({"v": (lambda: V.tensor_tensor(ap(out), ap(a), ap(b), o), vcost(out, a, c=c))}, views(a, b), [out])
 
-    def cp(out, a, r, w, n=16, c=1.0, dur=None):
-        return op("v", lambda: V.tensor_copy(out, a), r, w, dur or cost(n, c))
+    def cp(out, a):
+        return op({"v": (lambda: V.tensor_copy(ap(out), ap(a)), vcost(out, a))}, views(a), [out])
 
-    def scan(out, a, b, o0, o1, r, w, n, c=1.0):
-        return op("v", lambda: V.tensor_tensor_scan(out, a, b, 0.0, o0, o1), r, w, cost(n, c))
+    def scan(out, a, b, o0, o1):
+        return op({"v": (lambda: V.tensor_tensor_scan(ap(out), ap(a), ap(b), 0.0, o0, o1), vcost(out, a, b))}, [a, b], [out])
 
-    def qz(out, sc, a, r, w, n):
-        return op("v", lambda: V.quantize_mx(out, sc, a), r, w, 0.03 + n * 4 * 0.22e-3)
+    def turn(out, a):
+        return op({"v": (lambda: V.transpose(ap(out), ap(a)), vcost(out, a))}, [a], [out])
 
-    def act(out, a, f, r, w, n=16, gather=False, **kw):
-        return op("s", lambda: S.activation(out, a, f, **kw), r, w, gcost(n) + 0.02 if gather else 0.06 + n * CY)
+    def qz(name, a, z, tile):
+        out, sc = v("q" + name, a, z), v("s" + name, a, z)
+        return op({"v": (lambda: V.quantize_mx(ap(out), ap(sc), ap(tile)), 0.012 + size(tile) * 0.22e-3)}, [tile], [out, sc])
 
-    def move(out, a, r, w, n, gather=False):
-        return op("s", lambda: S.activation(out, a, F.Copy), r, w, gcost(n) + 0.01 if gather else 0.06 + n * CY,
-                  alt=lambda: V.tensor_copy(out, a))
+    def act(out, a, f, bias=0.0, scale=1.0, acc=None):
+        fn = lambda: S.activation(ap(out), ap(a), f, bias=ap(bias), scale=ap(scale), accum_out=ap(acc))
+        return op({"s": (fn, scost(a) + (0.02 if acc else 0.0))}, views(a, bias, scale), views(out, acc))
 
-    def iota(out, pat, base, cm, w, n, flt=True):
-        if flt:
-            return op("g", lambda: g.iota(out, pat, base, cm, allow_small_or_imprecise_dtypes=True), "", w, 0.13 + 2 * n * CY)
-        return op("g", lambda: g.iota(out, pat, base, cm), "", w, 0.13 + 2 * n * CY)
+    def lin(out, a, scale=1.0, bias=0.0):
+        return op({"s": (lambda: S.activation(ap(out), ap(a), F.Identity, bias=ap(bias), scale=ap(scale)), scost(a)),
+                   "v": (lambda: V.tensor_scalar(ap(out), ap(a), ap(scale), ap(bias), A.mult, A.add), vcost(out, a))},
+                  views(a, scale, bias), [out])
 
-    def fill(out, val, w, n):
-        return op("s", lambda: S.activation(out, T.it[:, 0:n], F.Identity, scale=0.0, bias=val), "it", w, 0.06 + n * CY,
-                  alt=lambda: V.memset(out, val))
+    def move(out, a, pool=False):
+        alt = {"s": (lambda: S.activation(ap(out), ap(a), F.Copy), scost(a)), "v": (lambda: V.tensor_copy(ap(out), ap(a)), vcost(out, a))}
+        if pool:
+            n = size(a)
+            alt = {"g": (lambda: g.affine_select(ap(out), ap(a), [[0, n]], A.is_ge, 0.0, 0, 0), 0.17 + 2 * n * CY), **alt}
+        return op(alt, views(a), [out])
 
-    def mm(out, lq, lsc, rq, rsc, r, w, n):
-        return op("t", lambda: g.tensor.matmul_mx(out, lq, lsc, rq, rsc, True, True), r, w, 0.03 + n * 0.6e-3, lat=0.04)
+    def iota(out, pat, base, cm=0):
+        if SCRATCH[out[0]][2] == "int32":
+            fn = lambda: g.iota(ap(out), pat, base, cm)
+        else:
+            fn = lambda: g.iota(ap(out), pat, base, cm, allow_small_or_imprecise_dtypes=True)
+        return op({"g": (fn, 0.13 + 2 * size(out) * CY)}, [], [out])
 
-    def dma(q, out, a, r, w, lat=2.0):
-        e = {"y": g.sync, "s": g.scalar, "g": g}[q]
-        return op(q, lambda: e.dma_start(out, a), r, w, 0.1, lat=lat, kind="d")
+    def fill(out, val):
+        n = size(out)
+        alt = {"v": (lambda: V.memset(ap(out), val), vcost(out, out))}
+        if val == int(val):
+            alt["g"] = (lambda: g.iota(ap(out), [[0, n]], int(val), 0, allow_small_or_imprecise_dtypes=True), 0.13 + 2 * n * CY)
+        return op(alt, [], [out])
+
+    def mm(bank, l, la, r, ra, n):
+        out = v("ps", 512 * bank, 512 * bank + n)
+        ins = [v("q" + l, la, la + 128), v("s" + l, la, la + 128), v("q" + r, ra, ra + n), v("s" + r, ra, ra + n)]
+        return op({"t": (lambda: g.tensor.matmul_mx(ap(out), *[ap(x) for x in ins], True, True), 0.03 + n * 0.6e-3)}, ins, [out], lat=0.04)
+
+    def dma(qs, out, a, r, w, lat=2.0, after=()):
+        e = {"y": g.sync, "s": g.scalar, "g": g}
+        return op({q: (lambda q=q: e[q].dma_start(out, a), 0.1) for q in qs}, r, w, lat=lat, kind="d", after=after)
 
     def plane(t, b, a=0, z=C + 1):
         o = (4 * t + b) * PL
-        return T.xp[:, o + a:o + z]
+        return v("xp", o + a, o + z)
+
+    def bank(k, n):
+        return v("ps", 512 * k, 512 * k + n)
 
     u8 = dt.uint8
-    ps = T.ps
-    cf = T.cf
-    I_ = F.Identity
-    dma("y", T.xi[:], T.x[:], "", "xn xe", 2.6)
-    dma("s", T.ut[:], T.u[:], "", "ut", 2.3)
-    dma("y", T.pai[:, 0:18], T.pa[:], "", "pa", 2.6)
-    dma("s", T.pbi[:, 0:18], T.pb[:], "", "pb", 2.6)
-    dma("y", T.qw[:].bitcast(u8), T.wc[:], "pa", "qw", 3.0)
-    dma("y", T.sw[:], T.ws[:], "pa", "sw", 3.0)
-    dma("y", T.vt[:], T.v[:], "pa", "vt", 3.0)
-    iota(T.ci[:, 0:1], [[0, 1]], 0, 1, "p", 1, False)
-    iota(T.ci[:, 6:7], [[0, 1]], 5, 0, "c6", 1, False)
-    iota(T.ci[:, 8:32], [[1, R], [16, 8]], 0, 0, "uli", 24, False)
-    iota(T.j16[:], [[0, 18], [1, 16]], 0, 0, "j16", P)
-    iota(T.it[:], [[1, 336]], -1, 0, "it", 336)
-    iota(T.tabn[:, 0:144], [[1, 144]], 113, 0, "tab0", 144)
-    iota(T.tabn[:, 144:256], [[1, 112]], 1, 0, "tab1", 112)
-    iota(T.tabn[:, 256:560], [[1, 304]], 1, 0, "tab2", 304)
-    iota(T.fi[:], [[0, 512]], 0, 0, "fi", 512)
-    iota(T.ones[:], [[0, 512]], 1, 0, "ones", 512)
-    lane = cf[:, 0:1]
-    ts(T.ci[:, 1:2], T.ci[:, 0:1], 15, None, A.bitwise_and, None, "p", "li")
-    cp(lane, T.ci[:, 1:2], "li", "lane")
-    cp(T.cu[:, 0:24], T.ci[:, 8:32], "uli", "ulu")
-    ts(T.nd[:], T.j16[:], lane, None, A.not_equal, None, "j16 lane", "nd", P)
-    act(T.md[:], T.nd[:], F.Copy, "nd", "md", P, scale=-1e29)
-    ts(T.dg[:], T.j16[:, 0:32], lane, None, A.is_equal, None, "j16 lane", "dg", 32)
-    ts(T.ci[:, 2:3], T.ci[:, 0:1], 4, None, A.logical_shift_right, None, "p", "c2")
-    tt(T.ci[:, 3:4], T.ci[:, 2:3], T.ci[:, 0:1], A.add, "c2 p", "c3")
-    ts(T.ci[:, 4:5], T.ci[:, 3:4], 1, None, A.bitwise_and, None, "c3", "c4")
-    ts(cf[:, 1:2], T.ci[:, 4:5], 304.0, None, A.mult, None, "c4", "odd")
-    act(cf[:, 16:17], lane, I_, "lane odd", "be", scale=16.0, bias=cf[:, 1:2])
-    ts(cf[:, 3:4], lane, 16.0, cf[:, 1:2], A.mult, A.subtract, "lane odd", "bo")
-    act(cf[:, 4:5], T.dg[:, 15:16], I_, "dg bo", "bo1", scale=1000.0, bias=cf[:, 3:4])
-    act(cf[:, 5:6], T.dg[:, 0:1], I_, "dg bo1", "bo2", scale=1000.0, bias=cf[:, 4:5])
-    act(cf[:, 6:7], T.dg[:, 0:1], I_, "dg be", "big", scale=-1000.0, bias=cf[:, 16:17])
-    act(cf[:, 7:8], T.dg[:, 1:2], I_, "dg big", "be1", scale=-1000.0, bias=cf[:, 6:7])
-    cl = 24
-    ts(cf[:, 17:18], cf[:, 7:8], 1256.0, 608.0, A.add, A.min, "be1", "cl1")
-    for c, src, tag, add in ((18, 4, "bo1", 353.0), (19, 16, "be", 34.0), (20, 5, "bo2", 355.0), (21, 16, "be", 36.0), (22, 5, "bo2", 357.0)):
-        act(cf[:, c:c + 1], cf[:, src:src + 1], I_, tag, "cl%d" % (c - 16), bias=add)
-    ts(T.cu[:, cl:cl + 7], cf[:, 16:23], 609.0, None, A.min, None, "be cl1 cl2 cl3 cl4 cl5 cl6", "cl")
-    fill(T.tt[:, 608:609], 274.0, "ttp0", 1)
-    fill(T.tt[:, 609:616], 273.0, "ttp1", 7)
-    ts(T.ci[:, 5:6], lane, 1.0 / 3, None, A.mult, None, "lane", "c5")
-    cp(T.cu[:, 32:34], T.ci[:, 5:7], "c5 c6", "rl")
-    fill(T.scl[:, 0:1], 1.0, "sc0", 1)
-    fill(T.scl[:, 1:2], 1.0 / 4096, "sc1", 1)
-    fill(T.scl[:, 2:32:3], 1.0, "sc2", 10)
-    fill(T.scl[:, 3:32:3], 1.0 / 256, "sc3", 10)
-    fill(T.scl[:, 4:32:3], 1.0 / 65536, "sc4", 10)
+    dma("y", T.xi[:], T.x[:], [], [v("xi")], 2.6)
+    dma("s", T.ut[:], T.u[:], [], [v("ut")], 2.3)
+    dma("y", T.pai[:, 0:18], T.pa[:], [], [v("pai")], 2.6)
+    first = dma("y", T.pbi[:, 0:18], T.pb[:], [], [v("pbi")], 2.6)
+    dma("y", T.qw[:].bitcast(u8), T.wc[:], [], [v("qw")], 3.0, [first])
+    dma("y", T.sw[:], T.ws[:], [], [v("sw")], 3.0, [first])
+    dma("y", T.vt[:], T.v[:], [], [v("vt")], 3.0, [first])
+    lane, grp = col("cf", 0), col("cf", 1)
+    iota(col("ci", 0), [[0, 1]], 0, 1)
+    iota(v("ci", 8, 32), [[1, R], [16, 8]], 0)
+    iota(v("j16"), [[0, 18], [1, 16]], 0)
+    iota(v("it"), [[1, 336]], -1)
+    iota(v("cf", 32, 39), [[16, 7]], -4)
+    iota(v("cf", 4, 8), [[1, 4]], 62)
+    ts(col("ci", 1), col("ci", 0), 15, A.bitwise_and)
+    cp(lane, col("ci", 1))
+    ts(col("ci", 2), col("ci", 0), 4, A.logical_shift_right)
+    cp(grp, col("ci", 2))
+    cp(v("cu", 0, 24), v("ci", 8, 32))
+    ts(v("hw"), v("j16"), lane, A.not_equal, 4.0, A.mult)
+    ts(v("nd"), v("j16", 0, 32), lane, A.not_equal)
+    ts(v("dg"), v("j16", 0, 32), lane, A.is_equal)
+    scan(v("cf", 64, 80), v("hw", 0, 16), v("dg", 0, 16), A.mult, A.add)
+    power = col("cf", 79)
+    lin(v("cf", 12, 16), v("cf", 4, 8), 0.5)
+    tt(v("cf", 16, 22), v("dg", 0, 12, 2), v("dg", 1, 12, 2), A.add)
+    tt(v("cf", 80, 86), v("dg", 0, 12, 2), v("dg", 1, 12, 2), A.subtract)
+    lin(v("cf", 24, 30), v("cf", 80, 86), 1.0 / 64)
+    fill(v("uu", 0, 64, 2), 0.0)
+    fill(v("uu", 640, 672), 0.0)
+    lin(v("uu", 1, 64, 2), v("it", 2, 34), col("cf", 24), col("dg", 1))
+    for k in range(NB - 1):
+        lin(v("sc", B * k, B * k + B), v("it", 2, 2 + B), col("cf", 25 + k), col("dg", 2 * k + 3))
+    fill(v("lm", 0, 2 * P, 2), 1.0)
+    LP, LQ, LL, LK = 24, 32, 40, 46
+    ef, ci = v("cf", 40, 47), v("ci", 32, 39)
+    ts(ef, v("cf", 32, 39), lane, A.add)
+    ts(ci, ef, 1.0 / 6, A.mult, -0.42, A.add)
+    ts(v("ci", 40, 47), ci, grp, A.add)
+    ts(v("ci", 48, 55), v("ci", 40, 47), 1, A.bitwise_and)
+    ts(v("cf", 48, 55), v("ci", 48, 55), 152.0, A.mult)
+    ts(v("cf", 56, 63), ci, 6.34, A.mult, 0.01, A.add)
+    tt(v("cf", 88, 95), ef, v("cf", 56, 63), A.is_gt)
+    ts(v("cf", 96, 103), v("cf", 88, 95), 1000.0, A.mult)
+    ts(v("cf", 104, 111), ci, 2.0, A.mult)
+    tt(v("cf", 48, 55), v("cf", 48, 55), ef, A.add)
+    tt(v("cf", 96, 103), v("cf", 96, 103), v("cf", 104, 111), A.add)
+    tt(v("cf", 48, 55), v("cf", 48, 55), v("cf", 96, 103), A.add)
+    ts(v("cf", 56, 63), v("cf", 48, 55), 2.0, A.mult, 608.0, A.min)
+    cp(v("cu", LP, LP + 7), v("cf", 56, 63))
+    ts(v("cu", LQ, LQ + 7), v("cf", 56, 63), 1.0, A.add)
+    fill(v("tt", 608, 624), 0.0)
+    fill(v("sd"), -B / 32768.0)
+    fill(v("sd", 4, 112, 6), -4.0)
+    fill(v("sd", 5, 112, 6), -E / 32768.0)
+    span = [(0, 18), (32, 48), (48, 61), (22, 32), (64, 71), (18, 22)]
+    ts(col("cf", 112), lane, 2.0, A.is_ge, -13.0, A.mult)
+    ts(col("cf", 113), lane, 6.0, A.is_ge, -62.0, A.mult)
+    ts(col("cf", 114), col("cf", 112), col("cf", 113), A.add, 100.0, A.add)
+    for c, add in enumerate((4.0, col("cf", 114), 23.0, 42.0, 80.0)):
+        lin(col("cf", 116 + c), lane, 6.0, add)
+    ts(v("cu", LL, LL + 5), v("cf", 116, 121), 112.0, A.min)
+    fill(v("val", 112, 120), 49 / 32768.0)
+    fill(col("oh", 0), 0.0)
+    fill(v("oh", 49, 64), -7.0 * 65793)
+    fill(col("oz", 0), 4097.0)
+    for f in range(3):
+        lin(v("oh", 1 + 16 * f, 17 + 16 * f), v("dg", 0, 16), 256.0 ** f)
+    for f in range(2):
+        lin(v("oz", 1 + 16 * f, 17 + 16 * f), v("dg", 0, 16), 4096.0 ** f, 4097.0)
+    iota(v("tabn", 0, 144), [[1, 144]], 113)
+    iota(v("tabn", 144, 256), [[1, 112]], 1)
+    iota(v("tabn", 256, 592), [[1, 336]], -31)
+    ts(col("ci", 5), lane, 1.0 / 3, A.mult)
+    ts(col("ci", 6), lane, 0.0, A.mult, 5.0, A.add)
+    cp(v("cu", LK, LK + 2), v("ci", 5, 7))
+    fill(col("scl", 0), 1.0)
+    fill(col("scl", 1), 1.0 / 4096)
+    for f in range(3):
+        fill(v("scl", 2 + f, 32, 3), 256.0 ** -f)
     for k in range(2):
-        act(cf[:, 8 + k:9 + k], lane, I_, "lane", "th%d" % k, scale=-1.0, bias=-1.5 - 16 * k)
-        act(cf[:, 10 + k:11 + k], lane, I_, "lane", "jj%d" % k, bias=0.5 + 16 * k)
-        act(cf[:, 12 + k:13 + k], cf[:, 10 + k:11 + k], F.Copy, "jj%d" % k, "jn%d" % k, scale=-1.0 / 64)
-        act(T.jt[:, 32 * k:32 * k + 32], T.it[:, 1:33], I_, "it jn%d" % k, "jt%d" % k, 32, scale=1.0 / 64, bias=cf[:, 12 + k:13 + k])
-    fill(T.cs[:, 2 * K:2 * K + 2], -1.0, "csp", 2)
-    fill(T.oh[:, 0:1], 0.0, "oh0", 1)
-    fill(T.oh[:, 273:274], -112.0 * 65793 / 16, "oh1", 1)
-    fill(T.oh[:, 274:275], 256.0 * 4097 / 16, "oh2", 1)
-    OH = "oh0 oh1 oh2"
-    for c in range(17):
-        wgt = 4096.0 ** c if c < 2 else 256.0 ** ((c - 2) % 3)
-        act(T.oh[:, 1 + 16 * c:17 + 16 * c], T.dg[:, 0:16], F.Copy, "dg", "ohc%d" % c, 16, scale=wgt)
-        OH += " ohc%d" % c
-    fill(T.uu[:, 0:66], 0.0, "ue", 66)
-    fill(T.uu[:, 642:674], 0.0, "up", 32)
-    fill(T.d0[:], 0.0, "d0", 128)
-    act(T.uu[:, 3:66:2], T.it[:, 2:34], F.Copy, "it dg", "ue", 32, scale=T.dg[:, 0:1])
-    for k in range(NB):
-        act(T.d1[:, 96 * k + 1:96 * k + 96:2], T.it[:, 34 + B * k:34 + B * k + B], F.Copy, "it dg", "self%d" % k, B,
-            scale=T.dg[:, k + 1:k + 2])
-    fill(T.nb[:, 0:1], 0.0, "nb0", 1)
-    fill(T.xp[:, 0:12 * PL:PL], 0.0, "xz", 12)
+        lin(col("cf", 8 + k), lane, -1.0, -1.5 - 16 * k)
+        lin(col("cf", 10 + k), lane, 1.0, 0.5 + 16 * k)
+    lin(v("jt"), v("it", 1, 33), 1.0 / 64)
+    fill(v("cs", 2 * K, 2 * K + 2), -1.0)
+    fill(col("nb", 0), 0.0)
+    fill(v("xp", 0, 12 * PL, PL), 0.0)
+    fill(v("sel", 0, 36, 2), 0.0)
+    fill(v("ft", 128, 512), 0.0)
+    fill(v("ft", 0, 128), 0.0)
+    iota(v("ones"), [[0, 512]], 1)
     for b in range(4):
-        op("g", lambda b=b: g.affine_select(T.et[:, 512 * b:512 * b + 512], T.ones[:], [[1, 512]], A.is_equal, 0.0, -b, -4),
-           "ones", "et%d" % b, 1.05)
-    qz(T.qi[:], T.si[:], T.et[:], "et0 et1 et2 et3", "qi", 512)
-    LA, LA0, LA1, LB, LB0, LD, LN, LF, LC, LR = 34, 52, 71, 90, 108, 0, 18, 36, 38, 40
-    lu, lv = T.cu, T.cw
-    ts(lu[:, LA:LA + 18], T.pai[:, 0:18], 1.0, None, A.add, None, "pa", "la")
-    ts(lu[:, LA0:LA0 + 18], T.pai[:, 0:18], 2.0, 3.0, A.mult, A.add, "pa", "la0")
-    ts(lu[:, LA1:LA1 + 18], T.pai[:, 0:18], 2.0, 3.0, A.mult, A.add, "pa", "la1")
-    tt(T.ab[:, 0:18], T.pai[:, 0:18], T.pbi[:, 0:18], A.subtract, "pa pb", "amb")
-    ts(T.ab[:, 18:36], T.pbi[:, 0:18], 1.0, None, A.add, None, "pb", "bf")
-    move(T.d1[:, 0:96:2], T.uu[:, 0:66].indirect(lu[:, LA0:LA0 + 3]), "ue la0", "a0", B, True)
-    qz(T.qu[:], T.su[:], T.ut[:], "ut", "qu", 128)
-    qz(T.qv[:], T.sv[:], T.vt[:], "vt", "qv", 128)
+        op({"g": (lambda b=b: g.affine_select(T.et[:, 512 * b:512 * b + 512], T.ones[:], [[1, 512]], A.is_equal, 0.0, -b, -4), 1.02)},
+           [v("ones")], [v("et", 512 * b, 512 * b + 512)])
+    qz("i", 0, 512, v("et"))
+    LA, LA0, LA1, LB0, LB1 = 48, 66, 85, 104, 123
+    LB, LD, LN, LF, LC, LR = 0, 18, 36, 54, 56, 58
+    pa, pb = v("pai", 0, 18), v("pbi", 0, 18)
+    ts(v("cu", LA, LA + 18), pa, 1.0, A.add)
+    for at, lst in ((LA0, pa), (LB0, pb), (LA1, pa), (LB1, pb)):
+        ts(v("cu", at, at + 18), lst, 2.0, A.mult, 1.0, A.add)
+    tt(v("sel", 36, 72, 2), pa, pb, A.subtract)
+    ts(v("sel", 37, 72, 2), pb, 1.0, A.add)
+
+    def preds(k):
+        win, x = v("uu", 0, 2 * (E + B * k)), k % 2
+        la, lb = (LA1 if x else LA0) + 3 * k, (LB1 if x else LB0) + 3 * k
+        a, b = (win, v("cu", la, la + 3)), (win, v("cu", lb, lb + 3))
+        oa, ob = v("ba", 96 * k + 1, 96 * k + 96, 2), v("ba", 96 * k, 96 * k + 96, 2)
+        if k < NB - 1:
+            tt(oa, a, v("sc", B * k, B * k + B), A.max)
+            lin(ob, b, 1.0, col("cf", 17 + k))
+        else:
+            move(oa, a)
+            move(ob, b)
+
+    preds(0)
+    qz("u", 0, 128, v("ut"))
+    qz("v", 0, 128, v("vt"))
     for t in range(R):
-        cp(T.qup[:, 128 * t:128 * t + 128].bitcast(dt.uint32), T.qu[:].bitcast(dt.uint32).indirect(T.cu[:, 8 * t:8 * t + 8]),
-           "qu ulu", "qup%d" % t, dur=gcost(128))
-        move(T.sup[:, 128 * t:128 * t + 128], T.su[:].indirect(T.cu[:, 8 * t:8 * t + 8]), "qu ulu", "sup%d" % t, 128, True)
+        out, src = v("qup", 128 * t, 128 * t + 128), (v("qu"), v("cu", 8 * t, 8 * t + 8))
+        op({"v": (lambda out=out, src=src: V.tensor_copy(ap(out, dt.uint32), ap(src, dt.uint32)), vcost(out, src))}, views(src), [out])
+        move(v("sup", 128 * t, 128 * t + 128), (v("su"), src[1]))
     for b in range(4):
-        act(plane(0, b, 1), T.xi[:, b:4 * C:4], F.Copy, "xn xe", "pn0%d pe0%d" % (b, b), C)
-    XN, XE = "xn xn0 xn1 xn2 xn3", " xe xe0 xe1 xe2 xe3"
-    span = [(0, 19), (32, 48), (52, 65), (70, 80), (90, 97), (108, 112)]
-    col = [0, 29, 46, 61, 78, 93]
+        move(plane(0, b, 1), v("xi", b, 4 * C, 4), True)
+    nodes = v("xi", 4 * E, 4 * C)
     for t in range(R):
         last = t == R - 1
-        qz(T["qf%d" % t][:], T["sf%d" % t][:], T.xi[:, 0:4 * K], XN + XE, "qf%d" % t, K)
-        sent = op("g", lambda t=t: hand_big(g, T, topo, core, way_out[1], "f", t), "qf%d" % t, "", 0.8, kind="r")
-        op("nb", None, "", "land%d" % t, 0.0, lat=3.5, kind="n", after=[sent], sem=("big%d" % t, 2 * arrive))
-        for b in range(4):
-            o = 512 * (5 + b % 3)
-            bank = "bank%d" % (5 + b % 3)
-            mm(ps[:, o:o + K], T.qi[:, 128 * b:128 * b + 128], T.si[:, 128 * b:128 * b + 128], T["ql%d" % t][:], T["sl%d" % t][:],
-               "qi land%d" % t, bank, K)
-            move(T.dp[:, K * b:K * b + K], ps[:, o:o + K], bank, "dp%d %s" % (b, bank), K)
-        qz(T.qx[:], T.sx[:], T.xi[:, 4 * E:4 * C], XN, "qx", P)
-        mm(ps[:, 0:P], T.qup[:, 128 * t:128 * t + 128], T.sup[:, 128 * t:128 * t + 128], T.qx[:], T.sx[:],
-           "qup%d sup%d qx" % (t, t), "bank0", P)
-        tt(T.lf[:], ps[:, 0:P], T.md[:], A.is_lt, "md bank0", "lf bank0", P, 1.0)
-        scan(T.ls[:], T.nd[:], T.lf[:], A.mult, A.add, "nd lf", "ls", P, 0.5)
-        tt(T.ab[:, 36:54], T.ls[:, 15:P:16], T.ab[:, 0:18], A.mult, "ls amb", "bq")
-        tt(T.ab[:, 54:72], T.ab[:, 36:54], T.ab[:, 18:36], A.add, "bq bf", "bc")
-        ts(lu[:, LB0:LB0 + 18], T.ab[:, 54:72], 2.0, 1.0, A.mult, A.add, "bc", "lb0")
-        cp(lu[:, LB:LB + 18], T.ab[:, 54:72], "bc", "lb")
-        US = "ue"
+        qz("x", 0, P, nodes)
+        mm(0, "up", 128 * t, "x", 0, P)
+        act(v("lm", 1, 2 * B, 2), bank(0, B), F.Sign, scale=-1.0)
+        act(v("lm", 2 * B + 1, 2 * P, 2), v("ps", B, P), F.Sign, scale=-1.0)
+        scan(v("ls"), v("hw"), v("lm", 1, 2 * P, 2), A.mult, A.add)
+        ts(v("sel", 1, 36, 2), v("ls", 15, P, 16), 2.0, A.mult, power, A.is_gt)
+        scan(v("sel", 72, 108), v("sel", 0, 36), v("sel", 36, 72), A.mult, A.add)
+        cp(v("cw", LB, LB + 18), v("sel", 73, 108, 2))
         for k in range(NB):
-            w, x = 2 * (33 + B * k), k % 2
-            a0 = LA1 if x else LA0
             if k:
-                move(T.d1[:, 96 * k:96 * k + 96:2], T.uu[:, 0:w].indirect(lu[:, a0 + 3 * k:a0 + 3 * k + 3]),
-                     US + " la%d" % x, "a%d" % k, B, True)
-            tt(T.d0[:, 33 - 32 * x:128:2], T.uu[:, 0:w].indirect(lu[:, LB0 + 3 * k - x:LB0 + 3 * k + 3]),
-               T.d1[:, 96 * k - 32 * x:96 * k + 96:2], A.is_equal, US + " lb0 a%d a%d d0" % (k - x, k), "d0", dur=gcost(B + 16 * x))
-            scan(T.uu[:, w:w + 96], T.d0[:, 32:128], T.d1[:, 96 * k:96 * k + 96], A.mult, A.add, "d0 a%d self%d" % (k, k), "u%d" % k, 96)
-            US += " u%d" % k
-        op("v", lambda: V.transpose(T.tt[:, 0:288], T.uu[:, 67:642:2]), US, "tt1", cost(288, 1))
-        op("v", lambda: V.transpose(T.tt[:, 288:608], T.uu[:, 35:674:2]), US + " up", "tt2", cost(320, 1))
-        pick = T.tt[:].indirect(T.cu[:, cl:cl + 7])
-        cp(T.llu[:], pick, "tt1 tt2 ttp0 ttp1 cl", "llu", dur=gcost(112))
-        move(T.llf[:], pick, "tt1 tt2 ttp0 ttp1 cl", "l0 l1 l2 l3 l4 l5", 112, True)
-        for a, b in ((4, 5), (2, 3), (0, 1), (2, 4), (0, 2)):
-            va = T.llf[:, col[a] + 3 * b:col[a] + 18]
-            tt(va, va, T.llf[:, col[b] + 3 * b:col[b] + 18], A.max, "l%d l%d" % (a, b), "l%d" % a)
-        cp(lv[:, LD:LD + 18], T.llf[:, 0:18], "l0", "ld")
+                preds(k)
+            w = 2 * (E + B * k)
+            scan(v("uu", w, w + 96), v("lm", 96 * k, 96 * k + 96), v("ba", 96 * k, 96 * k + 96), A.max, A.min)
+        turn(v("tt", 0, 192), v("uu", 65, 449, 2))
+        turn(v("tt", 288, 480), v("uu", 33, 417, 2))
+        turn(v("tt", 192, 288), v("uu", 449, 640, 2))
+        turn(v("tt", 480, 608), v("uu", 417, 672, 2))
+        lin(v("qa"), (v("tt"), v("cu", LQ, LQ + 7)), 511.0 / 512, -511.0 / 512)
+        tt(v("val", 0, 112), (v("tt"), v("cu", LP, LP + 7)), v("qa"), A.add)
+        scan(v("so"), v("sd"), v("val", 0, 112), A.add, A.max)
+        ts(v("cw", LD, LD + 18), v("so", 9, 112, 6), 32768.0, A.mult, float(E + 4 * B), A.add)
+        ts(v("llu"), (v("val"), v("cu", LL, LL + 5)), 32768.0, A.mult)
         o = 0
         for l, (a, z) in enumerate(span):
             n = 16 * (z - a)
-            src = T.oh[:, 0:275].indirect(T.llu[:, a:z])
-            if (t, l) == (2, 1):
-                cp(T.js[:, o:o + n], src, "llu " + OH, "js%d" % l, dur=gcost(n))
-                op("v", lambda o=o, n=n, l=l: V.tensor_reduce(T.pk[:, l:l + 1], T.js[:, o:o + n], AX.X, A.add), "js%d" % l, "pk%d" % l,
-                   cost(n, 1))
-            else:
-                act(T.js[:, o:o + n], src, F.Copy, "llu " + OH, "js%d pk%d" % (l, l), n, True, accum_out=T.pk[:, l:l + 1])
+            act(v("js", o, o + n), (v("oh") if l else v("oz", 0, 33), v("llu", a, z)), F.Copy, acc=col("pk", l))
             o += n
-        tt(T.ni[:], T.pk[:, 0:6].indirect(T.cu[:, 32:34]), T.scl[:], A.mult, "pk0 pk1 pk2 pk3 pk4 pk5 rl sc0 sc1 sc2 sc3 sc4",
-           "n0 n1 n2", dur=gcost(32))
-        ts(T.ni[:, 0:1], T.ni[:, 0:1], 4095, None, A.bitwise_and, None, "n0", "n0")
-        ts(T.ni[:, 2:17], T.ni[:, 2:17], 255, None, A.bitwise_and, None, "n2", "n2")
-        cp(lv[:, LN:LN + 17], T.ni[:, 0:17], "n0 n1 n2", "ln")
-        move(T.nb[:, 1:K + 1], T.tabn[:].indirect(lv[:, LN:LN + 17]), "tab0 tab1 tab2 ln", "nb", K, True)
-        sm = T.sm2
+        tt(v("ni"), (v("pk", 0, 6), v("cu", LK, LK + 2)), v("scl"), A.mult)
+        ts(col("ni", 0), col("ni", 0), 4095, A.bitwise_and)
+        ts(v("ni", 2, 17), v("ni", 2, 17), 255, A.bitwise_and)
+        cp(v("cw", LN, LN + 17), v("ni", 0, 17))
+        nb = v("nb", 1, K + 1)
+        move(nb, (v("tabn"), v("cw", LN, LN + 17)))
         for k in range(2):
-            act(T.jb[:, K * k:K * k + K], T.nb[:, 1:K + 1], F.Sign, "nb th%d" % k, "jb%d s%d" % (k, k), K,
-                bias=cf[:, 8 + k:9 + k], accum_out=sm[:, k:k + 1])
-        ts(lv[:, LF:LF + 2], sm[:, 0:2], float(2 * E - K), None, A.is_ge, None, "s0 s1", "lfl")
-        act(T.jb[:, 544:576], T.j16[:, 0:16].indirect(lv[:, LF:LF + 2]), F.Copy, "j16 lfl", "jb2 tau", 32, True, accum_out=sm[:, 2:3])
-        ts(T.fl[:, 0:K], T.nb[:, 1:K + 1], sm[:, 2:3], 1.0, A.subtract, A.is_gt, "nb tau", "fa", K, 0.5)
-        ts(T.fl[:, K:2 * K], T.nb[:, 1:K + 1], sm[:, 2:3], 1.0, A.subtract, A.is_equal, "nb tau", "fb", K, 0.5)
-        scan(T.cs[:, 0:2 * K], T.fl[:], T.fl[:], A.add, A.max, "fa fb", "cs", 2 * K, 0.5)
+            act(v("jb", K * k, K * k + K), nb, F.Sign, bias=col("cf", 8 + k), acc=col("sm2", k))
+        ts(v("cw", LF, LF + 2), v("sm2", 0, 2), float(2 * E - K), A.is_ge)
+        tau = col("sm2", 2)
+        act(v("jb", 544, 576), (v("j16", 0, 16), v("cw", LF, LF + 2)), F.Copy, acc=tau)
+        ts(v("fl", 0, K), nb, tau, A.subtract, 1.0, A.is_gt)
+        ts(v("fl", K, 2 * K), nb, tau, A.subtract, 1.0, A.is_equal)
+        scan(v("cs", 0, 2 * K), v("fl"), v("fl"), A.add, A.max)
         for k in range(2):
-            act(T.jb[:, 576 + 560 * k:1122 + 560 * k], T.cs[:], F.Sign, "cs csp jj%d" % k, "jb%d i%d" % (3 + k, k), 2 * K,
-                bias=cf[:, 10 + k:11 + k], scale=-1.0, accum_out=sm[:, 4 + k:5 + k])
-        ts(sm[:, 6:8], sm[:, 4:6], 1.0, float(K), A.is_lt, A.mult, "i0 i1", "j")
+            act(v("jb", 576 + 560 * k, 1122 + 560 * k), v("cs"), F.Sign, bias=col("cf", 10 + k), scale=-1.0, acc=col("sm2", 4 + k))
+        ts(v("sm2", 6, 8), v("sm2", 4, 6), 1.0, A.is_lt, float(K), A.mult)
         for k in range(2):
-            ts(lv[:, LC + k:LC + k + 1], sm[:, 4 + k:5 + k], 0.5, sm[:, 6 + k:7 + k], A.mult, A.add, "i%d j" % k, "lc%d" % k)
-        cand = T.nb[:, 0:K + 1].indirect(lv[:, LC:LC + 2])
-        tt(T.key[:, 64:96], cand, T.dg[:], A.mult, "nb nb0 lc0 lc1 dg", "k1", dur=gcost(32))
-        scan(T.key[:, 96:128], T.nd[:, 0:32], T.key[:, 64:96], A.mult, A.add, "nd k1", "k2", 32)
-        move(T.hb[:, 0:32], T.it[:, 0:K + 1].indirect(lv[:, LC:LC + 2]), "it lc0 lc1", "wb", 32, True)
+            ts(col("cw", LC + k), col("sm2", 4 + k), 0.5, A.mult, col("sm2", 6 + k), A.add)
+        lc = v("cw", LC, LC + 2)
+        tt(v("key", 0, 32), (v("nb", 0, K + 1), lc), v("jt"), A.subtract)
+        tt(v("key", 32, 64), v("key", 0, 32), v("dg"), A.mult)
+        scan(v("key", 64, 96), v("nd"), v("key", 32, 64), A.mult, A.add)
         for k in range(2):
-            tt(T.key[:, 32 * k:32 * k + 32], cand, T.jt[:, 32 * k:32 * k + 32], A.subtract, "nb nb0 lc0 lc1 jt%d" % k, "key%d" % k,
-               dur=gcost(32))
-            act(T.jb[:, 1696 + 32 * k:1728 + 32 * k], T.key[:, 32 * k:32 * k + 32], F.Sign, "key%d k2" % k, "jb%d r%d" % (5 + k, k), 32,
-                bias=T.key[:, 111 + 16 * k:112 + 16 * k], scale=-1.0, accum_out=sm[:, 10 + k:11 + k])
-        ts(lv[:, LR:LR + 2], sm[:, 10:12], -0.5, 15.0, A.mult, A.add, "r0 r1", "lr")
-        cp(T.hb[:, 32:64].indirect(lv[:, LR:LR + 2]), T.hb[:, 0:32], "wb lr", "hb", dur=0.16)
-        tt(T.hb[:, 64:96], T.hb[:, 32:64], T.dg[:], A.mult, "hb dg", "h1", 32)
-        scan(T.hb[:, 96:128], T.nd[:, 0:32], T.hb[:, 64:96], A.mult, A.add, "nd h1", "h2", 32)
-        cp(T["hs%d" % t][:], T.hb[:, 111:128:16], "h2", "hs%d" % t)
-        sent = op("g", lambda t=t: hand(g, T, topo, core, way_out[1], [(T["hl%d" % t][:], T["hs%d" % t][:])], "lst%d" % t),
-                  "hs%d" % t, "", 0.3, kind="r", after=[sent])
-        op("nl", None, "", "list%d" % t, 0.0, kind="n", after=[sent], sem=("lst%d" % t, arrive))
+            act(v("jb", 1696 + 32 * k, 1728 + 32 * k), v("key", 0, 32), F.Sign, bias=col("key", 79 + 16 * k), scale=-1.0,
+                acc=col("sm2", 10 + k))
+            ts(v("cw", LR + k, LR + 8, 2), v("cf", 12, 16), col("sm2", 10 + k), A.subtract, 2.0, A.mult)
         for b in range(4):
-            pr = "xz pn%d%d pe%d%d " % (t, b, t, b)
-            cut = slice(P * b, P * b + P)
-            move(T.g1[:, cut], plane(t, b).indirect(lu[:, LA:LA + 18]), pr + "la", "g1%d" % b, P, True)
-            tt(T.g2[:, cut], plane(t, b).indirect(lu[:, LB:LB + 18]), T.g1[:, cut], A.max, pr + "lb g1%d" % b, "g2%d" % b, dur=gcost(P))
-            tt(T.mt[:, b:4 * P:4], plane(t, b).indirect(lv[:, LD:LD + 18]), T.g2[:, cut], A.add, pr + "ld g2%d" % b, "mt%d" % b,
-               dur=gcost(P))
-        qz(T.qm[:], T.sm[:], T.mt[:], "mt0 mt1 mt2 mt3", "qm", P)
+            move(v("fc", E * b, E * b + E), (plane(t, b), lc))
+        lr = v("cw", LR, LR + 8)
+        op({"v": (lambda lr=lr: V.tensor_copy(T.ft[:, 0:128].indirect(ap(lr)), T.fc[:]), 0.05 + 128 * 3.8 * CY)},
+           [lr, v("fc")], [v("ft", 0, 128)])
+        own = E * R + 128 * t
+        qz("f", own, own + 128, v("ft"))
+        sent = []
+        for name in ("qf", "sf"):
+            sent = [op({"g": (lambda name=name, t=t, own=own: hand(g, T, topo, core, way_out[1], name, t, own), 0.3)},
+                       [v(name, own, own + E)], [], kind="r", after=sent)]
+            op({"n" + name: (None, 0.0)}, [], [v(name, landing(t), landing(t) + E)], kind="n", after=sent,
+               sem=("%s%d" % (name, t), arrive))
         for b in range(4):
-            z = ps[:, 512 * (b + 1):512 * (b + 1) + P]
-            bank = "bank%d" % (b + 1)
-            cut = slice(P * b, P * b + P)
-            mm(z, T.qw[:, 128 * b:128 * b + 128], T.sw[:, 128 * b:128 * b + 128], T.qm[:], T.sm[:], "qw sw qm", bank, P)
-            act(T.rr[:, cut], z, F.Relu, bank, "rr%d %s" % (b, bank), P, scale=0.015625)
-            tt(T.xi[:, 4 * E + b:4 * C:4], T.rr[:, cut], plane(t, b, E + 1), A.add, "rr%d pn%d%d xn" % (b, t, b), "xn%d" % b, P)
+            cut = (P * b, P * b + P)
+            move(v("g1", *cut), (plane(t, b), v("cu", LA, LA + 18)))
+            tt(v("g2", *cut), (plane(t, b), v("cw", LB, LB + 18)), v("g1", *cut), A.max)
+            tt(v("mt", b, 4 * P, 4), (plane(t, b), v("cw", LD, LD + 18)), v("g2", *cut), A.add)
+        qz("m", 0, P, v("mt"))
+        for b in range(4):
+            cut, mine = (P * b, P * b + P), v("xi", 4 * E + b, 4 * C, 4)
+            mm(b + 1, "w", 128 * b, "m", 0, P)
+            act(v("rr", *cut), bank(b + 1, P), F.Relu, scale=0.015625)
+            tt(mine, v("rr", *cut), mine, A.add)
             if not last:
-                act(plane(t + 1, b, E + 1), T.xi[:, 4 * E + b:4 * C:4], F.Copy, "xn%d" % b, "pn%d%d" % (t + 1, b), P)
+                move(plane(t + 1, b, E + 1), mine, True)
         for b in range(4):
-            came = T.dp[:, K * b:K * b + K].indirect(T["hl%d" % t][:])
-            rd = "dp%d list%d pe%d%d" % (b, t, t, b)
-            if last:
-                tt(T.fi[:, b:4 * E:4], came, plane(t, b, 1, E + 1), A.max, rd + " fi", "xf%d" % b, dur=gcost(32))
-            else:
-                tt(plane(t + 1, b, 1, E + 1), came, plane(t, b, 1, E + 1), A.max, rd, "pe%d%d" % (t + 1, b), dur=gcost(32))
-                move(T.xi[:, b:4 * E:4], plane(t + 1, b, 1, E + 1), "pe%d%d xe" % (t + 1, b), "xe%d" % b, E)
-    move(T.odb[:], T.it[:, 0:K + 1].indirect(lv[:, LD:LD + 18]), "it ld", "odb", P, True)
-    dma("y", T.od[:], T.odb[0:128:16, :], "odb", "")
-    qz(T.qx[:], T.sx[:], T.xi[:, 4 * E:4 * C], XN, "qx", P)
-    mm(ps[:, 0:P], T.qv[:], T.sv[:], T.qx[:], T.sx[:], "qv qx", "bank0", P)
-    move(T.ys[:, E:C], ps[:, 0:P], "bank0", "bank0 yn", P)
-    dma("y", T.oc[:, 4 * E:4 * C], T.qx[:].bitcast(u8), "qx", "")
-    dma("y", T.y[:, E:C], T.ys[:, E:C], "yn", "")
+            mm(5 + b % 3, "i", 128 * b, "f", landing(t), 128)
+            tt(v("xi", b, 4 * E, 4) if last else plane(t + 1, b, 1, E + 1), bank(5 + b % 3, E), plane(t, b, 1, E + 1), A.max)
+    move(v("odb"), (v("it", 0, K + 1), v("cw", LD, LD + 18)))
+    dma("y", T.od[:], T.odb[0:128:16, :], [v("odb")], [])
+    qz("x", 0, P, nodes)
+    mm(0, "v", 0, "x", 0, P)
+    move(v("ys", E, C), bank(0, P))
+    dma("y", T.oc[:, 4 * E:4 * C], T.qx[:].bitcast(u8), [v("qx")], [])
+    dma("y", T.y[:, E:C], T.ys[:, E:C], [v("ys", E, C)], [])
     for k in range(4):
-        dma("ys"[k % 2], T.osc[4 * k:4 * k + 4, E:C], T.sx[32 * k:32 * k + 4, :], "qx", "")
-    qz(T.qe[:], T.se[:], T.fi[:], "fi xf0 xf1 xf2 xf3", "qe", 128)
-    mm(ps[:, 3072:3072 + 128], T.qv[:], T.sv[:], T.qe[:], T.se[:], "qv qe", "bank6", 128)
-    move(T.ys[:, 0:E], ps[:, 3072:3072 + E], "bank6", "bank6 ye", 32)
-    dma("y", T.oc[:, 0:4 * E], T.qe[:, 0:E].bitcast(u8), "qe", "")
+        dma("ys", T.osc[4 * k:4 * k + 4, E:C], T.sx[32 * k:32 * k + 4, :], [v("sx")], [])
+    qz("e", 0, 128, v("xi", 0, 512))
+    mm(6, "v", 0, "e", 0, 128)
+    move(v("ys", 0, E), bank(6, E))
+    dma("ys", T.oc[:, 0:4 * E], T.qe[:, 0:E].bitcast(u8), [v("qe")], [])
     for k in range(4):
-        dma("ys"[k % 2], T.osc[4 * k:4 * k + 4, 0:E], T.se[32 * k:32 * k + 4, 0:E], "qe", "")
-    dma("s", T.y[:, 0:E], T.ys[:, 0:E], "ye", "")
+        dma("ys", T.osc[4 * k:4 * k + 4, 0:E], T.se[32 * k:32 * k + 4, 0:E], [v("se")], [])
+    dma("ys", T.y[:, 0:E], T.ys[:, 0:E], [v("ys", 0, E)], [])
     emit(g, T, ops)

@@ -7,28 +7,31 @@ K = C - B
 PL = 336
 X4, S_, BF, F32, U8 = "float8_e4m3fn_x4", "sbuf", "bfloat16", "float32", "uint8"
 SCRATCH = {"ps": ("psum", [128, 4096], F32)}
-for _n, _w in (("xi", 4 * C), ("xp", 12 * PL), ("ut", 512), ("vt", 512), ("et", 2048), ("ones", 512), ("uu", 672), ("ba", 2 * P),
-               ("lm", 2 * P), ("sc", 240), ("hw", P), ("j16", P), ("ls", P), ("tt", 624), ("jb", 1792), ("nb", 288), ("fl", 2 * K),
-               ("cs", 2 * K + 2), ("fc", 128), ("ft", 512), ("g1", 4 * P), ("g2", 4 * P), ("mt", 4 * P)):
+for _n, _w in (("xi", 4 * PL), ("xp", 12 * PL), ("ut", 512), ("vt", 512), ("et", 520), ("uu", 672), ("ba", 2 * P),
+               ("lm", 2 * P), ("sc", 240), ("hw", P), ("j16", P), ("ls", P), ("tt", 624), ("jb", 1792), ("nb", 288),
+               ("fl", 2 * K + 2), ("cs", 576), ("fc", 128), ("ft", 648), ("g1", 4 * P), ("g2", 4 * P), ("mt", 4 * P)):
     SCRATCH[_n] = (S_, [128, _w], BF)
 for _n, _w in (("cf", 128), ("dg", 32), ("nd", 32), ("it", 336), ("oh", 64), ("oz", 48), ("tabn", 592), ("scl", 32), ("jt", 32),
-               ("sel", 108), ("qa", 112), ("val", 120), ("sd", 112), ("so", 112), ("js", 1152), ("pk", 8), ("sm2", 32),
+               ("sel", 108), ("lp", 84), ("qa", 112), ("val", 120), ("sd", 112), ("so", 112), ("js", 1152), ("pk", 8), ("sm2", 32),
                ("key", 96), ("rr", 4 * P), ("ys", C), ("odb", P)):
     SCRATCH[_n] = (S_, [128, _w], F32)
-for _n, _w in (("pai", 32), ("pbi", 32), ("ci", 64), ("ni", 32)):
+for _n, _w in (("pab", 36), ("ci", 64), ("ni", 32)):
     SCRATCH[_n] = (S_, [128, _w], "int32")
-for _n, _w in (("cu", 160), ("cw", 80), ("llu", 80)):
+for _n, _w in (("cu", 160), ("cw", 80), ("llu", 112)):
     SCRATCH[_n] = (S_, [128, _w], "uint16")
 for _n, _w in (("u", 128), ("v", 128), ("up", 128 * R), ("w", 512), ("x", P), ("e", 128), ("m", P), ("i", 512),
                ("f", E * R + 128 * R)):
     SCRATCH["q" + _n] = (S_, [128, _w], X4)
     SCRATCH["s" + _n] = (S_, [128, _w], U8)
-NDMA = 22
+NDMA = 28
 SEMAPHORES = (["cv", "cs", "ct", "cg", "sent"] + ["%s%d" % (k, t) for k in ("qf", "sf") for t in range(R)]
               + ["dm%d" % i for i in range(NDMA)])
+HALF, FULL = ((0, 128), (128, P)), ((0, P),)
+BYDMA, HL, HP, HC = (), (0, 1, 2), (), (0, 1, 2)
 CY = 0.83e-3
 CASES = ((0.03, 1.2, 0.10, 3.0), (0.0, 1.0, 0.2, 3.0), (0.04, 1.4, 0.12, 4.0))
-TRIES = 60000
+DD, DL, DS = 0.6, 1.5, 1.0
+SHAKES, TRIES = 2500, 20000
 PLAN = {}
 
 
@@ -70,48 +73,82 @@ def plan(ops):
     for i in range(n):
         for d in dep[i]:
             succ[d].append(i)
-    qs = sorted(set(k for o in ops for k in o["alt"]))
-    alt = [[qs.index(k) for k in o["alt"]] for o in ops]
-    either = [i for i in range(n) if len(alt[i]) > 1]
     cases = []
     for add, f, w, net in CASES:
-        cases.append(([{qs.index(k): d * f + add if o["kind"] == "c" else d for k, (_fn, d) in o["alt"].items()} for o in ops],
+        cases.append(([{k: d * f + add if o["kind"] == "c" else d for k, (_fn, d) in o["alt"].items()} for o in ops],
                       [o["lat"] + (w if o["kind"] == "c" else net if o["kind"] == "n" else 0.0) for o in ops]))
     dur, lat = cases[0]
-    prio = [0.0] * n
-    for i in range(n - 1, -1, -1):
-        prio[i] = dur[i][alt[i][0]] + lat[i] + 1e-6 + max([prio[s] for s in succ[i]] + [0.0])
-    q, order, left = [a[0] for a in alt], [], [len(d) for d in dep]
-    free, done, ready = [0.0] * len(qs), [0.0] * n, [i for i in range(n) if not dep[i]]
-    while ready:
-        start = {}
-        for i in ready:
-            s = max([done[d] for d in dep[i]] + [0.0])
-            q[i] = min(alt[i], key=lambda k: max(s, free[k]) + dur[i][k])
-            start[i] = max(s, free[q[i]])
-        first = min(start.values())
-        i = max((j for j in ready if start[j] <= first + 0.15), key=lambda j: prio[j])
-        free[q[i]] = start[i] + dur[i][q[i]]
-        done[i] = free[q[i]] + lat[i]
-        order.append(i)
-        ready.remove(i)
-        for s in succ[i]:
-            left[s] -= 1
-            if not left[s]:
-                ready.append(s)
     seed = [99]
 
     def rnd():
         seed[0] = (seed[0] * 6364136223846793005 + 1442695040888963407) % (1 << 64)
         return (seed[0] >> 33) / float(1 << 31)
 
+    def lay(key, back):
+        pre, post = (succ, dep) if back else (dep, succ)
+        key = list(key)
+        for i in (range(n) if back else range(n - 1, -1, -1)):
+            for s in post[i]:
+                if key[s] >= key[i]:
+                    key[i] = key[s] + 1e-6
+        st, en, q, line = [0.0] * n, [0.0] * n, [None] * n, {}
+        for i in sorted(range(n), key=lambda j: -key[j]):
+            r = 0.0
+            for d in pre[i]:
+                x = en[d] if back else en[d] + lat[d]
+                if x > r:
+                    r = x
+            if back:
+                r += lat[i]
+            best = None
+            for k, du in dur[i].items():
+                a, z = line.setdefault(k, ([], []))
+                j, m, s = len(a), len(a), r
+                while j and z[j - 1] > r:
+                    j -= 1
+                while j < m and a[j] < s + du - 1e-9:
+                    s = max(s, z[j])
+                    j += 1
+                c = s + du * (1.5 if k == "v" else 1.0)
+                if best is None or c < best[0]:
+                    best = (c, k, s, j, du)
+            _c, k, s, j, du = best
+            line[k][0].insert(j, s)
+            line[k][1].insert(j, s + du)
+            st[i], en[i], q[i] = s, s + du, k
+        return max(en[i] + lat[i] for i in range(n)), st, en, q
+
+    def both(key):
+        best = got = lay(key, False)
+        for _ in range(3):
+            got = lay(lay([got[2][i] + lat[i] for i in range(n)], True)[2], False)
+            if got[0] >= best[0]:
+                break
+            best = got
+        return best
+
+    way = [0.0] * n
+    for i in range(n - 1, -1, -1):
+        way[i] = min(dur[i].values()) + lat[i] + max([way[s] for s in succ[i]] + [0.0])
+    best = cur = both(way)
+    for it in range(SHAKES):
+        mid, wide = rnd() * best[0], (3, 6, 12, 60)[int(rnd() * 4)]
+        got = both([-s + (5.0 * (rnd() - 0.5) if abs(s - mid) < wide else 0.0) for s in cur[1]])
+        if got[0] <= cur[0] + 0.1:
+            cur = got
+            if got[0] < best[0]:
+                best = got
+    q = best[3]
+    order = sorted(range(n), key=lambda i: (best[1][i], i))
+    either = [i for i in range(n) if len(dur[i]) > 1]
+
     def run(od):
         total = 0.0
         for du, la in cases[::-1]:
-            free, done = [0.0] * len(qs), [0.0] * n
+            free, done = {}, [0.0] * n
             for i in od:
                 k = q[i]
-                s = free[k]
+                s = free.get(k, 0.0)
                 for d in dep[i]:
                     if done[d] > s:
                         s = done[d]
@@ -131,7 +168,7 @@ def plan(ops):
         if rnd() < 0.06:
             flip = either[int(rnd() * len(either))]
             was = q[flip]
-            other = [k for k in alt[flip] if k != was]
+            other = [k for k in dur[flip] if k != was]
             q[flip] = other[int(rnd() * len(other))]
         else:
             a = int(rnd() * n)
@@ -148,7 +185,7 @@ def plan(ops):
             new = order[:a] + order[a + 1:]
             new.insert(b, i)
         got, dn = run(new)
-        if got <= cur or rnd() < math.exp((cur - got) / (0.08 * (1 - it / TRIES) + 0.003)):
+        if got <= cur or rnd() < math.exp((cur - got) / (0.03 * (1 - it / TRIES) + 0.003)):
             cur, order, done = got, new, dn
             if got < best:
                 best, bo, bq = got, list(new), list(q)
@@ -156,7 +193,7 @@ def plan(ops):
             q[flip] = was
     q[:] = bq
     done = run(bo)[1]
-    return best, bo, [done[i] - lat[i] - dur[i][q[i]] for i in range(n)], [qs[k] for k in bq]
+    return best, bo, [done[i] - lat[i] - dur[i][q[i]] for i in range(n)], bq
 
 
 def depend(ops):
@@ -164,8 +201,8 @@ def depend(ops):
     read = {n: [] for n in SCRATCH}
     for i, o in enumerate(ops):
         dep = set(o["after"])
-        rd = [x for x in o["r"] if x[0] in SCRATCH and x[0] != "ps"]
-        wr = [x for x in o["w"] if x[0] in SCRATCH and x[0] != "ps"]
+        rd = [x for x in o["r"] if x[0] != "ps"]
+        wr = [x for x in o["w"] if x[0] != "ps"]
         wr += [("ps", x[1] // 512 * 512, x[1] // 512 * 512 + 512, 1) for x in o["r"] + o["w"] if x[0] == "ps"]
         for n, a, z, s in rd + wr:
             dep.update(int(k) for k in set(wrote[n][a:z:s].tolist()) if k >= 0)
@@ -246,7 +283,7 @@ def rank_program(g, core, T, topo):
         return
     way_out, way_in = route(T, topo, rank), route(T, topo, (rank - 1) % n_ranks)
     arrive = len(topo.engines(way_in[-2], core))
-    V, S, ops = g.vector, g.scalar, []
+    V, S, ops, part = g.vector, g.scalar, [], ["head"]
 
     def v(name, a=0, z=None, s=1):
         return (name, a, SCRATCH[name][1][1] if z is None else z, s)
@@ -276,7 +313,7 @@ def rank_program(g, core, T, topo):
         return all(SCRATCH[x[0]][2] in (BF, "uint16") for x in xs)
 
     def op(alt, r, w, lat=0.0, kind="c", after=(), sem=None):
-        ops.append({"alt": alt, "r": r, "w": w, "lat": lat, "kind": kind, "after": list(after), "sem": sem})
+        ops.append({"alt": alt, "r": r, "w": w, "lat": lat, "kind": kind, "after": list(after), "sem": sem, "part": part[0]})
         return len(ops) - 1
 
     def vcost(out, a, *more, c=None):
@@ -301,8 +338,9 @@ def rank_program(g, core, T, topo):
     def cp(out, a):
         return op({"v": (lambda: V.tensor_copy(ap(out), ap(a)), vcost(out, a))}, views(a), [out])
 
-    def scan(out, a, b, o0, o1):
-        return op({"v": (lambda: V.tensor_tensor_scan(ap(out), ap(a), ap(b), 0.0, o0, o1), vcost(out, a, b))}, [a, b], [out])
+    def scan(out, a, b, o0, o1, first=0.0):
+        return op({"v": (lambda: V.tensor_tensor_scan(ap(out), ap(a), ap(b), ap(first), o0, o1), vcost(out, a, b))},
+                  views(a, b, first), [out])
 
     def turn(out, a):
         return op({"v": (lambda: V.transpose(ap(out), ap(a)), vcost(out, a))}, [a], [out])
@@ -339,7 +377,13 @@ def rank_program(g, core, T, topo):
         alt = {"v": (lambda: V.memset(ap(out), val), vcost(out, out))}
         if val == int(val):
             alt["g"] = (lambda: g.iota(ap(out), [[0, n]], int(val), 0, allow_small_or_imprecise_dtypes=True), 0.13 + 2 * n * CY)
-        return op(alt, [], [out])
+        if n > 64:
+            return op(alt, [], [out])
+        some = v("it", 0, n)
+        alt["s"] = (lambda: S.activation(ap(out), ap(some), F.Identity, bias=val, scale=0.0), scost(some))
+        if val != int(val):
+            alt["g"] = (lambda: g.affine_select(ap(out), ap(some), [[0, n]], A.is_gt, val, 0, 0), 0.17 + 2 * n * CY)
+        return op(alt, [some], [out])
 
     def mm(bank, l, la, r, ra, n):
         out = v("ps", 512 * bank, 512 * bank + n)
@@ -358,31 +402,31 @@ def rank_program(g, core, T, topo):
         return v("ps", 512 * k, 512 * k + n)
 
     u8 = dt.uint8
-    dma("y", T.xi[:], T.x[:], [], [v("xi")], 2.6)
+    first = dma("y", T.xi[:, 0:4 * C], T.x[:], [], [v("xi", 0, 4 * C)], 2.6)
     dma("s", T.ut[:], T.u[:], [], [v("ut")], 2.3)
-    dma("y", T.pai[:, 0:18], T.pa[:], [], [v("pai")], 2.6)
-    first = dma("y", T.pbi[:, 0:18], T.pb[:], [], [v("pbi")], 2.6)
+    dma("y", T.pab[:, 0:18], T.pa[:], [], [v("pab", 0, 18)], 2.4)
+    dma("y", T.pab[:, 18:36], T.pb[:], [], [v("pab", 18, 36)], 2.4)
     dma("y", T.qw[:].bitcast(u8), T.wc[:], [], [v("qw")], 3.0, [first])
     dma("y", T.sw[:], T.ws[:], [], [v("sw")], 3.0, [first])
     dma("y", T.vt[:], T.v[:], [], [v("vt")], 3.0, [first])
     lane, grp = col("cf", 0), col("cf", 1)
     iota(col("ci", 0), [[0, 1]], 0, 1)
     iota(v("ci", 8, 32), [[1, R], [16, 8]], 0)
-    iota(v("j16"), [[0, 18], [1, 16]], 0)
-    iota(v("it"), [[1, 336]], -1)
+    iota(v("j16", 0, 32), [[0, 2], [1, 16]], 0)
+    iota(v("j16", 32, P), [[0, 16], [1, 16]], 0)
+    iota(v("it", 0, 64), [[1, 64]], -1)
+    iota(v("it", 64, 336), [[1, 272]], 63)
     iota(v("cf", 32, 39), [[16, 7]], -4)
     iota(v("cf", 4, 8), [[1, 4]], 62)
     ts(col("ci", 1), col("ci", 0), 15, A.bitwise_and)
-    cp(lane, col("ci", 1))
     ts(col("ci", 2), col("ci", 0), 4, A.logical_shift_right)
-    cp(grp, col("ci", 2))
+    cp(v("cf", 0, 2), v("ci", 1, 3))
     cp(v("cu", 0, 24), v("ci", 8, 32))
     ts(v("hw"), v("j16"), lane, A.not_equal, 4.0, A.mult)
-    ts(v("nd"), v("j16", 0, 32), lane, A.not_equal)
     ts(v("dg"), v("j16", 0, 32), lane, A.is_equal)
+    lin(v("nd"), v("dg"), -1.0, 1.0)
     scan(v("cf", 64, 80), v("hw", 0, 16), v("dg", 0, 16), A.mult, A.add)
     power = col("cf", 79)
-    lin(v("cf", 12, 16), v("cf", 4, 8), 0.5)
     tt(v("cf", 16, 22), v("dg", 0, 12, 2), v("dg", 1, 12, 2), A.add)
     tt(v("cf", 80, 86), v("dg", 0, 12, 2), v("dg", 1, 12, 2), A.subtract)
     lin(v("cf", 24, 30), v("cf", 80, 86), 1.0 / 64)
@@ -392,34 +436,33 @@ def rank_program(g, core, T, topo):
     for k in range(NB - 1):
         lin(v("sc", B * k, B * k + B), v("it", 2, 2 + B), col("cf", 25 + k), col("dg", 2 * k + 3))
     fill(v("lm", 0, 2 * P, 2), 1.0)
-    LP, LQ, LL, LK = 24, 32, 40, 46
+    LP, LQ, LL, LK = 24, 32, 40, 48
     ef, ci = v("cf", 40, 47), v("ci", 32, 39)
-    ts(ef, v("cf", 32, 39), lane, A.add)
+    lin(ef, v("cf", 32, 39), 1.0, lane)
     ts(ci, ef, 1.0 / 6, A.mult, -0.42, A.add)
     ts(v("ci", 40, 47), ci, grp, A.add)
     ts(v("ci", 48, 55), v("ci", 40, 47), 1, A.bitwise_and)
-    ts(v("cf", 48, 55), v("ci", 48, 55), 152.0, A.mult)
+    lin(v("lp", 0, 28, 4), ef)
+    ts(v("lp", 1, 28, 4), ci, 2.0, A.mult)
+    ts(v("lp", 2, 28, 4), v("ci", 48, 55), 152.0, A.mult)
     ts(v("cf", 56, 63), ci, 6.34, A.mult, 0.01, A.add)
-    tt(v("cf", 88, 95), ef, v("cf", 56, 63), A.is_gt)
-    ts(v("cf", 96, 103), v("cf", 88, 95), 1000.0, A.mult)
-    ts(v("cf", 104, 111), ci, 2.0, A.mult)
-    tt(v("cf", 48, 55), v("cf", 48, 55), ef, A.add)
-    tt(v("cf", 96, 103), v("cf", 96, 103), v("cf", 104, 111), A.add)
-    tt(v("cf", 48, 55), v("cf", 48, 55), v("cf", 96, 103), A.add)
-    ts(v("cf", 56, 63), v("cf", 48, 55), 2.0, A.mult, 608.0, A.min)
-    cp(v("cu", LP, LP + 7), v("cf", 56, 63))
-    ts(v("cu", LQ, LQ + 7), v("cf", 56, 63), 1.0, A.add)
+    tt(v("lp", 3, 28, 4), ef, v("cf", 56, 63), A.is_gt)
+    fill(v("lp", 28, 56), 1.0)
+    fill(v("lp", 28, 56, 4), 0.0)
+    fill(v("lp", 31, 56, 4), 1.0 / 1024)
+    scan(v("lp", 56, 84), v("lp", 28, 56), v("lp", 0, 28), A.mult, A.add)
+    ts(v("cu", LP, LP + 7), v("lp", 59, 84, 4), 2048.0, A.mult, 608.0, A.min)
+    ts(v("cu", LQ, LQ + 7), v("cu", LP, LP + 7), 1.0, A.add)
     fill(v("tt", 608, 624), 0.0)
-    fill(v("sd"), -B / 32768.0)
+    fill(v("sd", 0, 56), -B / 32768.0)
+    fill(v("sd", 56, 112), -B / 32768.0)
     fill(v("sd", 4, 112, 6), -4.0)
     fill(v("sd", 5, 112, 6), -E / 32768.0)
-    span = [(0, 18), (32, 48), (48, 61), (22, 32), (64, 71), (18, 22)]
-    ts(col("cf", 112), lane, 2.0, A.is_ge, -13.0, A.mult)
-    ts(col("cf", 113), lane, 6.0, A.is_ge, -62.0, A.mult)
-    ts(col("cf", 114), col("cf", 112), col("cf", 113), A.add, 100.0, A.add)
-    for c, add in enumerate((4.0, col("cf", 114), 23.0, 42.0, 80.0)):
-        lin(col("cf", 116 + c), lane, 6.0, add)
-    ts(v("cu", LL, LL + 5), v("cf", 116, 121), 112.0, A.min)
+    span = [(0, 18), (32, 48), (48, 61), (64, 74), (80, 87), (96, 100)]
+    iota(v("cf", 112, 114), [[96, 2]], 4)
+    iota(v("cf", 114, 119), [[19, 5]], 23)
+    lin(col("cf", 120), lane, 6.0)
+    ts(v("cu", LL, LL + 7), v("cf", 112, 119), col("cf", 120), A.add, 112.0, A.min)
     fill(v("val", 112, 120), 49 / 32768.0)
     fill(col("oh", 0), 0.0)
     fill(v("oh", 49, 64), -7.0 * 65793)
@@ -432,33 +475,34 @@ def rank_program(g, core, T, topo):
     iota(v("tabn", 144, 256), [[1, 112]], 1)
     iota(v("tabn", 256, 592), [[1, 336]], -31)
     ts(col("ci", 5), lane, 1.0 / 3, A.mult)
-    ts(col("ci", 6), lane, 0.0, A.mult, 5.0, A.add)
+    iota(col("ci", 6), [[0, 1]], 5)
     cp(v("cu", LK, LK + 2), v("ci", 5, 7))
     fill(col("scl", 0), 1.0)
     fill(col("scl", 1), 1.0 / 4096)
     for f in range(3):
         fill(v("scl", 2 + f, 32, 3), 256.0 ** -f)
     for k in range(2):
-        lin(col("cf", 8 + k), lane, -1.0, -1.5 - 16 * k)
         lin(col("cf", 10 + k), lane, 1.0, 0.5 + 16 * k)
+    lin(v("cf", 8, 10), v("cf", 10, 12), 1.0, -float(E))
     lin(v("jt"), v("it", 1, 33), 1.0 / 64)
-    fill(v("cs", 2 * K, 2 * K + 2), -1.0)
+    iota(v("cf", 122, 126), [[2 * PL, 4]], K + 2)
+    fill(col("fl", K), -float(E))
+    fill(col("cs", 0), 0.0)
     fill(col("nb", 0), 0.0)
     fill(v("xp", 0, 12 * PL, PL), 0.0)
+    fill(v("xi", 4 * C, 4 * PL), 0.0)
     fill(v("sel", 0, 36, 2), 0.0)
-    fill(v("ft", 128, 512), 0.0)
-    fill(v("ft", 0, 128), 0.0)
-    iota(v("ones"), [[0, 512]], 1)
+    fill(v("ft"), 0.0)
+    op({"g": (lambda: g.affine_select(T.et[:], T.ft[:, 128:648], [[1, 520]], A.not_equal, 1.0, -3, -4), 0.17 + 1040 * CY)},
+       [v("ft", 128, 648)], [v("et")])
     for b in range(4):
-        op({"g": (lambda b=b: g.affine_select(T.et[:, 512 * b:512 * b + 512], T.ones[:], [[1, 512]], A.is_equal, 0.0, -b, -4), 1.02)},
-           [v("ones")], [v("et", 512 * b, 512 * b + 512)])
-    qz("i", 0, 512, v("et"))
-    LA, LA0, LA1, LB0, LB1 = 48, 66, 85, 104, 123
-    LB, LD, LN, LF, LC, LR = 0, 18, 36, 54, 56, 58
-    pa, pb = v("pai", 0, 18), v("pbi", 0, 18)
+        qz("i", 128 * b, 128 * b + 128, v("et", 3 - b, 515 - b))
+    LA, LA0, LB0, LA1, LB1 = 50, 68, 86, 105, 123
+    LB, LD, LN, LF, LC, LR = 0, 18, 36, 54, 56, 64
+    pa, pb = v("pab", 0, 18), v("pab", 18, 36)
     ts(v("cu", LA, LA + 18), pa, 1.0, A.add)
-    for at, lst in ((LA0, pa), (LB0, pb), (LA1, pa), (LB1, pb)):
-        ts(v("cu", at, at + 18), lst, 2.0, A.mult, 1.0, A.add)
+    for at in (LA0, LA1):
+        ts(v("cu", at, at + 36), v("pab"), 2.0, A.mult, 1.0, A.add)
     tt(v("sel", 36, 72, 2), pa, pb, A.subtract)
     ts(v("sel", 37, 72, 2), pb, 1.0, A.add)
 
@@ -477,19 +521,20 @@ def rank_program(g, core, T, topo):
     preds(0)
     qz("u", 0, 128, v("ut"))
     qz("v", 0, 128, v("vt"))
-    for t in range(R):
-        out, src = v("qup", 128 * t, 128 * t + 128), (v("qu"), v("cu", 8 * t, 8 * t + 8))
+    for a, z in ((0, 1), (1, R)):
+        out, src = v("qup", 128 * a, 128 * z), (v("qu"), v("cu", 8 * a, 8 * z))
         op({"v": (lambda out=out, src=src: V.tensor_copy(ap(out, dt.uint32), ap(src, dt.uint32)), vcost(out, src))}, views(src), [out])
-        move(v("sup", 128 * t, 128 * t + 128), (v("su"), src[1]))
+        move(v("sup", 128 * a, 128 * z), (v("su"), src[1]))
     for b in range(4):
-        move(plane(0, b, 1), v("xi", b, 4 * C, 4), True)
+        move(plane(0, b, 1, PL), v("xi", b, 4 * PL - 4, 4), True)
     nodes = v("xi", 4 * E, 4 * C)
     for t in range(R):
         last = t == R - 1
-        qz("x", 0, P, nodes)
-        mm(0, "up", 128 * t, "x", 0, P)
-        act(v("lm", 1, 2 * B, 2), bank(0, B), F.Sign, scale=-1.0)
-        act(v("lm", 2 * B + 1, 2 * P, 2), v("ps", B, P), F.Sign, scale=-1.0)
+        part[0] = "dom%d" % t
+        for a, z in (HALF if t in HC else FULL):
+            qz("x", a, z, v("xi", 4 * (E + a), 4 * (E + z)))
+            mm(0, "up", 128 * t, "x", a, z - a)
+            act(v("lm", 2 * a + 1, 2 * z, 2), bank(0, z - a), F.Sign, scale=-1.0)
         scan(v("ls"), v("hw"), v("lm", 1, 2 * P, 2), A.mult, A.add)
         ts(v("sel", 1, 36, 2), v("ls", 15, P, 16), 2.0, A.mult, power, A.is_gt)
         scan(v("sel", 72, 108), v("sel", 0, 36), v("sel", 36, 72), A.mult, A.add)
@@ -507,7 +552,8 @@ def rank_program(g, core, T, topo):
         tt(v("val", 0, 112), (v("tt"), v("cu", LP, LP + 7)), v("qa"), A.add)
         scan(v("so"), v("sd"), v("val", 0, 112), A.add, A.max)
         ts(v("cw", LD, LD + 18), v("so", 9, 112, 6), 32768.0, A.mult, float(E + 4 * B), A.add)
-        ts(v("llu"), (v("val"), v("cu", LL, LL + 5)), 32768.0, A.mult)
+        part[0] = "side%d" % t
+        ts(v("llu"), (v("val"), v("cu", LL, LL + 7)), 32768.0, A.mult)
         o = 0
         for l, (a, z) in enumerate(span):
             n = 16 * (z - a)
@@ -520,55 +566,69 @@ def rank_program(g, core, T, topo):
         nb = v("nb", 1, K + 1)
         move(nb, (v("tabn"), v("cw", LN, LN + 17)))
         for k in range(2):
-            act(v("jb", K * k, K * k + K), nb, F.Sign, bias=col("cf", 8 + k), acc=col("sm2", k))
-        ts(v("cw", LF, LF + 2), v("sm2", 0, 2), float(2 * E - K), A.is_ge)
+            act(v("jb", K * k, K * k + K), nb, F.Sign, bias=col("cf", 10 + k), scale=-1.0, acc=col("sm2", k))
+        ts(v("cw", LF, LF + 2), v("sm2", 0, 2), float(K - 2 * E), A.is_le)
         tau = col("sm2", 2)
         act(v("jb", 544, 576), (v("j16", 0, 16), v("cw", LF, LF + 2)), F.Copy, acc=tau)
-        ts(v("fl", 0, K), nb, tau, A.subtract, 1.0, A.is_gt)
-        ts(v("fl", K, 2 * K), nb, tau, A.subtract, 1.0, A.is_equal)
-        scan(v("cs", 0, 2 * K), v("fl"), v("fl"), A.add, A.max)
+        ts(v("fl", 0, K), nb, tau, A.is_gt)
+        ts(v("fl", K + 1, 2 * K + 1), nb, tau, A.is_ge)
+        scan(v("cs", 1, K + 1), v("fl", 0, K), v("fl", 0, K), A.add, A.max)
+        above = col("cs", K)
+        scan(v("cs", 288, 289 + K), v("fl", K, 2 * K + 1), v("cs", 0, K + 1), A.add, A.min, above)
+        act(v("sm2", 6, 8), v("cf", 8, 10), F.Identity, bias=above)
         for k in range(2):
-            act(v("jb", 576 + 560 * k, 1122 + 560 * k), v("cs"), F.Sign, bias=col("cf", 10 + k), scale=-1.0, acc=col("sm2", 4 + k))
-        ts(v("sm2", 6, 8), v("sm2", 4, 6), 1.0, A.is_lt, float(K), A.mult)
-        for k in range(2):
-            ts(col("cw", LC + k), col("sm2", 4 + k), 0.5, A.mult, col("sm2", 6 + k), A.add)
-        lc = v("cw", LC, LC + 2)
-        tt(v("key", 0, 32), (v("nb", 0, K + 1), lc), v("jt"), A.subtract)
+            act(v("jb", 576 + K * k, 576 + K * k + K), v("cs", 289, 289 + K), F.Sign, bias=col("sm2", 6 + k), scale=-1.0,
+                acc=col("sm2", 4 + k))
+            ts(v("cw", LC + k, LC + 8, 2), v("cf", 122, 126), col("sm2", 4 + k), A.add, 0.5, A.mult)
+        tt(v("key", 0, 32), (v("nb", 0, K + 1), v("cw", LC, LC + 2)), v("jt"), A.subtract)
         tt(v("key", 32, 64), v("key", 0, 32), v("dg"), A.mult)
         scan(v("key", 64, 96), v("nd"), v("key", 32, 64), A.mult, A.add)
         for k in range(2):
             act(v("jb", 1696 + 32 * k, 1728 + 32 * k), v("key", 0, 32), F.Sign, bias=col("key", 79 + 16 * k), scale=-1.0,
                 acc=col("sm2", 10 + k))
-            ts(v("cw", LR + k, LR + 8, 2), v("cf", 12, 16), col("sm2", 10 + k), A.subtract, 2.0, A.mult)
-        for b in range(4):
-            move(v("fc", E * b, E * b + E), (plane(t, b), lc))
+            ts(v("cw", LR + k, LR + 8, 2), v("cf", 4, 8), col("sm2", 10 + k), A.subtract, col("sm2", 10 + k), A.subtract)
+        move(v("fc"), (v("xp", 4 * t * PL, 4 * (t + 1) * PL), v("cw", LC, LC + 8)))
         lr = v("cw", LR, LR + 8)
         op({"v": (lambda lr=lr: V.tensor_copy(T.ft[:, 0:128].indirect(ap(lr)), T.fc[:]), 0.05 + 128 * 3.8 * CY)},
            [lr, v("fc")], [v("ft", 0, 128)])
         own = E * R + 128 * t
-        qz("f", own, own + 128, v("ft"))
+        qz("f", own, own + 128, v("ft", 0, 512))
         sent = []
         for name in ("qf", "sf"):
             sent = [op({"g": (lambda name=name, t=t, own=own: hand(g, T, topo, core, way_out[1], name, t, own), 0.3)},
                        [v(name, own, own + E)], [], kind="r", after=sent)]
             op({"n" + name: (None, 0.0)}, [], [v(name, landing(t), landing(t) + E)], kind="n", after=sent,
                sem=("%s%d" % (name, t), arrive))
+        part[0] = "layer%d" % t
         for b in range(4):
-            cut = (P * b, P * b + P)
-            move(v("g1", *cut), (plane(t, b), v("cu", LA, LA + 18)))
-            tt(v("g2", *cut), (plane(t, b), v("cw", LB, LB + 18)), v("g1", *cut), A.max)
-            tt(v("mt", b, 4 * P, 4), (plane(t, b), v("cw", LD, LD + 18)), v("g2", *cut), A.add)
-        qz("m", 0, P, v("mt"))
+            cut, win = (P * b, P * b + P), plane(t, b, 0, K + 1)
+            move(v("g1", *cut), (win, v("cu", LA, LA + 18)))
+            tt(v("g2", *cut), (win, v("cw", LB, LB + 18)), v("g1", *cut), A.max)
+        for a, z in (HALF if t in HL else FULL):
+            for b in range(4):
+                win = plane(t, b, 0, 1 + E + B * ((z - 1) // B))
+                tt(v("mt", 4 * a + b, 4 * z, 4), (win, v("cw", LD + a // 16, LD + z // 16)), v("g2", P * b + a, P * b + z), A.add)
+            qz("m", a, z, v("mt", 4 * a, 4 * z))
+            for b in range(4):
+                mine, rr = v("xi", 4 * (E + a) + b, 4 * (E + z), 4), v("rr", 4 * a + b, 4 * z, 4)
+                mm(b + 1, "w", 128 * b, "m", a, z - a)
+                act(rr, bank(b + 1, z - a), F.Relu, scale=0.015625)
+                if t not in BYDMA:
+                    tt(mine, rr, mine, A.add)
+            if t in BYDMA:
+                x, rr = v("xi", 4 * (E + a), 4 * (E + z)), v("rr", 4 * a, 4 * z)
+                op({"g": (lambda x=x, rr=rr: g.dma_start(ap(x), ap(rr), accum_op=A.add), DD)}, [rr, x], [x],
+                   lat=DL + DS * (z - a) / P, kind="d")
+        if not last:
+            for a, z in (HALF if t in HP else FULL):
+                z = PL - E - 1 if z == P else z
+                for b in range(4):
+                    move(plane(t + 1, b, E + 1 + a, E + 1 + z), v("xi", 4 * (E + a) + b, 4 * (E + z), 4), True)
+        part[0] = "ent%d" % t
         for b in range(4):
-            cut, mine = (P * b, P * b + P), v("xi", 4 * E + b, 4 * C, 4)
-            mm(b + 1, "w", 128 * b, "m", 0, P)
-            act(v("rr", *cut), bank(b + 1, P), F.Relu, scale=0.015625)
-            tt(mine, v("rr", *cut), mine, A.add)
-            if not last:
-                move(plane(t + 1, b, E + 1), mine, True)
-        for b in range(4):
-            mm(5 + b % 3, "i", 128 * b, "f", landing(t), 128)
-            tt(v("xi", b, 4 * E, 4) if last else plane(t + 1, b, 1, E + 1), bank(5 + b % 3, E), plane(t, b, 1, E + 1), A.max)
+            mm(7 - b, "i", 128 * b, "f", landing(t), 128)
+            tt(v("xi", b, 4 * E, 4) if last else plane(t + 1, b, 1, E + 1), bank(7 - b, E), plane(t, b, 1, E + 1), A.max)
+    part[0] = "out"
     move(v("odb"), (v("it", 0, K + 1), v("cw", LD, LD + 18)))
     dma("y", T.od[:], T.odb[0:128:16, :], [v("odb")], [])
     qz("x", 0, P, nodes)

@@ -4,65 +4,80 @@ from concourse.mybir import dt, AluOpType as A, ActivationFunctionType as F
 
 C, E, B, NB, P, R = 320, 32, 48, 6, 288, 3
 K = C - B
-PL = 336
+PL = 288
+XO = 96
+XF = 162
+XW = XO + C
 X4, S_, BF, F32, U8 = "float8_e4m3fn_x4", "sbuf", "bfloat16", "float32", "uint8"
 SCRATCH = {"ps": ("psum", [128, 4096], F32)}
-for _n, _w in (("xi", 4 * PL), ("xp", 12 * PL), ("ut", 512), ("vt", 512), ("et", 520), ("uu", 672), ("ba", 2 * P),
-               ("lm", 2 * P), ("sc", 240), ("hw", P), ("j16", P), ("ls", P), ("tt", 624), ("jb", 1792), ("nb", 288),
-               ("fl", 2 * K + 2), ("cs", 576), ("fc", 128), ("ft", 648), ("g1", 4 * P), ("g2", 4 * P), ("mt", 4 * P)):
+for _n, _w in (("xi", 4 * (XF + C)), ("xp", 12 * PL), ("ut", 512), ("vt", 512), ("et", 520), ("uu", 1008), ("ba", 3 * P),
+               ("lm", 3 * P), ("hw", P), ("j16", P), ("ls", P), ("tt", 624), ("jb", 1792), ("nb", 288), ("fl", 2 * K + 2),
+               ("cs", 576), ("fc", 128), ("dp", 4 * PL), ("dor", 128), ("g1", 4 * P), ("g2", 4 * P), ("mt", 4 * P)):
     SCRATCH[_n] = (S_, [128, _w], BF)
-for _n, _w in (("cf", 128), ("dg", 32), ("nd", 32), ("it", 336), ("oh", 64), ("oz", 48), ("tabn", 592), ("scl", 32), ("jt", 32),
-               ("sel", 108), ("lp", 84), ("qa", 112), ("val", 120), ("sd", 112), ("so", 112), ("js", 1152), ("pk", 8), ("sm2", 32),
-               ("key", 96), ("rr", 4 * P), ("ys", C), ("odb", P)):
+for _n, _w in (("cf", 128), ("dg", 32), ("nd", 32), ("it", 336), ("oh", 64), ("oz", 64), ("scl", 48), ("un", 96), ("jt", 64),
+               ("sel", 108), ("lp", 84), ("qa", 112), ("val", 120), ("sd", 112), ("dd", 112), ("js", 1168), ("pk", 8), ("sm2", 32),
+               ("key", 128), ("rr", 4 * P), ("ys", C), ("odb", P)):
     SCRATCH[_n] = (S_, [128, _w], F32)
-for _n, _w in (("pab", 36), ("ci", 64), ("ni", 32)):
+for _n, _w in (("pab", 36), ("ci", 64), ("ni", 48)):
     SCRATCH[_n] = (S_, [128, _w], "int32")
-for _n, _w in (("cu", 160), ("cw", 80), ("llu", 112)):
+for _n, _w in (("cu", 160), ("cw", 80), ("llu", 112), ("hs", 16 * R), ("hl", 16 * R)):
     SCRATCH[_n] = (S_, [128, _w], "uint16")
-for _n, _w in (("u", 128), ("v", 128), ("up", 128 * R), ("w", 512), ("x", P), ("e", 128), ("m", P), ("i", 512),
+for _n, _w in (("u", 128), ("v", 128), ("up", 128 * R), ("w", 512), ("x", XW * (R + 1)), ("m", P), ("i", 512), ("l", K * R),
                ("f", E * R + 128 * R)):
     SCRATCH["q" + _n] = (S_, [128, _w], X4)
     SCRATCH["s" + _n] = (S_, [128, _w], U8)
-NDMA = 28
-SEMAPHORES = (["cv", "cs", "ct", "cg", "sent"] + ["%s%d" % (k, t) for k in ("qf", "sf") for t in range(R)]
-              + ["dm%d" % i for i in range(NDMA)])
-HALF, FULL = ((0, 128), (128, P)), ((0, P),)
-BYDMA, HL, HP, HC = (), (0, 1, 2), (), (0, 1, 2)
+NDMA = 24
+SEMAPHORES = ["cv", "cs", "ct", "cg", "sent"] + ["got%d" % k for k in range(4 * R)] + ["dm%d" % i for i in range(NDMA)]
+EARLY = (0, 2)
+HALF = ((0, 160), (160, P))
 CY = 0.83e-3
-CASES = ((0.03, 1.2, 0.10, 3.0), (0.0, 1.0, 0.2, 3.0), (0.04, 1.4, 0.12, 4.0))
-DD, DL, DS = 0.6, 1.5, 1.0
-SHAKES, TRIES = 2500, 20000
+CASES = ((0.015, 1.15, 0.16, 3.0), (0.0, 1.0, 0.2, 3.0), (0.04, 1.4, 0.12, 4.0))
+FIRST = 1.5
+SHAKES, TRIES, SEED = 10000, 40000, 99
 PLAN = {}
 
 
-def route(T, topo, r):
+def route(T, topo, r, way):
     src, dst = T.cores[r], T.cores[(r + 1) % len(T.cores)]
     if topo.may_write(src, dst):
         return [src, dst]
     able = [c for c in topo.cores_of(src) if c != src and topo.may_write(c, dst)]
-    near = [c for c in able if topo.die(c) == topo.die(src)]
-    return [src, (near or able)[0], dst]
+    able.sort(key=lambda c: topo.die(c) != topo.die(src))
+    return [src, able[way % len(able)], dst]
 
 
-def landing(t):
-    return E * (R - 1 - t)
+def feed_at(t):
+    late = [k for k in range(R) if k not in EARLY]
+    return E * (len(late) - 1 - late.index(t)), E * len(late) + 128 * late.index(t)
 
 
-def hand(g, T, topo, src, dst, name, t, frm):
+def letters():
+    got = []
+    for t in range(R):
+        if t in EARLY:
+            got += [(0, "qx", XW * t + XO, "ql", K * t, K), (1, "sx", XW * t + XO, "sl", K * t, K),
+                    (0, "hs", 16 * t, "hl", 16 * t, 2), (1, "hs", 16 * t + 8, "hl", 16 * t + 8, 4)]
+        else:
+            got += [(k, n, feed_at(t)[1], n, feed_at(t)[0], E) for k, n in enumerate(("qf", "sf"))]
+    return got
+
+
+def hand(g, T, topo, src, dst, k, first):
+    _way, a, a0, z, z0, n = letters()[k]
     rid, pid = topo.addr(dst, src)
-    out, in_ = T[name][:, landing(t):landing(t) + E], T[name][:, frm:frm + E]
-    if name == "qf":
+    out, in_ = T[z][:, z0:z0 + n], T[a][:, a0:a0 + n] if first else T[z][:, z0:z0 + n]
+    if SCRATCH[z][2] == X4:
         out, in_ = out.bitcast(dt.uint8), in_.bitcast(dt.uint8)
-    g.remote_dma(out, in_, T.sem["%s%d" % (name, t)], T.sem.sent, pid, rid, topo.mask(src, dst))
+    g.remote_dma(out, in_, T.sem["got%d" % k], T.sem.sent, pid, rid, topo.mask(src, dst))
     return len(topo.engines(src, dst))
 
 
-def relay(g, T, topo, src, me, dst):
+def relay(g, T, topo, src, me, dst, ways):
     n, e = 0, len(topo.engines(src, me))
-    for t in range(R):
-        for name in ("qf", "sf"):
-            g.wait_ge(T.sem["%s%d" % (name, t)], e)
-            n += hand(g, T, topo, me, dst, name, t, landing(t))
+    for k, letter in enumerate(letters()):
+        if letter[0] in ways:
+            g.wait_ge(T.sem["got%d" % k], e)
+            n += hand(g, T, topo, me, dst, k, False)
     g.wait_ge(T.sem.sent, n)
 
 
@@ -78,7 +93,9 @@ def plan(ops):
         cases.append(([{k: d * f + add if o["kind"] == "c" else d for k, (_fn, d) in o["alt"].items()} for o in ops],
                       [o["lat"] + (w if o["kind"] == "c" else net if o["kind"] == "n" else 0.0) for o in ops]))
     dur, lat = cases[0]
-    seed = [99]
+    names = sorted(set(k for d in dur for k in d))
+    can = [[(k, du, du * (1.5 if k == "v" else 1.0)) for k, du in d.items()] for d in dur]
+    seed = [SEED]
 
     def rnd():
         seed[0] = (seed[0] * 6364136223846793005 + 1442695040888963407) % (1 << 64)
@@ -91,50 +108,53 @@ def plan(ops):
             for s in post[i]:
                 if key[s] >= key[i]:
                     key[i] = key[s] + 1e-6
-        st, en, q, line = [0.0] * n, [0.0] * n, [None] * n, {}
+        st, en, over, q, line = [0.0] * n, [0.0] * n, [0.0] * n, [None] * n, {k: ([], []) for k in names}
         for i in sorted(range(n), key=lambda j: -key[j]):
             r = 0.0
             for d in pre[i]:
-                x = en[d] if back else en[d] + lat[d]
-                if x > r:
-                    r = x
+                if over[d] > r:
+                    r = over[d]
             if back:
                 r += lat[i]
-            best = None
-            for k, du in dur[i].items():
-                a, z = line.setdefault(k, ([], []))
-                j, m, s = len(a), len(a), r
+            best = 1e9
+            for k, du, pen in can[i]:
+                a, z = line[k]
+                j = m = len(a)
+                s = r
                 while j and z[j - 1] > r:
                     j -= 1
                 while j < m and a[j] < s + du - 1e-9:
-                    s = max(s, z[j])
+                    if z[j] > s:
+                        s = z[j]
                     j += 1
-                c = s + du * (1.5 if k == "v" else 1.0)
-                if best is None or c < best[0]:
-                    best = (c, k, s, j, du)
-            _c, k, s, j, du = best
-            line[k][0].insert(j, s)
-            line[k][1].insert(j, s + du)
-            st[i], en[i], q[i] = s, s + du, k
+                if s + pen < best:
+                    best, bk, bs, bj, bd = s + pen, k, s, j, du
+            a, z = line[bk]
+            a.insert(bj, bs)
+            z.insert(bj, bs + bd)
+            st[i], en[i], q[i] = bs, bs + bd, bk
+            over[i] = bs + bd if back else bs + bd + lat[i]
         return max(en[i] + lat[i] for i in range(n)), st, en, q
 
     def both(key):
-        best = got = lay(key, False)
-        for _ in range(3):
-            got = lay(lay([got[2][i] + lat[i] for i in range(n)], True)[2], False)
-            if got[0] >= best[0]:
-                break
-            best = got
-        return best
+        first = lay(key, False)
+        again = lay(lay([first[2][i] + lat[i] for i in range(n)], True)[2], False)
+        return min(first, again, key=lambda x: x[0])
 
     way = [0.0] * n
     for i in range(n - 1, -1, -1):
         way[i] = min(dur[i].values()) + lat[i] + max([way[s] for s in succ[i]] + [0.0])
     best = cur = both(way)
+    parts = sorted(set(o["part"] for o in ops))
     for it in range(SHAKES):
-        mid, wide = rnd() * best[0], (3, 6, 12, 60)[int(rnd() * 4)]
-        got = both([-s + (5.0 * (rnd() - 0.5) if abs(s - mid) < wide else 0.0) for s in cur[1]])
-        if got[0] <= cur[0] + 0.1:
+        mid, wide = rnd() * best[0], (2, 4, 8)[int(rnd() * 3)]
+        if rnd() < 0.3:
+            one, by = parts[int(rnd() * len(parts))], 7.0 * (rnd() - 0.5)
+            key = [-s + (by if o["part"] == one and abs(s - mid) < 2 * wide else 0.0) for s, o in zip(cur[1], ops)]
+        else:
+            key = [-s + (3.5 * (rnd() - 0.5) if abs(s - mid) < wide else 0.0) for s in cur[1]]
+        got = both(key)
+        if got[0] <= cur[0] - 0.06 * (1 - it / SHAKES) * math.log(rnd() + 1e-9):
             cur = got
             if got[0] < best[0]:
                 best = got
@@ -277,12 +297,12 @@ def rank_program(g, core, T, topo):
     n_ranks = len(T.cores)
     if rank is None:
         for r in range(n_ranks):
-            way = route(T, topo, r)
-            if len(way) == 3 and way[1] == core:
-                relay(g, T, topo, way[0], core, way[2])
+            ways = [k for k in range(2) if route(T, topo, r, k)[1:-1] == [core]]
+            if ways:
+                relay(g, T, topo, T.cores[r], core, T.cores[(r + 1) % n_ranks], ways)
         return
-    way_out, way_in = route(T, topo, rank), route(T, topo, (rank - 1) % n_ranks)
-    arrive = len(topo.engines(way_in[-2], core))
+    to = [route(T, topo, rank, k)[1] for k in range(2)]
+    arrive = [len(topo.engines(route(T, topo, (rank - 1) % n_ranks, k)[-2], core)) for k in range(2)]
     V, S, ops, part = g.vector, g.scalar, [], ["head"]
 
     def v(name, a=0, z=None, s=1):
@@ -394,16 +414,37 @@ def rank_program(g, core, T, topo):
         e = {"y": g.sync, "s": g.scalar, "g": g}
         return op({q: (lambda q=q: e[q].dma_start(out, a), 0.1) for q in qs}, r, w, lat=lat, kind="d", after=after)
 
-    def plane(t, b, a=0, z=C + 1):
+    def plane(t, b, a=0, z=K + 1):
         o = (4 * t + b) * PL
         return v("xp", o + a, o + z)
+
+    def state(a, z, b=None):
+        return v("xi", 4 * (XF + a), 4 * (XF + z)) if b is None else v("xi", 4 * (XF + a) + b, 4 * (XF + z), 4)
+
+    def pack(t, a, z):
+        qz("x", XW * t + XO + a, XW * t + XO + z, state(a, z))
+        return XW * t + XO + a
 
     def bank(k, n):
         return v("ps", 512 * k, 512 * k + n)
 
+    def scatter(win, lst, src):
+        op({"v": (lambda: V.tensor_copy(ap(win).indirect(ap(lst)), ap(src)), 0.05 + size(src) * 3.8 * CY)}, [lst, src], [win])
+
+    sent = []
+
+    def post():
+        k = len(sent)
+        way, a, a0, z, z0, n = letters()[k]
+        sent.append(op({"g": (lambda: hand(g, T, topo, core, to[way], k, True), 0.3)}, [v(a, a0, a0 + n)], [], kind="r", after=sent[-1:]))
+        op({"n%d" % way: (None, 0.0)}, [], [v(z, z0, z0 + n)], kind="n", after=sent[-1:], sem=("got%d" % k, arrive[way]),
+           lat=(FIRST if k < 2 else 0.0) + (1.0 if n == K else -0.3 if n < E else 0.0))
+
     u8 = dt.uint8
-    first = dma("y", T.xi[:, 0:4 * C], T.x[:], [], [v("xi", 0, 4 * C)], 2.6)
+    mid = E + HALF[0][1]
+    dma("y", ap(state(0, mid)), T.x[:, 0:4 * mid], [], [state(0, mid)], 2.25)
     dma("s", T.ut[:], T.u[:], [], [v("ut")], 2.3)
+    first = dma("y", ap(state(mid, C)), T.x[:, 4 * mid:4 * C], [], [state(mid, C)], 2.6)
     dma("y", T.pab[:, 0:18], T.pa[:], [], [v("pab", 0, 18)], 2.4)
     dma("y", T.pab[:, 18:36], T.pb[:], [], [v("pab", 18, 36)], 2.4)
     dma("y", T.qw[:].bitcast(u8), T.wc[:], [], [v("qw")], 3.0, [first])
@@ -427,16 +468,17 @@ def rank_program(g, core, T, topo):
     lin(v("nd"), v("dg"), -1.0, 1.0)
     scan(v("cf", 64, 80), v("hw", 0, 16), v("dg", 0, 16), A.mult, A.add)
     power = col("cf", 79)
-    tt(v("cf", 16, 22), v("dg", 0, 12, 2), v("dg", 1, 12, 2), A.add)
     tt(v("cf", 80, 86), v("dg", 0, 12, 2), v("dg", 1, 12, 2), A.subtract)
     lin(v("cf", 24, 30), v("cf", 80, 86), 1.0 / 64)
-    fill(v("uu", 0, 64, 2), 0.0)
-    fill(v("uu", 640, 672), 0.0)
-    lin(v("uu", 1, 64, 2), v("it", 2, 34), col("cf", 24), col("dg", 1))
+    fill(v("uu", 0, 96), 0.0)
+    fill(v("uu", 960, 1008), 0.0)
+    lin(v("uu", 2, 96, 3), v("it", 2, 34), col("cf", 24), col("dg", 1))
+    fill(v("lm", 0, 3 * P, 3), 1.0)
+    fill(v("ba", 2, 3 * P, 3), 1.0)
     for k in range(NB - 1):
-        lin(v("sc", B * k, B * k + B), v("it", 2, 2 + B), col("cf", 25 + k), col("dg", 2 * k + 3))
-    fill(v("lm", 0, 2 * P, 2), 1.0)
-    LP, LQ, LL, LK = 24, 32, 40, 48
+        lin(v("lm", 144 * k + 2, 144 * k + 144, 3), v("it", 2, 2 + B), col("cf", 25 + k), col("dg", 2 * k + 3))
+    fill(v("lm", 3 * (P - B) + 2, 3 * P, 3), 0.0)
+    LP, LQ, LL, LK = 24, 32, 40, 142
     ef, ci = v("cf", 40, 47), v("ci", 32, 39)
     lin(ef, v("cf", 32, 39), 1.0, lane)
     ts(ci, ef, 1.0 / 6, A.mult, -0.42, A.add)
@@ -458,7 +500,7 @@ def rank_program(g, core, T, topo):
     fill(v("sd", 56, 112), -B / 32768.0)
     fill(v("sd", 4, 112, 6), -4.0)
     fill(v("sd", 5, 112, 6), -E / 32768.0)
-    span = [(0, 18), (32, 48), (48, 61), (64, 74), (80, 87), (96, 100)]
+    span = [(0, 19), (32, 48), (48, 61), (64, 74), (80, 87), (96, 100)]
     iota(v("cf", 112, 114), [[96, 2]], 4)
     iota(v("cf", 114, 119), [[19, 5]], 23)
     lin(col("cf", 120), lane, 6.0)
@@ -466,35 +508,42 @@ def rank_program(g, core, T, topo):
     fill(v("val", 112, 120), 49 / 32768.0)
     fill(col("oh", 0), 0.0)
     fill(v("oh", 49, 64), -7.0 * 65793)
-    fill(col("oz", 0), 4097.0)
+    fill(v("oz", 0, 49), 0.0)
+    fill(v("oz", 49, 64), -7.0 * 4097)
     for f in range(3):
         lin(v("oh", 1 + 16 * f, 17 + 16 * f), v("dg", 0, 16), 256.0 ** f)
     for f in range(2):
-        lin(v("oz", 1 + 16 * f, 17 + 16 * f), v("dg", 0, 16), 4096.0 ** f, 4097.0)
-    iota(v("tabn", 0, 144), [[1, 144]], 113)
-    iota(v("tabn", 144, 256), [[1, 112]], 1)
-    iota(v("tabn", 256, 592), [[1, 336]], -31)
-    ts(col("ci", 5), lane, 1.0 / 3, A.mult)
-    iota(col("ci", 6), [[0, 1]], 5)
-    cp(v("cu", LK, LK + 2), v("ci", 5, 7))
-    fill(col("scl", 0), 1.0)
-    fill(col("scl", 1), 1.0 / 4096)
-    for f in range(3):
-        fill(v("scl", 2 + f, 32, 3), 256.0 ** -f)
+        lin(v("oz", 1 + 16 * f, 17 + 16 * f), v("dg", 0, 16), 4096.0 ** f)
+    ts(col("ci", 5), lane, 1.0 / 6, A.mult, -0.09, A.add)
+    ts(col("ci", 6), lane, 1.0 / 6, A.mult, 16.0 / 6 - 0.09, A.add)
+    iota(col("ci", 7), [[0, 1]], 5)
+    cp(v("cu", LK, LK + 3), v("ci", 5, 8))
+    fill(v("scl"), 0.0)
+    fill(v("scl", 0, 4, 3), 1.0 / 4096)
+    fill(col("scl", 1), 1.0)
+    fill(v("scl", 5, 34, 6), 1.0)
+    fill(v("scl", 4, 34, 3), 1.0 / 256)
+    fill(v("scl", 6, 34, 3), 1.0 / 65536)
+    fill(v("scl", 8, 34, 6), 0.0)
+    fill(v("un", 0, 34), -256.0)
+    fill(v("un", 0, 34, 2), 0.0)
+    fill(col("un", 1), -4096.0)
     for k in range(2):
         lin(col("cf", 10 + k), lane, 1.0, 0.5 + 16 * k)
+        lin(col("cf", 2 + k), lane, -1.0 / 64, -k / 4.0)
+        lin(v("jt", 32 * k, 32 * k + 32), v("it", 1, 33), 1.0 / 64, col("cf", 2 + k))
     lin(v("cf", 8, 10), v("cf", 10, 12), 1.0, -float(E))
-    lin(v("jt"), v("it", 1, 33), 1.0 / 64)
     iota(v("cf", 122, 126), [[2 * PL, 4]], K + 2)
+    iota(v("cf", 104, 106), [[2 * E, 2]], E - 1)
+    fill(v("dp", 0, 4 * PL, PL), 0.0)
     fill(col("fl", K), -float(E))
     fill(col("cs", 0), 0.0)
     fill(col("nb", 0), 0.0)
     fill(v("xp", 0, 12 * PL, PL), 0.0)
-    fill(v("xi", 4 * C, 4 * PL), 0.0)
     fill(v("sel", 0, 36, 2), 0.0)
-    fill(v("ft"), 0.0)
-    op({"g": (lambda: g.affine_select(T.et[:], T.ft[:, 128:648], [[1, 520]], A.not_equal, 1.0, -3, -4), 0.17 + 1040 * CY)},
-       [v("ft", 128, 648)], [v("et")])
+    fill(state(-XF, 0), 0.0)
+    op({"g": (lambda: g.affine_select(T.et[:], T.xi[:, 128:648], [[1, 520]], A.not_equal, 1.0, -3, -4), 0.17 + 1040 * CY)},
+       [v("xi", 128, 648)], [v("et")])
     for b in range(4):
         qz("i", 128 * b, 128 * b + 128, v("et", 3 - b, 515 - b))
     LA, LA0, LB0, LA1, LB1 = 50, 68, 86, 105, 123
@@ -502,21 +551,15 @@ def rank_program(g, core, T, topo):
     pa, pb = v("pab", 0, 18), v("pab", 18, 36)
     ts(v("cu", LA, LA + 18), pa, 1.0, A.add)
     for at in (LA0, LA1):
-        ts(v("cu", at, at + 36), v("pab"), 2.0, A.mult, 1.0, A.add)
+        ts(v("cu", at, at + 36), v("pab"), 3.0, A.mult, 2.0, A.add)
     tt(v("sel", 36, 72, 2), pa, pb, A.subtract)
     ts(v("sel", 37, 72, 2), pb, 1.0, A.add)
 
     def preds(k):
-        win, x = v("uu", 0, 2 * (E + B * k)), k % 2
+        win, x = v("uu", 0, 3 * (E + B * k)), k % 2
         la, lb = (LA1 if x else LA0) + 3 * k, (LB1 if x else LB0) + 3 * k
-        a, b = (win, v("cu", la, la + 3)), (win, v("cu", lb, lb + 3))
-        oa, ob = v("ba", 96 * k + 1, 96 * k + 96, 2), v("ba", 96 * k, 96 * k + 96, 2)
-        if k < NB - 1:
-            tt(oa, a, v("sc", B * k, B * k + B), A.max)
-            lin(ob, b, 1.0, col("cf", 17 + k))
-        else:
-            move(oa, a)
-            move(ob, b)
+        move(v("ba", 144 * k, 144 * k + 144, 3), (win, v("cu", lb, lb + 3)))
+        move(v("ba", 144 * k + 1, 144 * k + 144, 3), (win, v("cu", la, la + 3)))
 
     preds(0)
     qz("u", 0, 128, v("ut"))
@@ -526,47 +569,49 @@ def rank_program(g, core, T, topo):
         op({"v": (lambda out=out, src=src: V.tensor_copy(ap(out, dt.uint32), ap(src, dt.uint32)), vcost(out, src))}, views(src), [out])
         move(v("sup", 128 * a, 128 * z), (v("su"), src[1]))
     for b in range(4):
-        move(plane(0, b, 1, PL), v("xi", b, 4 * PL - 4, 4), True)
-    nodes = v("xi", 4 * E, 4 * C)
+        move(plane(0, b, 1, PL), state(0, PL - 1, b), True)
     for t in range(R):
         last = t == R - 1
         part[0] = "dom%d" % t
-        for a, z in (HALF if t in HC else FULL):
-            qz("x", a, z, v("xi", 4 * (E + a), 4 * (E + z)))
-            mm(0, "up", 128 * t, "x", a, z - a)
-            act(v("lm", 2 * a + 1, 2 * z, 2), bank(0, z - a), F.Sign, scale=-1.0)
-        scan(v("ls"), v("hw"), v("lm", 1, 2 * P, 2), A.mult, A.add)
+        for a, z in HALF:
+            mm(0, "up", 128 * t, "x", pack(t, E + a, E + z), z - a)
+            act(v("lm", 3 * a + 1, 3 * z, 3), bank(0, z - a), F.Sign, scale=-1.0)
+        if t in EARLY:
+            pack(t, -XO, E)
+            post()
+            post()
+            for b in range(4):
+                mm(7 - b, "i", 128 * b, "l", K * t, K)
+                move(v("dp", PL * b + 1, PL * b + K + 1), bank(7 - b, K))
+        scan(v("ls"), v("hw"), v("lm", 1, 3 * P, 3), A.mult, A.add)
         ts(v("sel", 1, 36, 2), v("ls", 15, P, 16), 2.0, A.mult, power, A.is_gt)
         scan(v("sel", 72, 108), v("sel", 0, 36), v("sel", 36, 72), A.mult, A.add)
         cp(v("cw", LB, LB + 18), v("sel", 73, 108, 2))
         for k in range(NB):
             if k:
                 preds(k)
-            w = 2 * (E + B * k)
-            scan(v("uu", w, w + 96), v("lm", 96 * k, 96 * k + 96), v("ba", 96 * k, 96 * k + 96), A.max, A.min)
-        turn(v("tt", 0, 192), v("uu", 65, 449, 2))
-        turn(v("tt", 288, 480), v("uu", 33, 417, 2))
-        turn(v("tt", 192, 288), v("uu", 449, 640, 2))
-        turn(v("tt", 480, 608), v("uu", 417, 672, 2))
+            w = 3 * (E + B * k)
+            scan(v("uu", w, w + 144), v("lm", 144 * k, 144 * k + 144), v("ba", 144 * k, 144 * k + 144), A.max, A.min)
+        for o, a, z in ((0, E, 224), (288, 16, 208), (192, 224, C), (480, 208, 336)):
+            turn(v("tt", o, o + z - a), v("uu", 3 * a + 2, 3 * z, 3))
         lin(v("qa"), (v("tt"), v("cu", LQ, LQ + 7)), 511.0 / 512, -511.0 / 512)
         tt(v("val", 0, 112), (v("tt"), v("cu", LP, LP + 7)), v("qa"), A.add)
-        scan(v("so"), v("sd"), v("val", 0, 112), A.add, A.max)
-        ts(v("cw", LD, LD + 18), v("so", 9, 112, 6), 32768.0, A.mult, float(E + 4 * B), A.add)
+        scan(v("dd"), v("sd"), v("val", 0, 112), A.add, A.max)
+        ts(v("cw", LD, LD + 18), v("dd", 9, 112, 6), 32768.0, A.mult, float(E + 4 * B), A.add)
         part[0] = "side%d" % t
         ts(v("llu"), (v("val"), v("cu", LL, LL + 7)), 32768.0, A.mult)
         o = 0
         for l, (a, z) in enumerate(span):
             n = 16 * (z - a)
-            act(v("js", o, o + n), (v("oh") if l else v("oz", 0, 33), v("llu", a, z)), F.Copy, acc=col("pk", l))
+            act(v("js", o, o + n), (v("oh" if l else "oz", 0, 50), v("llu", a, z)), F.Copy, acc=col("pk", l))
             o += n
-        tt(v("ni"), (v("pk", 0, 6), v("cu", LK, LK + 2)), v("scl"), A.mult)
-        ts(col("ni", 0), col("ni", 0), 4095, A.bitwise_and)
-        ts(v("ni", 2, 17), v("ni", 2, 17), 255, A.bitwise_and)
-        cp(v("cw", LN, LN + 17), v("ni", 0, 17))
-        nb = v("nb", 1, K + 1)
-        move(nb, (v("tabn"), v("cw", LN, LN + 17)))
+        tt(v("ni"), (v("pk", 0, 6), v("cu", LK, LK + 3)), v("scl"), A.mult)
+        scan(v("un", 48, 82), v("un", 0, 34), v("ni", 0, 34), A.mult, A.add)
+        ts(v("cw", LN, LN + 17), v("un", 49, 82, 2), 114.0, A.add)
+        nb, counts = v("nb", 1, K + 1), (v("it"), v("cw", LN, LN + 17))
+        move(nb, counts)
         for k in range(2):
-            act(v("jb", K * k, K * k + K), nb, F.Sign, bias=col("cf", 10 + k), scale=-1.0, acc=col("sm2", k))
+            act(v("jb", K * k, K * k + K), counts, F.Sign, bias=col("cf", 10 + k), scale=-1.0, acc=col("sm2", k))
         ts(v("cw", LF, LF + 2), v("sm2", 0, 2), float(K - 2 * E), A.is_le)
         tau = col("sm2", 2)
         act(v("jb", 544, 576), (v("j16", 0, 16), v("cw", LF, LF + 2)), F.Copy, acc=tau)
@@ -579,70 +624,69 @@ def rank_program(g, core, T, topo):
         for k in range(2):
             act(v("jb", 576 + K * k, 576 + K * k + K), v("cs", 289, 289 + K), F.Sign, bias=col("sm2", 6 + k), scale=-1.0,
                 acc=col("sm2", 4 + k))
-            ts(v("cw", LC + k, LC + 8, 2), v("cf", 122, 126), col("sm2", 4 + k), A.add, 0.5, A.mult)
-        tt(v("key", 0, 32), (v("nb", 0, K + 1), v("cw", LC, LC + 2)), v("jt"), A.subtract)
-        tt(v("key", 32, 64), v("key", 0, 32), v("dg"), A.mult)
-        scan(v("key", 64, 96), v("nd"), v("key", 32, 64), A.mult, A.add)
+            if t not in EARLY:
+                ts(v("cw", LC + k, LC + 8, 2), v("cf", 122, 126), col("sm2", 4 + k), A.add, 0.5, A.mult)
+        if t in EARLY:
+            ts(v("hs", 16 * t, 16 * t + 2), v("sm2", 4, 6), K + 2.0, A.add, 0.5, A.mult)
+            post()
+        cand = (v("nb", 0, K + 1), v("hs", 16 * t, 16 * t + 2) if t in EARLY else v("cw", LC, LC + 2))
+        tt(v("key", 64, 96), cand, v("dg"), A.mult)
+        scan(v("key", 96, 128), v("nd"), v("key", 64, 96), A.mult, A.add)
         for k in range(2):
-            act(v("jb", 1696 + 32 * k, 1728 + 32 * k), v("key", 0, 32), F.Sign, bias=col("key", 79 + 16 * k), scale=-1.0,
-                acc=col("sm2", 10 + k))
-            ts(v("cw", LR + k, LR + 8, 2), v("cf", 4, 8), col("sm2", 10 + k), A.subtract, col("sm2", 10 + k), A.subtract)
-        move(v("fc"), (v("xp", 4 * t * PL, 4 * (t + 1) * PL), v("cw", LC, LC + 8)))
-        lr = v("cw", LR, LR + 8)
-        op({"v": (lambda lr=lr: V.tensor_copy(T.ft[:, 0:128].indirect(ap(lr)), T.fc[:]), 0.05 + 128 * 3.8 * CY)},
-           [lr, v("fc")], [v("ft", 0, 128)])
-        own = E * R + 128 * t
-        qz("f", own, own + 128, v("ft", 0, 512))
-        sent = []
-        for name in ("qf", "sf"):
-            sent = [op({"g": (lambda name=name, t=t, own=own: hand(g, T, topo, core, way_out[1], name, t, own), 0.3)},
-                       [v(name, own, own + E)], [], kind="r", after=sent)]
-            op({"n" + name: (None, 0.0)}, [], [v(name, landing(t), landing(t) + E)], kind="n", after=sent,
-               sem=("%s%d" % (name, t), arrive))
+            tt(v("key", 32 * k, 32 * k + 32), cand, v("jt", 32 * k, 32 * k + 32), A.subtract)
+            act(v("jb", 1696 + 32 * k, 1728 + 32 * k), v("key", 32 * k, 32 * k + 32), F.Sign, bias=col("key", 111 + 16 * k),
+                scale=-1.0, acc=col("sm2", 10 + k))
+            if t in EARLY:
+                ts(v("hs", 16 * t + 8 + k, 16 * t + 12, 2), v("cf", 104, 106), col("sm2", 10 + k), A.subtract, 0.5, A.mult)
+            else:
+                ts(v("cw", LR + k, LR + 8, 2), v("cf", 4, 8), col("sm2", 10 + k), A.subtract, col("sm2", 10 + k), A.subtract)
+        if t in EARLY:
+            post()
+        else:
+            move(v("fc"), (v("xp", 4 * t * PL, 4 * (t + 1) * PL), v("cw", LC, LC + 8)))
+            scatter(v("xi", 0, 128), v("cw", LR, LR + 8), v("fc"))
+            qz("f", feed_at(t)[1], feed_at(t)[1] + 128, v("xi", 0, 512))
+            post()
+            post()
         part[0] = "layer%d" % t
         for b in range(4):
-            cut, win = (P * b, P * b + P), plane(t, b, 0, K + 1)
-            move(v("g1", *cut), (win, v("cu", LA, LA + 18)))
-            tt(v("g2", *cut), (win, v("cw", LB, LB + 18)), v("g1", *cut), A.max)
-        for a, z in (HALF if t in HL else FULL):
+            cut = (P * b, P * b + P)
+            move(v("g1", *cut), (plane(t, b), v("cu", LA, LA + 18)))
+            tt(v("g2", *cut), (plane(t, b), v("cw", LB, LB + 18)), v("g1", *cut), A.max)
+        for a, z in HALF:
             for b in range(4):
-                win = plane(t, b, 0, 1 + E + B * ((z - 1) // B))
-                tt(v("mt", 4 * a + b, 4 * z, 4), (win, v("cw", LD + a // 16, LD + z // 16)), v("g2", P * b + a, P * b + z), A.add)
+                tt(v("mt", 4 * a + b, 4 * z, 4), (plane(t, b), v("cw", LD + a // 16, LD + z // 16)), v("g2", P * b + a, P * b + z), A.add)
             qz("m", a, z, v("mt", 4 * a, 4 * z))
             for b in range(4):
-                mine, rr = v("xi", 4 * (E + a) + b, 4 * (E + z), 4), v("rr", 4 * a + b, 4 * z, 4)
+                mine, rr = state(E + a, E + z, b), v("rr", 4 * a + b, 4 * z, 4)
                 mm(b + 1, "w", 128 * b, "m", a, z - a)
                 act(rr, bank(b + 1, z - a), F.Relu, scale=0.015625)
-                if t not in BYDMA:
-                    tt(mine, rr, mine, A.add)
-            if t in BYDMA:
-                x, rr = v("xi", 4 * (E + a), 4 * (E + z)), v("rr", 4 * a, 4 * z)
-                op({"g": (lambda x=x, rr=rr: g.dma_start(ap(x), ap(rr), accum_op=A.add), DD)}, [rr, x], [x],
-                   lat=DL + DS * (z - a) / P, kind="d")
+                tt(mine, rr, mine, A.add)
         if not last:
-            for a, z in (HALF if t in HP else FULL):
-                z = PL - E - 1 if z == P else z
-                for b in range(4):
-                    move(plane(t + 1, b, E + 1 + a, E + 1 + z), v("xi", 4 * (E + a) + b, 4 * (E + z), 4), True)
+            for b in range(4):
+                move(plane(t + 1, b, E + 1, PL), state(E, PL - 1, b), True)
         part[0] = "ent%d" % t
+        if t in EARLY:
+            for b in range(4):
+                move(v("fc", E * b, E * b + E), (v("dp", PL * b, PL * b + K + 1), v("hl", 16 * t, 16 * t + 2)))
+            for o in (0, 64):
+                scatter(v("dor", o, o + 64), v("hl", 16 * t + 8, 16 * t + 12), v("fc", o, o + 64))
         for b in range(4):
-            mm(7 - b, "i", 128 * b, "f", landing(t), 128)
-            tt(v("xi", b, 4 * E, 4) if last else plane(t + 1, b, 1, E + 1), bank(7 - b, E), plane(t, b, 1, E + 1), A.max)
+            if t not in EARLY:
+                mm(7 - b, "i", 128 * b, "f", feed_at(t)[0], 128)
+            came = v("dor", E * b, E * b + E) if t in EARLY else bank(7 - b, E)
+            tt(state(0, E, b) if last else plane(t + 1, b, 1, E + 1), came, plane(t, b, 1, E + 1), A.max)
+            if t + 1 in EARLY:
+                move(state(0, E, b), plane(t + 1, b, 1, E + 1), True)
     part[0] = "out"
     move(v("odb"), (v("it", 0, K + 1), v("cw", LD, LD + 18)))
     dma("y", T.od[:], T.odb[0:128:16, :], [v("odb")], [])
-    qz("x", 0, P, nodes)
-    mm(0, "v", 0, "x", 0, P)
-    move(v("ys", E, C), bank(0, P))
-    dma("y", T.oc[:, 4 * E:4 * C], T.qx[:].bitcast(u8), [v("qx")], [])
-    dma("y", T.y[:, E:C], T.ys[:, E:C], [v("ys", E, C)], [])
+    for a, z, k in ((E, mid, 0), (mid, C, 1), (-XO, E, 6)):
+        mm(k, "v", 0, "x", pack(R, a, z), z - a)
+        lo, o = max(a, 0), XW * R + XO
+        move(v("ys", lo, z), v("ps", 512 * k + lo - a, 512 * k + z - a))
+        dma("ys", T.oc[:, 4 * lo:4 * z], T.qx[:, o + lo:o + z].bitcast(u8), [v("qx", o + lo, o + z)], [])
+        dma("ys", T.y[:, lo:z], T.ys[:, lo:z], [v("ys", lo, z)], [])
     for k in range(4):
-        dma("ys", T.osc[4 * k:4 * k + 4, E:C], T.sx[32 * k:32 * k + 4, :], [v("sx")], [])
-    qz("e", 0, 128, v("xi", 0, 512))
-    mm(6, "v", 0, "e", 0, 128)
-    move(v("ys", 0, E), bank(6, E))
-    dma("ys", T.oc[:, 0:4 * E], T.qe[:, 0:E].bitcast(u8), [v("qe")], [])
-    for k in range(4):
-        dma("ys", T.osc[4 * k:4 * k + 4, 0:E], T.se[32 * k:32 * k + 4, 0:E], [v("se")], [])
-    dma("ys", T.y[:, 0:E], T.ys[:, 0:E], [v("ys", 0, E)], [])
+        dma("ys", T.osc[4 * k:4 * k + 4, :], T.sx[32 * k:32 * k + 4, o:o + C], [v("sx", o, o + C)], [])
     emit(g, T, ops)

import math
import numpy as np
from concourse.mybir import dt, AluOpType as A, ActivationFunctionType as F

C, E, B, NB, P, R = 320, 32, 48, 6, 288, 3
K = C - B
PL = 288
XO = 96
XF = 162
XW = XO + C
X4, S_, BF, F32, U8 = "float8_e4m3fn_x4", "sbuf", "bfloat16", "float32", "uint8"
SCRATCH = {"ps": ("psum", [128, 4096], F32)}
for _n, _w in (("xi", 4 * (XF + C)), ("xp", 12 * PL), ("ut", 512), ("vt", 512), ("et", 520), ("uu", 1008), ("ba", 3 * P),
               ("lm", 3 * P), ("hw", P), ("j16", P), ("ls", P), ("tt", 624), ("jb", 1792), ("nb", 288), ("fl", 2 * K + 2),
               ("cs", 576), ("fc", 128), ("dp", 4 * PL), ("dor", 128), ("g1", 4 * P), ("g2", 4 * P), ("mt", 4 * P)):
    SCRATCH[_n] = (S_, [128, _w], BF)
for _n, _w in (("cf", 128), ("dg", 32), ("nd", 32), ("it", 336), ("oh", 64), ("oz", 64), ("scl", 48), ("un", 96), ("jt", 64),
               ("sel", 108), ("lp", 84), ("qa", 112), ("val", 120), ("sd", 112), ("dd", 112), ("js", 1168), ("pk", 8), ("sm2", 32),
               ("key", 128), ("rr", 4 * P), ("ys", C), ("odb", P)):
    SCRATCH[_n] = (S_, [128, _w], F32)
for _n, _w in (("pab", 36), ("ci", 64), ("ni", 48)):
    SCRATCH[_n] = (S_, [128, _w], "int32")
for _n, _w in (("cu", 160), ("cw", 80), ("llu", 112), ("hs", 16 * R), ("hl", 16 * R)):
    SCRATCH[_n] = (S_, [128, _w], "uint16")
for _n, _w in (("u", 128), ("v", 128), ("up", 128 * R), ("w", 512), ("x", XW * (R + 1)), ("m", P), ("i", 512), ("l", K * R),
               ("f", E * R + 128 * R)):
    SCRATCH["q" + _n] = (S_, [128, _w], X4)
    SCRATCH["s" + _n] = (S_, [128, _w], U8)
NDMA = 24
SEMAPHORES = ["cv", "cs", "ct", "cg", "sent"] + ["got%d" % k for k in range(4 * R)] + ["dm%d" % i for i in range(NDMA)]
EARLY = (0, 2)
HALF = ((0, 160), (160, P))
CY = 0.83e-3
CASES = ((0.015, 1.15, 0.16, 3.0), (0.0, 1.0, 0.2, 3.0), (0.04, 1.4, 0.12, 4.0))
FIRST = 1.5
SHAKES, TRIES, SEED = 10000, 40000, 99
PLAN = {}


def route(T, topo, r, way):
    src, dst = T.cores[r], T.cores[(r + 1) % len(T.cores)]
    if topo.may_write(src, dst):
        return [src, dst]
    able = [c for c in topo.cores_of(src) if c != src and topo.may_write(c, dst)]
    able.sort(key=lambda c: topo.die(c) != topo.die(src))
    return [src, able[way % len(able)], dst]


def feed_at(t):
    late = [k for k in range(R) if k not in EARLY]
    return E * (len(late) - 1 - late.index(t)), E * len(late) + 128 * late.index(t)


def letters():
    got = []
    for t in range(R):
        if t in EARLY:
            got += [(0, "qx", XW * t + XO, "ql", K * t, K), (1, "sx", XW * t + XO, "sl", K * t, K),
                    (0, "hs", 16 * t, "hl", 16 * t, 2), (1, "hs", 16 * t + 8, "hl", 16 * t + 8, 4)]
        else:
            got += [(k, n, feed_at(t)[1], n, feed_at(t)[0], E) for k, n in enumerate(("qf", "sf"))]
    return got


def hand(g, T, topo, src, dst, k, first):
    _way, a, a0, z, z0, n = letters()[k]
    rid, pid = topo.addr(dst, src)
    out, in_ = T[z][:, z0:z0 + n], T[a][:, a0:a0 + n] if first else T[z][:, z0:z0 + n]
    if SCRATCH[z][2] == X4:
        out, in_ = out.bitcast(dt.uint8), in_.bitcast(dt.uint8)
    g.remote_dma(out, in_, T.sem["got%d" % k], T.sem.sent, pid, rid, topo.mask(src, dst))
    return len(topo.engines(src, dst))


def relay(g, T, topo, src, me, dst, ways):
    n, e = 0, len(topo.engines(src, me))
    for k, letter in enumerate(letters()):
        if letter[0] in ways:
            g.wait_ge(T.sem["got%d" % k], e)
            n += hand(g, T, topo, me, dst, k, False)
    g.wait_ge(T.sem.sent, n)


def plan(ops):
    n = len(ops)
    dep = [sorted(o["dep"]) for o in ops]
    succ = [[] for _ in ops]
    for i in range(n):
        for d in dep[i]:
            succ[d].append(i)
    cases = []
    for add, f, w, net in CASES:
        cases.append(([{k: d * f + add if o["kind"] == "c" else d for k, (_fn, d) in o["alt"].items()} for o in ops],
                      [o["lat"] + (w if o["kind"] == "c" else net if o["kind"] == "n" else 0.0) for o in ops]))
    dur, lat = cases[0]
    names = sorted(set(k for d in dur for k in d))
    can = [[(k, du, du * (1.5 if k == "v" else 1.0)) for k, du in d.items()] for d in dur]
    seed = [SEED]

    def rnd():
        seed[0] = (seed[0] * 6364136223846793005 + 1442695040888963407) % (1 << 64)
        return (seed[0] >> 33) / float(1 << 31)

    def lay(key, back):
        pre, post = (succ, dep) if back else (dep, succ)
        key = list(key)
        for i in (range(n) if back else range(n - 1, -1, -1)):
            for s in post[i]:
                if key[s] >= key[i]:
                    key[i] = key[s] + 1e-6
        st, en, over, q, line = [0.0] * n, [0.0] * n, [0.0] * n, [None] * n, {k: ([], []) for k in names}
        for i in sorted(range(n), key=lambda j: -key[j]):
            r = 0.0
            for d in pre[i]:
                if over[d] > r:
                    r = over[d]
            if back:
                r += lat[i]
            best = 1e9
            for k, du, pen in can[i]:
                a, z = line[k]
                j = m = len(a)
                s = r
                while j and z[j - 1] > r:
                    j -= 1
                while j < m and a[j] < s + du - 1e-9:
                    if z[j] > s:
                        s = z[j]
                    j += 1
                if s + pen < best:
                    best, bk, bs, bj, bd = s + pen, k, s, j, du
            a, z = line[bk]
            a.insert(bj, bs)
            z.insert(bj, bs + bd)
            st[i], en[i], q[i] = bs, bs + bd, bk
            over[i] = bs + bd if back else bs + bd + lat[i]
        return max(en[i] + lat[i] for i in range(n)), st, en, q

    def both(key):
        first = lay(key, False)
        again = lay(lay([first[2][i] + lat[i] for i in range(n)], True)[2], False)
        return min(first, again, key=lambda x: x[0])

    way = [0.0] * n
    for i in range(n - 1, -1, -1):
        way[i] = min(dur[i].values()) + lat[i] + max([way[s] for s in succ[i]] + [0.0])
    best = cur = both(way)
    parts = sorted(set(o["part"] for o in ops))
    for it in range(SHAKES):
        mid, wide = rnd() * best[0], (2, 4, 8)[int(rnd() * 3)]
        if rnd() < 0.3:
            one, by = parts[int(rnd() * len(parts))], 7.0 * (rnd() - 0.5)
            key = [-s + (by if o["part"] == one and abs(s - mid) < 2 * wide else 0.0) for s, o in zip(cur[1], ops)]
        else:
            key = [-s + (3.5 * (rnd() - 0.5) if abs(s - mid) < wide else 0.0) for s in cur[1]]
        got = both(key)
        if got[0] <= cur[0] - 0.06 * (1 - it / SHAKES) * math.log(rnd() + 1e-9):
            cur = got
            if got[0] < best[0]:
                best = got
    q = best[3]
    order = sorted(range(n), key=lambda i: (best[1][i], i))
    either = [i for i in range(n) if len(dur[i]) > 1]

    def run(od):
        total = 0.0
        for du, la in cases[::-1]:
            free, done = {}, [0.0] * n
            for i in od:
                k = q[i]
                s = free.get(k, 0.0)
                for d in dep[i]:
                    if done[d] > s:
                        s = done[d]
                s += du[i][k]
                free[k] = s
                done[i] = s + la[i]
            total += max(done) + 0.02 * sum(done) / n
        return total / len(cases), done

    cur, done = run(order)
    best, bo, bq = cur, list(order), list(q)
    for it in range(TRIES):
        if it % 1000 == 0:
            order = sorted(order, key=lambda i: done[i] - lat[i] - dur[i][q[i]])
            cur, done = run(order)
        flip, new = None, order
        if rnd() < 0.06:
            flip = either[int(rnd() * len(either))]
            was = q[flip]
            other = [k for k in dur[flip] if k != was]
            q[flip] = other[int(rnd() * len(other))]
        else:
            a = int(rnd() * n)
            i = order[a]
            step = 1 if rnd() < 0.5 else -1
            stop = succ[i] if step > 0 else dep[i]
            b, more = a, 1 + int(rnd() ** 3 * 12)
            while more and 0 <= b + step < n and order[b + step] not in stop:
                b += step
                if q[order[b]] == q[i]:
                    more -= 1
            if b == a:
                continue
            new = order[:a] + order[a + 1:]
            new.insert(b, i)
        got, dn = run(new)
        if got <= cur or rnd() < math.exp((cur - got) / (0.03 * (1 - it / TRIES) + 0.003)):
            cur, order, done = got, new, dn
            if got < best:
                best, bo, bq = got, list(new), list(q)
        elif flip is not None:
            q[flip] = was
    q[:] = bq
    done = run(bo)[1]
    return best, bo, [done[i] - lat[i] - dur[i][q[i]] for i in range(n)], bq


def depend(ops):
    wrote = {n: np.full(v[1][1], -1) for n, v in SCRATCH.items()}
    read = {n: [] for n in SCRATCH}
    for i, o in enumerate(ops):
        dep = set(o["after"])
        rd = [x for x in o["r"] if x[0] != "ps"]
        wr = [x for x in o["w"] if x[0] != "ps"]
        wr += [("ps", x[1] // 512 * 512, x[1] // 512 * 512 + 512, 1) for x in o["r"] + o["w"] if x[0] == "ps"]
        for n, a, z, s in rd + wr:
            dep.update(int(k) for k in set(wrote[n][a:z:s].tolist()) if k >= 0)
        for n, a, z, s in wr:
            for j, mask in read[n]:
                if mask[a:z:s].any():
                    dep.add(j)
                    mask[a:z:s] = False
            wrote[n][a:z:s] = i
        for n, a, z, s in rd:
            mask = np.zeros(len(wrote[n]), bool)
            mask[a:z:s] = True
            read[n].append((i, mask))
        dep.discard(i)
        o["dep"] = dep


def emit(g, T, ops):
    if "p" not in PLAN:
        depend(ops)
        PLAN["p"] = plan(ops)
        PLAN["dep"] = [o["dep"] for o in ops]
    _end, order, _at, where = PLAN["p"]
    place = {i: k for k, i in enumerate(order)}
    queue = {"v": g.vector, "s": g.scalar, "t": g.tensor, "g": g, "y": g.sync}
    count, known, ndma = {}, {q: {} for q in queue}, 0
    for i in order:
        o = ops[i]
        q = where[i]
        if o["kind"] == "n":
            o["sig"], o["clock"] = o["sem"], {}
            count[o["sem"][0]] = o["sem"][1]
            continue
        kn = known[q]
        for d in sorted(PLAN["dep"][i], key=lambda j: -place[j]):
            p = ops[d]
            if p["sig"] is None:
                continue
            name, val = p["sig"]
            if kn.get(name, 0) < val:
                queue[q].wait_ge(T.sem[name], val)
                kn[name] = val
                for a, b in p["clock"].items():
                    kn[a] = max(kn.get(a, 0), b)
        ins = o["alt"][q][0]()
        o["clock"] = dict(kn)
        if o["kind"] == "c":
            name = "c" + q
            count[name] = count.get(name, 0) + 1
            ins.then_inc(T.sem[name], 1)
            o["sig"] = (name, count[name])
        elif o["kind"] == "d":
            name = "dm%d" % ndma
            ndma += 1
            count[name] = 16
            ins.then_inc(T.sem[name], 16)
            o["sig"] = (name, 16)
        else:
            count["sent"] = count.get("sent", 0) + ins
            o["sig"] = None
    seen = {}
    for q in known:
        for a, b in known[q].items():
            seen[a] = max(seen.get(a, 0), b)
    for name, val in count.items():
        if seen.get(name, 0) < val:
            g.wait_ge(T.sem[name], val)


def rank_program(g, core, T, topo):
    rank = T.rank_of(core)
    n_ranks = len(T.cores)
    if rank is None:
        for r in range(n_ranks):
            ways = [k for k in range(2) if route(T, topo, r, k)[1:-1] == [core]]
            if ways:
                relay(g, T, topo, T.cores[r], core, T.cores[(r + 1) % n_ranks], ways)
        return
    to = [route(T, topo, rank, k)[1] for k in range(2)]
    arrive = [len(topo.engines(route(T, topo, (rank - 1) % n_ranks, k)[-2], core)) for k in range(2)]
    V, S, ops, part = g.vector, g.scalar, [], ["head"]

    def v(name, a=0, z=None, s=1):
        return (name, a, SCRATCH[name][1][1] if z is None else z, s)

    def col(name, a):
        return (name, a, a + 1, 1)

    def ap(x, cast=None):
        if not isinstance(x, tuple):
            return x
        if len(x) == 2:
            return ap(x[0], cast).indirect(ap(x[1]))
        y = T[x[0]][:, x[1]:x[2]:x[3]] if x[3] != 1 else T[x[0]][:, x[1]:x[2]]
        return y.bitcast(cast) if cast else y

    def views(*xs):
        got = []
        for x in xs:
            if isinstance(x, tuple):
                got += list(x) if len(x) == 2 else [x]
        return got

    def size(x):
        return 16 * size(x[1]) if len(x) == 2 else len(range(x[1], x[2], x[3]))

    def narrow(*xs):
        return all(SCRATCH[x[0]][2] in (BF, "uint16") for x in xs)

    def op(alt, r, w, lat=0.0, kind="c", after=(), sem=None):
        ops.append({"alt": alt, "r": r, "w": w, "lat": lat, "kind": kind, "after": list(after), "sem": sem, "part": part[0]})
        return len(ops) - 1

    def vcost(out, a, *more, c=None):
        if len(a) == 2:
            return 0.05 + size(a) * 1.56 * CY
        return max(64, size(a) * (c or (0.5 if narrow(out, a, *more) else 1.0))) * CY

    def scost(a):
        return 0.065 + size(a) * (1.56 if len(a) == 2 else 1.0) * CY

    def ts(out, a, s1, o0, s2=None, o1=None):
        if o1 is None:
            fn = lambda: V.tensor_scalar(ap(out), ap(a), ap(s1), None, o0)
        else:
            fn = lambda: V.tensor_scalar(ap(out), ap(a), ap(s1), ap(s2), o0, o1)
        return op({"v": (fn, vcost(out, a))}, views(a, s1, s2), [out])

    def tt(out, a, b, o):
        c = 1.0 if "ps" in (a[0], b[0]) else 2.0
        return op({"v": (lambda: V.tensor_tensor(ap(out), ap(a), ap(b), o), vcost(out, a, c=c))}, views(a, b), [out])

    def cp(out, a):
        return op({"v": (lambda: V.tensor_copy(ap(out), ap(a)), vcost(out, a))}, views(a), [out])

    def scan(out, a, b, o0, o1, first=0.0):
        return op({"v": (lambda: V.tensor_tensor_scan(ap(out), ap(a), ap(b), ap(first), o0, o1), vcost(out, a, b))},
                  views(a, b, first), [out])

    def turn(out, a):
        return op({"v": (lambda: V.transpose(ap(out), ap(a)), vcost(out, a))}, [a], [out])

    def qz(name, a, z, tile):
        out, sc = v("q" + name, a, z), v("s" + name, a, z)
        return op({"v": (lambda: V.quantize_mx(ap(out), ap(sc), ap(tile)), 0.012 + size(tile) * 0.22e-3)}, [tile], [out, sc])

    def act(out, a, f, bias=0.0, scale=1.0, acc=None):
        fn = lambda: S.activation(ap(out), ap(a), f, bias=ap(bias), scale=ap(scale), accum_out=ap(acc))
        return op({"s": (fn, scost(a) + (0.02 if acc else 0.0))}, views(a, bias, scale), views(out, acc))

    def lin(out, a, scale=1.0, bias=0.0):
        return op({"s": (lambda: S.activation(ap(out), ap(a), F.Identity, bias=ap(bias), scale=ap(scale)), scost(a)),
                   "v": (lambda: V.tensor_scalar(ap(out), ap(a), ap(scale), ap(bias), A.mult, A.add), vcost(out, a))},
                  views(a, scale, bias), [out])

    def move(out, a, pool=False):
        alt = {"s": (lambda: S.activation(ap(out), ap(a), F.Copy), scost(a)), "v": (lambda: V.tensor_copy(ap(out), ap(a)), vcost(out, a))}
        if pool:
            n = size(a)
            alt = {"g": (lambda: g.affine_select(ap(out), ap(a), [[0, n]], A.is_ge, 0.0, 0, 0), 0.17 + 2 * n * CY), **alt}
        return op(alt, views(a), [out])

    def iota(out, pat, base, cm=0):
        if SCRATCH[out[0]][2] == "int32":
            fn = lambda: g.iota(ap(out), pat, base, cm)
        else:
            fn = lambda: g.iota(ap(out), pat, base, cm, allow_small_or_imprecise_dtypes=True)
        return op({"g": (fn, 0.13 + 2 * size(out) * CY)}, [], [out])

    def fill(out, val):
        n = size(out)
        alt = {"v": (lambda: V.memset(ap(out), val), vcost(out, out))}
        if val == int(val):
            alt["g"] = (lambda: g.iota(ap(out), [[0, n]], int(val), 0, allow_small_or_imprecise_dtypes=True), 0.13 + 2 * n * CY)
        if n > 64:
            return op(alt, [], [out])
        some = v("it", 0, n)
        alt["s"] = (lambda: S.activation(ap(out), ap(some), F.Identity, bias=val, scale=0.0), scost(some))
        if val != int(val):
            alt["g"] = (lambda: g.affine_select(ap(out), ap(some), [[0, n]], A.is_gt, val, 0, 0), 0.17 + 2 * n * CY)
        return op(alt, [some], [out])

    def mm(bank, l, la, r, ra, n):
        out = v("ps", 512 * bank, 512 * bank + n)
        ins = [v("q" + l, la, la + 128), v("s" + l, la, la + 128), v("q" + r, ra, ra + n), v("s" + r, ra, ra + n)]
        return op({"t": (lambda: g.tensor.matmul_mx(ap(out), *[ap(x) for x in ins], True, True), 0.03 + n * 0.6e-3)}, ins, [out], lat=0.04)

    def dma(qs, out, a, r, w, lat=2.0, after=()):
        e = {"y": g.sync, "s": g.scalar, "g": g}
        return op({q: (lambda q=q: e[q].dma_start(out, a), 0.1) for q in qs}, r, w, lat=lat, kind="d", after=after)

    def plane(t, b, a=0, z=K + 1):
        o = (4 * t + b) * PL
        return v("xp", o + a, o + z)

    def state(a, z, b=None):
        return v("xi", 4 * (XF + a), 4 * (XF + z)) if b is None else v("xi", 4 * (XF + a) + b, 4 * (XF + z), 4)

    def pack(t, a, z):
        qz("x", XW * t + XO + a, XW * t + XO + z, state(a, z))
        return XW * t + XO + a

    def bank(k, n):
        return v("ps", 512 * k, 512 * k + n)

    def scatter(win, lst, src):
        op({"v": (lambda: V.tensor_copy(ap(win).indirect(ap(lst)), ap(src)), 0.05 + size(src) * 3.8 * CY)}, [lst, src], [win])

    sent = []

    def post():
        k = len(sent)
        way, a, a0, z, z0, n = letters()[k]
        sent.append(op({"g": (lambda: hand(g, T, topo, core, to[way], k, True), 0.3)}, [v(a, a0, a0 + n)], [], kind="r", after=sent[-1:]))
        op({"n%d" % way: (None, 0.0)}, [], [v(z, z0, z0 + n)], kind="n", after=sent[-1:], sem=("got%d" % k, arrive[way]),
           lat=(FIRST if k < 2 else 0.0) + (1.0 if n == K else -0.3 if n < E else 0.0))

    u8 = dt.uint8
    mid = E + HALF[0][1]
    dma("y", ap(state(0, mid)), T.x[:, 0:4 * mid], [], [state(0, mid)], 2.25)
    dma("s", T.ut[:], T.u[:], [], [v("ut")], 2.3)
    first = dma("y", ap(state(mid, C)), T.x[:, 4 * mid:4 * C], [], [state(mid, C)], 2.6)
    dma("y", T.pab[:, 0:18], T.pa[:], [], [v("pab", 0, 18)], 2.4)
    dma("y", T.pab[:, 18:36], T.pb[:], [], [v("pab", 18, 36)], 2.4)
    dma("y", T.qw[:].bitcast(u8), T.wc[:], [], [v("qw")], 3.0, [first])
    dma("y", T.sw[:], T.ws[:], [], [v("sw")], 3.0, [first])
    dma("y", T.vt[:], T.v[:], [], [v("vt")], 3.0, [first])
    lane, grp = col("cf", 0), col("cf", 1)
    iota(col("ci", 0), [[0, 1]], 0, 1)
    iota(v("ci", 8, 32), [[1, R], [16, 8]], 0)
    iota(v("j16", 0, 32), [[0, 2], [1, 16]], 0)
    iota(v("j16", 32, P), [[0, 16], [1, 16]], 0)
    iota(v("it", 0, 64), [[1, 64]], -1)
    iota(v("it", 64, 336), [[1, 272]], 63)
    iota(v("cf", 32, 39), [[16, 7]], -4)
    iota(v("cf", 4, 8), [[1, 4]], 62)
    ts(col("ci", 1), col("ci", 0), 15, A.bitwise_and)
    ts(col("ci", 2), col("ci", 0), 4, A.logical_shift_right)
    cp(v("cf", 0, 2), v("ci", 1, 3))
    cp(v("cu", 0, 24), v("ci", 8, 32))
    ts(v("hw"), v("j16"), lane, A.not_equal, 4.0, A.mult)
    ts(v("dg"), v("j16", 0, 32), lane, A.is_equal)
    lin(v("nd"), v("dg"), -1.0, 1.0)
    scan(v("cf", 64, 80), v("hw", 0, 16), v("dg", 0, 16), A.mult, A.add)
    power = col("cf", 79)
    tt(v("cf", 80, 86), v("dg", 0, 12, 2), v("dg", 1, 12, 2), A.subtract)
    lin(v("cf", 24, 30), v("cf", 80, 86), 1.0 / 64)
    fill(v("uu", 0, 96), 0.0)
    fill(v("uu", 960, 1008), 0.0)
    lin(v("uu", 2, 96, 3), v("it", 2, 34), col("cf", 24), col("dg", 1))
    fill(v("lm", 0, 3 * P, 3), 1.0)
    fill(v("ba", 2, 3 * P, 3), 1.0)
    for k in range(NB - 1):
        lin(v("lm", 144 * k + 2, 144 * k + 144, 3), v("it", 2, 2 + B), col("cf", 25 + k), col("dg", 2 * k + 3))
    fill(v("lm", 3 * (P - B) + 2, 3 * P, 3), 0.0)
    LP, LQ, LL, LK = 24, 32, 40, 142
    ef, ci = v("cf", 40, 47), v("ci", 32, 39)
    lin(ef, v("cf", 32, 39), 1.0, lane)
    ts(ci, ef, 1.0 / 6, A.mult, -0.42, A.add)
    ts(v("ci", 40, 47), ci, grp, A.add)
    ts(v("ci", 48, 55), v("ci", 40, 47), 1, A.bitwise_and)
    lin(v("lp", 0, 28, 4), ef)
    ts(v("lp", 1, 28, 4), ci, 2.0, A.mult)
    ts(v("lp", 2, 28, 4), v("ci", 48, 55), 152.0, A.mult)
    ts(v("cf", 56, 63), ci, 6.34, A.mult, 0.01, A.add)
    tt(v("lp", 3, 28, 4), ef, v("cf", 56, 63), A.is_gt)
    fill(v("lp", 28, 56), 1.0)
    fill(v("lp", 28, 56, 4), 0.0)
    fill(v("lp", 31, 56, 4), 1.0 / 1024)
    scan(v("lp", 56, 84), v("lp", 28, 56), v("lp", 0, 28), A.mult, A.add)
    ts(v("cu", LP, LP + 7), v("lp", 59, 84, 4), 2048.0, A.mult, 608.0, A.min)
    ts(v("cu", LQ, LQ + 7), v("cu", LP, LP + 7), 1.0, A.add)
    fill(v("tt", 608, 624), 0.0)
    fill(v("sd", 0, 56), -B / 32768.0)
    fill(v("sd", 56, 112), -B / 32768.0)
    fill(v("sd", 4, 112, 6), -4.0)
    fill(v("sd", 5, 112, 6), -E / 32768.0)
    span = [(0, 19), (32, 48), (48, 61), (64, 74), (80, 87), (96, 100)]
    iota(v("cf", 112, 114), [[96, 2]], 4)
    iota(v("cf", 114, 119), [[19, 5]], 23)
    lin(col("cf", 120), lane, 6.0)
    ts(v("cu", LL, LL + 7), v("cf", 112, 119), col("cf", 120), A.add, 112.0, A.min)
    fill(v("val", 112, 120), 49 / 32768.0)
    fill(col("oh", 0), 0.0)
    fill(v("oh", 49, 64), -7.0 * 65793)
    fill(v("oz", 0, 49), 0.0)
    fill(v("oz", 49, 64), -7.0 * 4097)
    for f in range(3):
        lin(v("oh", 1 + 16 * f, 17 + 16 * f), v("dg", 0, 16), 256.0 ** f)
    for f in range(2):
        lin(v("oz", 1 + 16 * f, 17 + 16 * f), v("dg", 0, 16), 4096.0 ** f)
    ts(col("ci", 5), lane, 1.0 / 6, A.mult, -0.09, A.add)
    ts(col("ci", 6), lane, 1.0 / 6, A.mult, 16.0 / 6 - 0.09, A.add)
    iota(col("ci", 7), [[0, 1]], 5)
    cp(v("cu", LK, LK + 3), v("ci", 5, 8))
    fill(v("scl"), 0.0)
    fill(v("scl", 0, 4, 3), 1.0 / 4096)
    fill(col("scl", 1), 1.0)
    fill(v("scl", 5, 34, 6), 1.0)
    fill(v("scl", 4, 34, 3), 1.0 / 256)
    fill(v("scl", 6, 34, 3), 1.0 / 65536)
    fill(v("scl", 8, 34, 6), 0.0)
    fill(v("un", 0, 34), -256.0)
    fill(v("un", 0, 34, 2), 0.0)
    fill(col("un", 1), -4096.0)
    for k in range(2):
        lin(col("cf", 10 + k), lane, 1.0, 0.5 + 16 * k)
        lin(col("cf", 2 + k), lane, -1.0 / 64, -k / 4.0)
        lin(v("jt", 32 * k, 32 * k + 32), v("it", 1, 33), 1.0 / 64, col("cf", 2 + k))
    lin(v("cf", 8, 10), v("cf", 10, 12), 1.0, -float(E))
    iota(v("cf", 122, 126), [[2 * PL, 4]], K + 2)
    iota(v("cf", 104, 106), [[2 * E, 2]], E - 1)
    fill(v("dp", 0, 4 * PL, PL), 0.0)
    fill(col("fl", K), -float(E))
    fill(col("cs", 0), 0.0)
    fill(col("nb", 0), 0.0)
    fill(v("xp", 0, 12 * PL, PL), 0.0)
    fill(v("sel", 0, 36, 2), 0.0)
    fill(state(-XF, 0), 0.0)
    op({"g": (lambda: g.affine_select(T.et[:], T.xi[:, 128:648], [[1, 520]], A.not_equal, 1.0, -3, -4), 0.17 + 1040 * CY)},
       [v("xi", 128, 648)], [v("et")])
    for b in range(4):
        qz("i", 128 * b, 128 * b + 128, v("et", 3 - b, 515 - b))
    LA, LA0, LB0, LA1, LB1 = 50, 68, 86, 105, 123
    LB, LD, LN, LF, LC, LR = 0, 18, 36, 54, 56, 64
    pa, pb = v("pab", 0, 18), v("pab", 18, 36)
    ts(v("cu", LA, LA + 18), pa, 1.0, A.add)
    for at in (LA0, LA1):
        ts(v("cu", at, at + 36), v("pab"), 3.0, A.mult, 2.0, A.add)
    tt(v("sel", 36, 72, 2), pa, pb, A.subtract)
    ts(v("sel", 37, 72, 2), pb, 1.0, A.add)

    def preds(k):
        win, x = v("uu", 0, 3 * (E + B * k)), k % 2
        la, lb = (LA1 if x else LA0) + 3 * k, (LB1 if x else LB0) + 3 * k
        move(v("ba", 144 * k, 144 * k + 144, 3), (win, v("cu", lb, lb + 3)))
        move(v("ba", 144 * k + 1, 144 * k + 144, 3), (win, v("cu", la, la + 3)))

    preds(0)
    qz("u", 0, 128, v("ut"))
    qz("v", 0, 128, v("vt"))
    for a, z in ((0, 1), (1, R)):
        out, src = v("qup", 128 * a, 128 * z), (v("qu"), v("cu", 8 * a, 8 * z))
        op({"v": (lambda out=out, src=src: V.tensor_copy(ap(out, dt.uint32), ap(src, dt.uint32)), vcost(out, src))}, views(src), [out])
        move(v("sup", 128 * a, 128 * z), (v("su"), src[1]))
    for b in range(4):
        move(plane(0, b, 1, PL), state(0, PL - 1, b), True)
    for t in range(R):
        last = t == R - 1
        part[0] = "dom%d" % t
        for a, z in HALF:
            mm(0, "up", 128 * t, "x", pack(t, E + a, E + z), z - a)
            act(v("lm", 3 * a + 1, 3 * z, 3), bank(0, z - a), F.Sign, scale=-1.0)
        if t in EARLY:
            pack(t, -XO, E)
            post()
            post()
            for b in range(4):
                mm(7 - b, "i", 128 * b, "l", K * t, K)
                move(v("dp", PL * b + 1, PL * b + K + 1), bank(7 - b, K))
        scan(v("ls"), v("hw"), v("lm", 1, 3 * P, 3), A.mult, A.add)
        ts(v("sel", 1, 36, 2), v("ls", 15, P, 16), 2.0, A.mult, power, A.is_gt)
        scan(v("sel", 72, 108), v("sel", 0, 36), v("sel", 36, 72), A.mult, A.add)
        cp(v("cw", LB, LB + 18), v("sel", 73, 108, 2))
        for k in range(NB):
            if k:
                preds(k)
            w = 3 * (E + B * k)
            scan(v("uu", w, w + 144), v("lm", 144 * k, 144 * k + 144), v("ba", 144 * k, 144 * k + 144), A.max, A.min)
        for o, a, z in ((0, E, 224), (288, 16, 208), (192, 224, C), (480, 208, 336)):
            turn(v("tt", o, o + z - a), v("uu", 3 * a + 2, 3 * z, 3))
        lin(v("qa"), (v("tt"), v("cu", LQ, LQ + 7)), 511.0 / 512, -511.0 / 512)
        tt(v("val", 0, 112), (v("tt"), v("cu", LP, LP + 7)), v("qa"), A.add)
        scan(v("dd"), v("sd"), v("val", 0, 112), A.add, A.max)
        ts(v("cw", LD, LD + 18), v("dd", 9, 112, 6), 32768.0, A.mult, float(E + 4 * B), A.add)
        part[0] = "side%d" % t
        ts(v("llu"), (v("val"), v("cu", LL, LL + 7)), 32768.0, A.mult)
        o = 0
        for l, (a, z) in enumerate(span):
            n = 16 * (z - a)
            act(v("js", o, o + n), (v("oh" if l else "oz", 0, 50), v("llu", a, z)), F.Copy, acc=col("pk", l))
            o += n
        tt(v("ni"), (v("pk", 0, 6), v("cu", LK, LK + 3)), v("scl"), A.mult)
        scan(v("un", 48, 82), v("un", 0, 34), v("ni", 0, 34), A.mult, A.add)
        ts(v("cw", LN, LN + 17), v("un", 49, 82, 2), 114.0, A.add)
        nb, counts = v("nb", 1, K + 1), (v("it"), v("cw", LN, LN + 17))
        move(nb, counts)
        for k in range(2):
            act(v("jb", K * k, K * k + K), counts, F.Sign, bias=col("cf", 10 + k), scale=-1.0, acc=col("sm2", k))
        ts(v("cw", LF, LF + 2), v("sm2", 0, 2), float(K - 2 * E), A.is_le)
        tau = col("sm2", 2)
        act(v("jb", 544, 576), (v("j16", 0, 16), v("cw", LF, LF + 2)), F.Copy, acc=tau)
        ts(v("fl", 0, K), nb, tau, A.is_gt)
        ts(v("fl", K + 1, 2 * K + 1), nb, tau, A.is_ge)
        scan(v("cs", 1, K + 1), v("fl", 0, K), v("fl", 0, K), A.add, A.max)
        above = col("cs", K)
        scan(v("cs", 288, 289 + K), v("fl", K, 2 * K + 1), v("cs", 0, K + 1), A.add, A.min, above)
        act(v("sm2", 6, 8), v("cf", 8, 10), F.Identity, bias=above)
        for k in range(2):
            act(v("jb", 576 + K * k, 576 + K * k + K), v("cs", 289, 289 + K), F.Sign, bias=col("sm2", 6 + k), scale=-1.0,
                acc=col("sm2", 4 + k))
            if t not in EARLY:
                ts(v("cw", LC + k, LC + 8, 2), v("cf", 122, 126), col("sm2", 4 + k), A.add, 0.5, A.mult)
        if t in EARLY:
            ts(v("hs", 16 * t, 16 * t + 2), v("sm2", 4, 6), K + 2.0, A.add, 0.5, A.mult)
            post()
        cand = (v("nb", 0, K + 1), v("hs", 16 * t, 16 * t + 2) if t in EARLY else v("cw", LC, LC + 2))
        tt(v("key", 64, 96), cand, v("dg"), A.mult)
        scan(v("key", 96, 128), v("nd"), v("key", 64, 96), A.mult, A.add)
        for k in range(2):
            tt(v("key", 32 * k, 32 * k + 32), cand, v("jt", 32 * k, 32 * k + 32), A.subtract)
            act(v("jb", 1696 + 32 * k, 1728 + 32 * k), v("key", 32 * k, 32 * k + 32), F.Sign, bias=col("key", 111 + 16 * k),
                scale=-1.0, acc=col("sm2", 10 + k))
            if t in EARLY:
                ts(v("hs", 16 * t + 8 + k, 16 * t + 12, 2), v("cf", 104, 106), col("sm2", 10 + k), A.subtract, 0.5, A.mult)
            else:
                ts(v("cw", LR + k, LR + 8, 2), v("cf", 4, 8), col("sm2", 10 + k), A.subtract, col("sm2", 10 + k), A.subtract)
        if t in EARLY:
            post()
        else:
            move(v("fc"), (v("xp", 4 * t * PL, 4 * (t + 1) * PL), v("cw", LC, LC + 8)))
            scatter(v("xi", 0, 128), v("cw", LR, LR + 8), v("fc"))
            qz("f", feed_at(t)[1], feed_at(t)[1] + 128, v("xi", 0, 512))
            post()
            post()
        part[0] = "layer%d" % t
        for b in range(4):
            cut = (P * b, P * b + P)
            move(v("g1", *cut), (plane(t, b), v("cu", LA, LA + 18)))
            tt(v("g2", *cut), (plane(t, b), v("cw", LB, LB + 18)), v("g1", *cut), A.max)
        for a, z in HALF:
            for b in range(4):
                tt(v("mt", 4 * a + b, 4 * z, 4), (plane(t, b), v("cw", LD + a // 16, LD + z // 16)), v("g2", P * b + a, P * b + z), A.add)
            qz("m", a, z, v("mt", 4 * a, 4 * z))
            for b in range(4):
                mine, rr = state(E + a, E + z, b), v("rr", 4 * a + b, 4 * z, 4)
                mm(b + 1, "w", 128 * b, "m", a, z - a)
                act(rr, bank(b + 1, z - a), F.Relu, scale=0.015625)
                tt(mine, rr, mine, A.add)
        if not last:
            for b in range(4):
                move(plane(t + 1, b, E + 1, PL), state(E, PL - 1, b), True)
        part[0] = "ent%d" % t
        if t in EARLY:
            for b in range(4):
                move(v("fc", E * b, E * b + E), (v("dp", PL * b, PL * b + K + 1), v("hl", 16 * t, 16 * t + 2)))
            for o in (0, 64):
                scatter(v("dor", o, o + 64), v("hl", 16 * t + 8, 16 * t + 12), v("fc", o, o + 64))
        for b in range(4):
            if t not in EARLY:
                mm(7 - b, "i", 128 * b, "f", feed_at(t)[0], 128)
            came = v("dor", E * b, E * b + E) if t in EARLY else bank(7 - b, E)
            tt(state(0, E, b) if last else plane(t + 1, b, 1, E + 1), came, plane(t, b, 1, E + 1), A.max)
            if t + 1 in EARLY:
                move(state(0, E, b), plane(t + 1, b, 1, E + 1), True)
    part[0] = "out"
    move(v("odb"), (v("it", 0, K + 1), v("cw", LD, LD + 18)))
    dma("y", T.od[:], T.odb[0:128:16, :], [v("odb")], [])
    for a, z, k in ((E, mid, 0), (mid, C, 1), (-XO, E, 6)):
        mm(k, "v", 0, "x", pack(R, a, z), z - a)
        lo, o = max(a, 0), XW * R + XO
        move(v("ys", lo, z), v("ps", 512 * k + lo - a, 512 * k + z - a))
        dma("ys", T.oc[:, 4 * lo:4 * z], T.qx[:, o + lo:o + z].bitcast(u8), [v("qx", o + lo, o + z)], [])
        dma("ys", T.y[:, lo:z], T.ys[:, lo:z], [v("ys", lo, z)], [])
    for k in range(4):
        dma("ys", T.osc[4 * k:4 * k + 4, :], T.sx[32 * k:32 * k + 4, o:o + C], [v("sx", o, o + C)], [])
    emit(g, T, ops)
